import numpy as np, ml_dtypes
CORES = [48,51,52,55]
N = 4
import mx_ref
BF = ml_dtypes.bfloat16
def entries(a):
    return np.ascontiguousarray(a.T).reshape(-1)
def table(e):
    return np.ascontiguousarray(np.reshape(e, (-1, 16)).T).astype(np.int32)
def gentries(a):
    return np.ascontiguousarray(a.reshape(8, 16, -1).transpose(0, 2, 1)).reshape(8, -1)
def gtable(e):
    e = np.asarray(e); return np.ascontiguousarray(e.reshape(8, -1, 16).transpose(0, 2, 1)).reshape(128, -1).astype(np.int32)
def gcols(t, e):
    v = np.concatenate([t.reshape(8, 16, -1, 4), np.zeros((8, 16, 1, 4), BF)], axis=2)
    return np.ascontiguousarray(np.stack([v[g][:, e[g]] for g in range(8)])).reshape(128, -1)
def tile(rs):
    return np.stack(rs, axis=2).reshape(128, -1).astype(BF)
def cut(t, i, w=512):
    return t[:, w * i:w * i + w]
def pick(q, e):
    c = np.concatenate([q[0].reshape(128, -1, 4), np.zeros((128, 1, 4), np.uint8)], axis=1); s = np.concatenate([q[1], np.ones((16, 1), np.uint8)], axis=1)
    return (np.ascontiguousarray(c[:, e].reshape(128, -1)), np.ascontiguousarray(s[:, e]))
def join(*qs):
    return (np.concatenate([q[0] for q in qs], axis=1), np.concatenate([q[1] for q in qs], axis=1))
def put(q, e, v):
    c, s = q[0].reshape(128, -1, 4).copy(), q[1].copy(); c[:, e] = v[0].reshape(128, -1, 4); s[:, e] = v[1]
    return (c.reshape(128, -1), s)
def pk(c, s):
    return (np.ascontiguousarray(c), mx_ref.live(s))
def emit(q):
    return q[0], q[1]
def packed(v, rng):
    q = [mx_ref.quantize(np.ascontiguousarray(v[r])) for r in range(N)]
    return np.stack([a for a, b in q]), np.stack([mx_ref.plane(b, rng) for a, b in q])
def values_of_codes():
    e, c = np.zeros((128, 128, 4), np.float32), np.zeros((128, 2, 4), np.uint8)
    e[np.arange(128), np.arange(128), 0] = 1
    c[:127, :, 0] = np.arange(256).reshape(2, 128).T[:127]
    return mx_ref.matmul(mx_ref.quantize(e.reshape(128, 512).astype(BF)), (c.reshape(128, 8), np.full((16, 2), 127, np.uint8))).T.reshape(-1).astype(np.float64)
CODE_VALUE, SCALE_VALUE = values_of_codes(), 2.0 ** (np.arange(256) - 127.0)
def decode(q):
    return (CODE_VALUE[q[0]].reshape(16, 8, -1, 4) * SCALE_VALUE[q[1]][:, None, :, None] + 0.0).reshape(128, -1).astype(np.float32)
def f(rng, *shape):
    return mx_ref.flush((rng.standard_normal(shape, dtype=np.float32) * np.exp2(rng.integers(-2, 3, shape[:-1] + (1,)))).astype(BF))
def wide(rng, *shape, cols=0):
    v = rng.standard_normal(shape, dtype=np.float32) * np.exp2(rng.integers(-12, 13, shape)).astype(np.float32)
    if cols: v *= np.repeat(np.exp2(rng.integers(-cols, cols + 1, shape[:-2] + (1, shape[-1] // 4))) * (rng.random(shape[:-2] + (1, shape[-1] // 4)) > 0.0625), 4, axis=-1).astype(np.float32)
    return mx_ref.flush(v.astype(BF))
H, A, C, L, M, R = 8, 40, 320, 256, 24, 3
WAY = [(-1, -1), (-1, 0), (-1, 1), (0, -1), (0, 1), (1, -1), (1, 0), (1, 1)]
ROW, COL = np.arange(C) // A, np.arange(C) % A
def seen(place, life):
    e = np.full((N, 8, C), -1)
    for g in range(8):
        k = place[:, g]
        lives = np.take_along_axis(life, k, axis=1)
        b = [np.where(lives, k + C * i, -1).reshape(N, H, A) for i in range(3)]
        field = np.concatenate([np.roll(b[0], 1, axis=0), b[1], np.roll(b[2], -1, axis=0)], axis=1)
        near = np.full((N, C), -1)
        for n in range(A + 2 * H, 0, -1):
            i, j = H + ROW + n * WAY[g][0], COL + n * WAY[g][1]
            ok = (i >= 0) & (i < 3 * H) & (j >= 0) & (j < A)
            z = field[:, np.where(ok, i, 0), np.where(ok, j, 0)]
            near = np.where(ok & (z >= 0), z, near)
        np.put_along_axis(e[:, g], k, near, axis=1)
    return e
def big(v):
    v = v.astype(np.float32)
    v[np.abs(v) < np.float32(2.0 ** -16)] = 0
    return v.astype(BF)
def numbers_of(rng):
    return {"x": big(f(rng, N, 128, 4 * C)), "u": np.array(f(rng, N, 128, 512)), "v": np.array(f(rng, N, 128, 512))}
def layers(rng, still=[]):
    w = np.array(f(rng, N, 128, 2048)).reshape(N, 8, 16, 4, 8, 16, 4)
    for i in still:
        w[:, :, i] = 0
        w[:, :, :, :, :, i] = 0
    return w
def weights(rng, w):
    c, p = packed(np.ascontiguousarray(w).reshape(N, 128, 2048), rng)
    return {"wc": c, "ws": p}
def signs(rng):
    return np.stack([rng.permutation(8) % 2 * 2.0 - 1.0 for r in range(N)])
def lives_of(rng):
    return np.stack([rng.permutation(C) < L for r in range(N)])
def seats_of(rng):
    return np.argsort(rng.random((N, 8, C)), axis=2)
def lists_of(place, life):
    return {"seat": np.stack([gtable(place[r]) for r in range(N)]), "alive": np.stack([table(life[r].astype(int)) for r in range(N)])}
def sit(e, squares, cells):
    others = e[~np.isin(e, cells)]
    e[squares] = cells
    e[np.setdiff1d(np.arange(C), squares)] = others
def marks(d, a, m):
    x, u = d["x"].reshape(N, 8, 16, C, 4), d["u"].reshape(N, 128, 128, 4)
    x[:, :, 0] = 0
    x[:, :, 0, :, 0] = a.astype(np.float32).astype(BF)
    x[:, 3, 8] = 0
    x[:, 3, 8, :, 0] = m.astype(np.float32).astype(BF)
    u[:, :, ::16] = 0
    u[:, :, 1] = 0
    for i in range(0, 128, 16): u[:, i, i, 0] = 1
    u[:, 56, 1, 0] = 1
def setup_inputs(rng):
    return {**numbers_of(rng), **weights(rng, layers(rng)), **lists_of(seats_of(rng), lives_of(rng))}
def setup_inputs_ties(rng):
    d = numbers_of(rng)
    k = np.array([1.5, 0.0, -1.25])
    a, m = k[rng.integers(0, 3, (N, 8, C))], k[rng.integers(0, 3, (N, C))]
    e = rng.permutation(N)
    a[e[0]], m[e[0]] = 1.5, 1.5
    marks(d, a, m)
    d["x"][e[1]] = 0
    return {**d, **weights(rng, layers(rng, [0, 8])), **lists_of(seats_of(rng), lives_of(rng))}
def setup_inputs_near(rng):
    d = numbers_of(rng)
    life, place = lives_of(rng), seats_of(rng)
    x = np.zeros((N, 8, 16, C, 4), np.float32)
    u = d["u"].reshape(N, 128, 128, 4)
    u[:, :, ::16] = 0
    u[:, :, 1] = 0
    w = layers(rng, [0, 8, 9, 10, 11, 12, 13, 14, 15])
    o, c = rng.permutation(N) % 4, signs(rng)
    j = np.arange(C)
    for r in range(N):
        place[r, 3] = j
        s = j // 2
        size = 1.0 if o[r] < 2 else 2.0 ** -4
        if o[r] < 2:
            x[r, :, 1:8] = d["x"][r].astype(np.float32).reshape(8, 16, C, 4)[:, 1:8]
            x[r, :, 0, :, 0] = c[r][:, None]
            for i in rng.permutation(8)[:4]: x[r, i, 0, rng.choice(np.flatnonzero(life[r])), 0] *= np.float32(2.0 ** 30)
        else: w[r] = 0
        if o[r] == 3:
            h = rng.permutation(C // 2) < L // 2
            life[r] = np.concatenate([h, h])
            s = j % (C // 2)
            x[r, :, 0, :, 0] = (8 + j // (C // 2)) * 2.0 ** -33
            n = np.flatnonzero(life[r])
            x[r, 3, 0, n[0], 0] = 2.0 ** -18
            who, left = n[1:], n[:-1]
            low = who[(who // A == left // A) & (who < C // 2)][-(M // 2):]
            fight = np.concatenate([n[1:2], low, low + C // 2])
            behind = rng.permutation(np.setdiff1d(n, np.concatenate([fight, left[np.isin(who, fight)]])))[:3 * M + 3]
            sit(place[r, 6], (np.arange(4)[:, None] * A + np.arange(M + 1)).reshape(-1), np.concatenate([fight, behind]))
            x[r, 6, 0, behind, 0] = -2.0 ** -18
        z = ((s[:, None] >> np.arange(8)) & 1) * np.exp2(np.arange(8) - 23.0) * size
        x[r, :, 8] = z[:, :4]
        x[r, :, 9] = z[:, 4:]
        x[r, :, 10:] = rng.integers(4, 8, (8, 6, C, 4)) * rng.choice([-1.0, 1.0], (8, 6, C, 4)) * 2.0 ** -20 * size
        k = 1.0 if o[r] == 0 else 2.0 ** -30
        for h in range(0, 128, 16):
            u[r, h, h, 0] = k
            u[r, h + 8:h + 10, h] = k
        u[r, 48, 1, 0] = k
        u[r, 56:58, 1] = k
    d["x"] = x.reshape(N, 128, 4 * C).astype(BF)
    return {**d, **weights(rng, w), **lists_of(place, life)}
def setup_inputs_huge(rng):
    d = numbers_of(rng)
    life, place = lives_of(rng), seats_of(rng)
    x = 2.0 ** 30 * (0.75 + 0.15 * rng.random((N, 128, C, 4)))
    a = 2.0 ** 30 * (1 - 0.1 * rng.random((N, 8, 16, 9, 4)))
    a[:, :, :, 8] *= -1
    a[:, [1, 6], :, 8] = 0
    c = signs(rng)
    for r in rng.permutation(N)[:N // 2]:
        x[r] *= (rng.permutation(C) % 2 * 2.0 - 1.0)[:, None]
        for g in range(8):
            a[r, np.arange(8) != g, :, g] = 0
            a[r, :, :, g] *= c[r, g]
        a[r, np.arange(8) != 3, :, 8] = 0
    u = d["u"].reshape(N, 128, 128, 4)
    a = a.reshape(N, 128, 9, 4).astype(np.float32).astype(BF)
    u[:, :, ::16] = a[:, :, :8]
    u[:, :, 1] = a[:, :, 8]
    corner = [0, 0, A - 1, 0, A - 1, C - A, C - A, C - 1]
    for g in range(8):
        k, way = rng.permutation(A), WAY[g][0] * WAY[g][1]
        q = rng.integers(H)
        for r in range(N):
            z = (ROW == q) & (COL > 0) & (COL < A - 1)
            if WAY[g][0]:
                n = k[(COL - way * (ROW + H * r)) % A]
                kept = (n + r) % 4
                z = (n < (C - L) // H) & ~((ROW == 0) & (kept % 2 == 1)) & ~((ROW == H - 1) & (kept >= 2))
            z[corner[g]] = False
            free = rng.permutation(np.flatnonzero(~z & (np.arange(C) != corner[g])))
            z[free[:C - L - int(np.sum(z))]] = True
            e = place[r, g]
            e[z] = rng.permutation(np.flatnonzero(~life[r]))
            e[~z] = rng.permutation(np.flatnonzero(life[r]))
            lone = np.flatnonzero(life[r])[0]
            e[np.flatnonzero(e == lone)[0]] = e[corner[g]]
            e[corner[g]] = lone
    w = np.zeros((N, 128, 4, 128, 4), np.float32)
    i = np.arange(128)
    for b in range(4): w[:, i, b, i, b] = -1
    d["x"] = x.astype(np.float32).reshape(N, 128, 4 * C).astype(BF)
    return {**d, **weights(rng, w.astype(BF)), **lists_of(place, life)}
def setup_inputs_deaths(rng):
    d = numbers_of(rng)
    life, place = lives_of(rng), seats_of(rng)
    a, m = rng.integers(8, 16, (N, 8, C)) * 0.125, np.zeros((N, C))
    o = rng.permutation(N) % 2
    for r in range(N):
        life[r] = np.roll(life[r], -int(np.flatnonzero(life[r])[0]))
        k = rng.permutation(np.flatnonzero(life[r])[1:])
        fight, behind = k[:M], k[M + 1:4 * M + 1]
        n = M - 1 - int(o[r])
        m[r, k[M]] = 1
        m[r, fight[:n]] = rng.integers(8, 16, n) * 0.125
        if o[r]:
            lone = fight[-1]
            sit(place[r, 0], [1, C - A], [lone, 0])
            for g, s in ((1, 0), (2, A - 1), (5, C - A), (6, C - A), (7, C - 1)): sit(place[r, g], [s], [lone])
            sit(place[r, 3], np.append(np.arange(M), A), np.concatenate([k[M:M + 1], fight]))
            sit(place[r, 4], np.arange(A - M, A), fight)
            for g in (3, 4): a[r, g, fight] *= -1
            a[r, 4, lone] = -4
        else:
            sit(place[r, 0], [C - A], [0])
            sit(place[r, 3], np.arange(M + 1), np.concatenate([k[M:M + 1], fight]))
            sit(place[r, 6], (np.arange(4)[:, None] * A + np.arange(M)).reshape(-1), np.concatenate([fight, behind]))
            a[r, 6, behind] *= -1
    marks(d, a, m)
    x, u = d["x"].reshape(N, 8, 16, C, 4), d["u"].reshape(N, 128, 128, 4)
    x[:, 0, 8] = 0
    x[:, 0, 8, 0, 0] = np.roll(o, -1).astype(np.float32).astype(BF)
    u[:, 8, 1, 0] = 1
    return {**d, **weights(rng, layers(rng, [0, 8])), **lists_of(place, life)}
def setup_inputs_spread(rng):
    d = setup_inputs(rng)
    d["x"] = big(wide(rng, N, 128, 4 * C, cols=6))
    return d
def check_inputs(d):
    b = []
    for k in ("x", "u", "v"):
        a = np.abs(d[k].astype(np.float32))
        if not (np.isfinite(a).all() and ((a == 0) | (a >= 2.0 ** -30) & (a <= 2.0 ** 30)).all()): b.append("a value of " + k)
    if ((d["wc"] & 0x7F) == 0x7F).any(): b.append("a code of wc that is no number")
    z = np.zeros((128, 4, 4), np.float32)
    z[:, 1] = 2.0 ** -30
    z[:, 2] = 2.0 ** 30
    c, s = emit(mx_ref.quantize(z.reshape(128, 16).astype(BF)))
    for r in range(N):
        p = mx_ref.live(d["ws"][r])
        if not ((p == s[0, 0]) | (p >= s[0, 1]) & (p <= s[0, 2])).all(): b.append("a scale of ws")
        if not (np.sort(gentries(d["seat"][r]), axis=1) == np.arange(C)).all(): b.append("seat: a permutation for every group")
        e = entries(d["alive"][r])
        if not ((e == 0) | (e == 1)).all(): b.append("alive: zeros and ones")
        if int(np.sum(e == 1)) != L: b.append("alive: the number of ones")
    return b
def reference(x, u, v, wc, ws, seat, alive):
    qu = [mx_ref.quantize(u[r]) for r in range(N)]
    lay = [pk(wc[r], ws[r]) for r in range(N)]
    place = np.stack([gentries(seat[r]) for r in range(N)])
    life = np.stack([entries(alive[r]) == 1 for r in range(N)])
    now = [x[r] for r in range(N)]
    for t in range(R):
        came = decode(join(*[mx_ref.quantize(now[r]) for r in range(N)])).astype(BF)
        e, after, now = seen(place, life), life.copy(), []
        for r in range(N):
            above, own, below = [cut(came, (r + i) % N, 4 * C) for i in (-1, 0, 1)]
            q = mx_ref.quantize(gcols(np.concatenate([above, own, below], axis=1), e[r]))
            p = mx_ref.matmul(qu[r], q) + np.float32(0.0)
            made = tile([mx_ref.matmul(pick(lay[r], np.arange(128 * b, 128 * b + 128)), q) * np.float32(0.015625) + own[:, b::4].astype(np.float32) for b in range(4)])
            now.append(np.where(np.repeat(life[r], 4), made, own))
            c = np.argsort(-np.where(life[r], p[1], -np.inf), kind="stable")[:M]
            k = e[r][:, c]
            mine = (k >= C) & (k < 2 * C)
            g = np.argmin(np.where(mine, p[::16][:, c], np.inf), axis=0)
            named = k[g, np.arange(M)][mine.any(axis=0)] - C
            after[r, named[~np.isin(named, c)]] = False
        life = after
    y, ol = np.zeros((N, 128, C), np.float32), np.zeros((N, 1, C), np.float32)
    oc, osc = np.zeros((N, 128, 4 * C), np.uint8), np.zeros((N, 16, C), np.uint8)
    for r in range(N):
        q = mx_ref.quantize(now[r])
        y[r] = mx_ref.matmul(mx_ref.quantize(v[r]), q)
        ol[r, 0] = life[r]
        oc[r], osc[r] = emit(q)
    return {"y": y, "ol": ol, "oc": oc, "osc": osc}

@@ -1,0 +1,508 @@
+from concourse.bass import DstId, RemoteDMATransfer
+from concourse.mybir import dt, AluOpType as A, ActivationFunctionType as F
+
+H, W, C, M, R = 8, 40, 320, 24, 3
+K = 432
+TP = 416
+X4, U8, BF, F32, I32, U16 = "float8_e4m3fn_x4", "uint8", "bfloat16", "float32", "int32", "uint16"
+
+
+def _sb(n, d):
+    return ("sbuf", [128, n], d)
+
+
+SCRATCH = {
+    "seatb": _sb(20, I32), "alv": _sb(20, I32), "ik": _sb(28, I32), "ib": _sb(16, I32), "ik9": _sb(4, I32),
+    "o_seat": _sb(20, U16), "o_alive": _sb(20, U16), "o_sig": _sb(28, U16), "o_end": _sb(4, U16), "o_end1": _sb(4, U16),
+    "o_pos": _sb(20, U16), "o_z": _sb(20, U16), "o_cmp": _sb(10, U16), "o_u": _sb(10, U16), "o_g": _sb(4, U16), "o_dc": _sb(2, U16),
+    "cf": _sb(64, F32), "kt": _sb(28, F32), "tb": _sb(15 * 28, F32), "tc": _sb(9 * 20, F32), "ctab0": _sb(20, F32),
+    "iof": _sb(C, F32), "iob": _sb(C, BF), "c16": _sb(C, F32), "l16": _sb(C, BF), "r16": _sb(C, BF), "j4": _sb(48, F32),
+    "lend": _sb(48, F32), "aend": _sb(48, F32), "r4": _sb(48, F32), "rm16": _sb(48, F32), "cc": _sb(48, F32),
+    "w10": _sb(16, BF), "idwin": _sb(416, F32), "dwin": _sb(416, BF), "dead": _sb(C, BF), "ds": _sb(C, BF),
+    "idseq": _sb(448, F32), "delta": _sb(K, F32), "dseq": _sb(K, BF), "st": _sb(K, F32),
+    "inv": _sb(C, BF), "invm": _sb(C, BF), "invs": _sb(C, BF),
+    "ev": _sb(48, F32), "es": _sb(48, F32), "adyn": _sb(C, F32), "zv": _sb(C, F32), "zs": _sb(C, F32), "zt": _sb(20, F32),
+    "vraw": _sb(C, F32), "tr": _sb(C, F32), "gb": _sb(96, F32), "e": _sb(48, F32), "nb": _sb(48, F32), "de": _sb(48, F32),
+    "ms": _sb(48, F32), "rm": _sb(48, F32), "ge": _sb(48, F32), "nm": _sb(48, F32), "rd": _sb(48, F32), "sm": _sb(16, F32),
+    "rowm": _sb(C, F32), "sg": _sb(3 * C, BF), "eq": _sb(3 * C, BF), "fs": _sb(3 * C, BF),
+    "f64": _sb(512, BF), "k64": _sb(516, BF), "eb": _sb(516, BF), "fl": _sb(512, BF), "id32": _sb(128, BF), "k1024": _sb(512, BF),
+    "xt": _sb(1296, BF), "xn": _sb(1296, BF), "ut": _sb(512, BF), "vt": _sb(512, BF), "tp": _sb(4 * TP, BF),
+    "z": _sb(4 * C, BF), "kill": _sb(4 * C, BF), "cm": _sb(512, BF), "ysb": _sb(C, F32), "olb": _sb(C, F32),
+    "qe": _sb(512, X4), "se": _sb(512, U8), "qw": _sb(512, X4), "sw": _sb(512, U8), "qu": _sb(128, X4), "su": _sb(128, U8),
+    "qu2": _sb(144, X4), "su2": _sb(144, U8), "qv": _sb(128, X4), "sv": _sb(128, U8), "qo": _sb(128, X4), "so": _sb(128, U8),
+    "qz": _sb(C, X4), "sz": _sb(C, U8), "qk": _sb(C, X4), "sk": _sb(C, U8), "qc": _sb(384, X4), "sc": _sb(384, U8),
+    "qx0": _sb(400, X4), "sx0": _sb(400, U8), "qx1": _sb(400, X4), "sx1": _sb(400, U8), "qx2": _sb(400, X4), "sx2": _sb(400, U8),
+    "qx3": _sb(C, X4), "sx3": _sb(C, U8),
+    "pa": ("psum", [128, 2048], F32), "pb": ("psum", [128, 2048], F32),
+}
+SEMAPHORES = ["cv", "cs", "ct", "cg", "sent", "arr0", "arr1", "arr2", "d_seat", "d_al0", "d_al1", "d_x", "d_u", "d_v", "d_wc", "d_ws", "d_out"]
+COLS = ("ng16 t1 t2 t3 t4 ndr ndc h v invl nl a1 a3 a3s a3b b1 b3 b3b ke ke1 q6 tq tmax ni6 c1 c2 c2b d1 d1b d2 d2b d3 d3s d3b "
+        "y0 y1 y2 y3 y4").split()
+OPT = {"seed": 2, "jit": 0.5, "muts": 20, "turns": 1500, "eps": 0.1, "hop": 2.7, "first": 2.5, "wake": 0.08, "small": 0.07}
+
+
+def rank_program(g, core, T, topo):
+    rank = T.rank_of(core)
+    if rank is None:
+        return
+    n_ranks = len(T.cores)
+    below, above = T.cores[(rank + 1) % n_ranks], T.cores[(rank - 1) % n_ranks]
+    qs = {"v": g.vector, "s": g.scalar, "t": g.tensor, "g": g, "y": g.sync}
+    V, S, PE = g.vector, g.scalar, g.tensor
+    steps, writer, readers = [], {}, {}
+    small = OPT["small"]
+
+    def step(ways, r, w, busy, done=None, sem=None):
+        r, w = r.split(), w.split()
+        firm, loose = set(), set()
+        for k in r:
+            firm.update([writer[k]] if k in writer else [])
+            if k[0] == "P":
+                loose.update(readers.get(k, []))
+        for k in w:
+            firm.update(readers.get(k, []))
+            if k in writer:
+                (loose if k[0] == "P" else firm).add(writer[k])
+        n = len(steps)
+        steps.append({"ways": ways, "firm": firm, "loose": loose - firm, "busy": busy, "done": done or busy, "sem": sem})
+        for k in r:
+            readers.setdefault(k, []).append(n)
+        for k in w:
+            writer[k] = n
+            readers[k] = []
+
+    def op(q, call, args, r, w, us=small, **kw):
+        step({q: (call, args, kw)}, r, w, us)
+
+    def dma(q, out, in_, sem, r, w, us=1.9):
+        step({q: (qs[q].dma_start, (out, in_), {})}, r, w, 0.1, us, sem)
+
+    def ts(out, in0, s1, op0, s2, op1, r, w, us=small):
+        op("v", V.tensor_scalar, (out, in0, s1, s2, op0) + (() if s2 is None else (op1,)), r, w, us)
+
+    def tt(out, a, b, o, r, w, us=small):
+        op("v", V.tensor_tensor, (out, a, b, o), r, w, us)
+
+    def cp(out, a, r, w, us=small, q="vs"):
+        ways = {"v": (V.tensor_copy, (out, a), {}), "s": (S.activation, (out, a, F.Copy), {})}
+        step({k: ways[k] for k in q}, r, w, us)
+
+    def mul(out, a, c, r, w, us=small, q="sv"):
+        ways = {"v": (V.tensor_scalar, (out, a, c, None, A.mult), {}), "s": (S.activation, (out, a, F.Copy), {"scale": c})}
+        step({k: ways[k] for k in q}, r, w, us)
+
+    def scan(out, d0, d1, o0, o1, r, w, us, first=0.0):
+        op("v", V.tensor_tensor_scan, (out, d0, d1, first, o0, o1), r, w, us)
+
+    def fill(ap, val, w):
+        op("v", V.memset, (ap, val), "", w)
+
+    def act(out, a, f, r, w, us=small, **kw):
+        op("s", S.activation, (out, a, f), r, w, us, **kw)
+
+    def quant(q, s, a, r, w, n=128):
+        op("v", V.quantize_mx, (q, s, a), r, w, 0.015 + 0.0011 * n)
+
+    def mm(out, lq, ls, rq, rs, start, stop, r, w, n=C):
+        op("t", PE.matmul_mx, (out, lq, ls, rq, rs, start, stop), r, w, (n + 16) * 0.0006)
+
+    def iota(out, pat, base, cm, w, flt=True, r=""):
+        n = 1
+        for a in pat:
+            n *= a[1]
+        op("g", g.iota, (out, pat, base, cm), r, w, 0.13 + 0.0021 * n, **({"allow_small_or_imprecise_dtypes": True} if flt else {}))
+
+    def col(n):
+        return T.cf[:, COLS.index(n):COLS.index(n) + 1]
+
+    def lin(q, out, w, a, r, m_, a_, us=small, f=F.Identity):
+        rr = r + "".join(" " + x for x in (m_, a_) if isinstance(x, str))
+        m_, a_ = [col(x) if isinstance(x, str) else float(x) for x in (m_, a_)]
+        ways = {"v": (V.tensor_scalar, (out, a, m_, a_, A.mult, A.add), {}), "s": (S.activation, (out, a, f), {"scale": m_, "bias": a_})}
+        step({k: ways[k] for k in q}, rr, w, us)
+
+    def clin(w, a, m_, a_):
+        lin("sv", col(w), w, col(a), a, m_, a_)
+
+    def ib(j):
+        return T.ib[:, j:j + 1]
+
+    def bits(j, src, r, sh, mask):
+        if sh:
+            ts(ib(j), src, sh, A.logical_shift_right, mask, A.bitwise_and, r, "ib%d" % j)
+        else:
+            ts(ib(j), src, mask, A.bitwise_and, None, None, r, "ib%d" % j)
+
+    def tb(j, n=27):
+        return T.tb[:, 28 * j:28 * j + n]
+
+    def tc(j):
+        return T.tc[:, 20 * j:20 * j + 20]
+
+    def bank(name, b, lo, hi):
+        return T[name][:, 512 * b + lo:512 * b + hi]
+
+    def part(q, s, lo, hi):
+        return q[:, lo:hi], s[:, lo:hi]
+
+    BIG, RND, FAR = 1.0e29, 12582912.0, 1.0e5
+    p = T.ik[:, 0:1]
+    al = "o_al0 o_al1 o_al2 o_al3"
+    xs = " x0 x1 x2 x3"
+
+    def rays(t):
+        for q, a, b in (("v", 0, 10), ("s", 10, 20)):
+            cp(T.dwin[:, W + 16 * a:W + 16 * b], T.dead[:].indirect(T.o_seat[:, a:b]), "dead o_seat", "dwin" + q, 0.32, "vs" if t == 0 else q)
+        for q, a, b in (("v", 0, 14), ("s", 14, 27)):
+            cp(T.dseq[:, 16 * a:16 * b], T.dwin[:].indirect(T.o_sig[:, a:b]), "dwinv dwins dwiny dwinz o_sig", "dseq" + q, 0.42, "vs" if t == 0 else q)
+
+    def send(t, xb):
+        scan(T.st[:], T.dseq[:], T.delta[:], A.mult, A.add, "dseqv dseqs delta", "st", 0.48)
+        tt(T.ev[:], T.st[:].indirect(T.o_end[:, 0:3]), T.aend[:], A.add, "st o_end aend", "ev", 0.13)
+        scan(T.es[:, 0:W], T.r4[:, 0:W], T.ev[:, 0:W], A.max, A.min, "r4 ev", "es", 0.08)
+        ts(T.o_cmp[:], T.es[:, 3:W:4], 4.0, A.mult, col("tmax"), A.min, "es tmax", "o_cmp")
+        cp(T.cm[:, 0:160], T[xb][:].indirect(T.o_cmp[:]), xb + " " + xb + "z o_cmp" + (xs if t else ""), "cm", 0.31, "v")
+        quant(*part(T.qc, T.sc, 128 * t, 128 * t + 128), T.cm[:], "cm cmy cmz", "qc%d" % t)
+        calls = []
+        for src, dst, cast in ((T.qc, T["qx%d" % t], True), (T.sc, T["sx%d" % t], False)):
+            trs = []
+            for j, to in enumerate((below, above)):
+                eng = topo.engines(core, to)
+                half = eng[j * len(eng) // 2:(j + 1) * len(eng) // 2]
+                rid, pid = topo.addr(to)[:2]
+                a, b = src[:, 128 * t:128 * t + W], dst[:, C + W * j:C + W * j + W]
+                trs.append(RemoteDMATransfer(dst_ids=[DstId(rid=rid, pnc=pid)], dma_engine_mask=sum(1 << e for e in half),
+                                             remote_sem=T.sem["arr%d" % t], src=a.bitcast(dt.uint8) if cast else a,
+                                             dst=b.bitcast(dt.uint8) if cast else b))
+            calls.append(trs)
+        late = 0.0 if t else OPT["first"]
+        step({"g": (calls, (), {})}, "qc%d" % t, "land%d" % t, 0.8 + late, OPT["hop"] + late, "arr%d" % t)
+
+    def unpack(t, xb):
+        q = part(T["qx%d" % t], T["sx%d" % t], 0, C)
+        quant(*q, T[xb][:, 0:4 * C], xb + (xs if t else ""), "qx%d" % t, C)
+        for b in range(4):
+            mm(bank("pb", b, 0, C), *part(T.qe, T.se, 128 * b, 128 * b + 128), *q, True, True, "qe%d qx%d" % (b, t), "PB%d" % b)
+            mul(T.tp[:, TP * b:TP * b + C], bank("pb", b, 0, C), 0.015625, "PB%d" % b, "tp%d" % b, 0.36)
+        for b in range(4):
+            mm(bank("pa", b, 0, C), *part(T.qe, T.se, 128 * b, 128 * b + 128), *q, True, False, "qe%d qx%d" % (b, t), "PA%d" % b)
+
+    def zlist(t):
+        a, ak = (T.l16[:], "l16") if t == 0 else (T.adyn[:], "adyn")
+        tt(T.zv[:], T.st[:].indirect(T.o_pos[:]), a, A.add, "st o_pos " + ak, "zv", 0.57)
+        scan(T.zs[:], T.r16[:], T.zv[:], A.max, A.min, "r16 zv", "zs", 0.36)
+        tt(T.zt[:], T.zs[:, 15:C:16], T.ctab0[:], A.add, "zs ctab0", "zt")
+        ts(T.o_z[:], T.zt[:], 401.0, A.min, None, None, "zt", "o_z")
+
+    def elist():
+        cp(T.vraw[:], T.st[:].indirect(T.o_pos[:]), "st o_pos", "vraw", 0.58, "s")
+        op("v", V.transpose, (T.tr[:], T.vraw[:]), "vraw", "tr", 0.36)
+        for a in range(4):
+            for d in (a, a ^ 1):
+                cp(T.gb[32 * d:32 * d + 32, 20 * a:20 * a + 20], T.tr[32 * a:32 * a + 32, 0:C:16], "tr", "gb%d%d" % (a, d), q="sv")
+        cp(T.gb[64:128, 0:40], T.gb[0:64, 0:40], "gb00 gb01 gb10 gb11", "gbl", q="sv")
+        cp(T.gb[0:64, 40:80], T.gb[64:128, 40:80], "gb22 gb23 gb32 gb33", "gbh", q="sv")
+        tt(T.e[:], T.gb[:].indirect(T.o_g[:, 0:3]), T.cc[:], A.add,
+           "gb00 gb01 gb10 gb11 gb22 gb23 gb32 gb33 gbl gbh gbz o_g cc cc4 cc5 cc6 cc15", "e", 0.13)
+        act(T.nb[:], T.e[:], F.Relu, "e", "nb", 0.08, scale=1.0e27, bias=-159.5e27)
+        tt(T.de[:, 0:47], T.e[:, 0:47], T.e[:, 1:48], A.subtract, "e", "de", 0.13)
+
+    def gather_z(t):
+        q = part(T["qx%d" % t], T["sx%d" % t], 272, 400)
+        for b in range(4):
+            mm(bank("pb", b, 0, 128), *part(T.qe, T.se, 128 * b, 128 * b + 128), *q, True, True, "qe%d qx%d land%d" % (b, t, t), "PB%d" % b, 128)
+        for b in range(4):
+            mul(T.tp[:, TP * b + C + 1:TP * b + C + 81], bank("pb", b, 48, 128), 0.015625, "PB%d" % b, "tn%d" % b, 0.12, "sv"[b % 2])
+        for b in range(4):
+            cp(T.z[:, b:4 * C:4], T.tp[:, TP * b:TP * b + 402].indirect(T.o_z[:]), "tp%d tn%d tpz tpy o_z" % (b, b), "z%d" % b, 0.58, "sv"[b % 2])
+        quant(T.qz[:], T.sz[:], T.z[:], "z0 z1 z2 z3", "qz", C)
+
+    def contest(t):
+        def seg(b, h):
+            return b[:, C * h:C * h + C]
+
+        mm(bank("pb", 0, 0, C), *part(T.qu2, T.su2, 0, 128), T.qz[:], T.sz[:], True, True, "qz qu2 su2", "PB0")
+        for h in range(3):
+            mm(bank("pb", h + 1, 0, 128), *part(T.qz, T.sz, 96 * h, 96 * h + 128), *part(T.qu2, T.su2, 16, 144), True, True,
+               "qz qu2 su2", "PB%d" % (h + 1), 128)
+            tt(T.ms[:, 16 * h:16 * h + 16], bank("pb", h + 1, 105, 121), T.nb[:, 16 * h:16 * h + 16], A.add, "PB%d nb" % (h + 1), "ms%d" % h)
+        for b in range(4):
+            mm(bank("pa", b, 0, C), *part(T.qw, T.sw, 128 * b, 128 * b + 128), T.qz[:], T.sz[:], False, True, "qz qw sw", "PA%d" % b)
+            mul(T.xn[:, b:4 * C:4], bank("pa", b, 0, C), 0.015625, "PA%d" % b, "x%d" % b, 0.36, "s" if t < R - 1 else "sv")
+        tt(T.rowm[:], bank("pb", 0, 0, C), T.ds[:], A.add, "PB0 ds", "rowm", 0.36)
+        for h in range(3):
+            act(seg(T.sg, h), T.rowm[:], F.Sign, "rowm ms%d" % h, "sg%d sa%d" % (h, h), 0.38, scale=-1.0, bias=T.ms[:, 16 * h + 5:16 * h + 6],
+                accum_out=T.sm[:, h:h + 1])
+        lin("s", T.sm[:, 4:7], "thr", T.sm[:, 0:3], "sa0 sa1 sa2", -1, C + 1 - 2 * M)
+        scan(T.rm[:], T.rm16[:], T.ms[:], A.max, A.min, "rm16 ms0 ms1 ms2", "rm", 0.08)
+        tt(T.ge[:, 1:48], T.ms[:, 1:48], T.rm[:, 0:47], A.is_ge, "ms0 ms1 ms2 rm", "ge", 0.13)
+        scan(T.nm[:, 0:47], T.ge[:, 0:47], T.de[:, 0:47], A.mult, A.add, "ge gez de", "nm", 0.08)
+        for h in range(3):
+            ts(seg(T.eq, h), seg(T.sg, h), 0.0, A.is_equal, None, None, "sg%d" % h, "eq%d" % h, 0.2)
+            scan(seg(T.fs, h), T.fl[:, 192 - 96 * h:512 - 96 * h], seg(T.eq, h), A.mult, A.add, "fl eq%d rd%d%d" % (h, t, h), "fs%d" % h, 0.2,
+                 T.rd[:, 16 * t + h:16 * t + h + 1])
+        tt(T.sm[:, 8:11], T.fs[:, C - 1:3 * C:C], T.sm[:, 4:7], A.is_gt, "fs0 fs1 fs2 thr", "con")
+        for h in range(3):
+            ts(T.kill[:, h:4 * C:4], T.iob[:], T.nm[:, 16 * h + 14:16 * h + 15], A.is_equal, T.sm[:, 8 + h:9 + h], A.mult, "iob nm con", "k%d" % h, 0.2)
+            n = 96 if h < 2 else 128
+            mul(T.kill[:, 384 * h + 3:384 * h + 4 * n:4], T.id32[:, 0:n], T.sm[:, 8 + h:9 + h], "id32 con", "km%d" % h, 0.14)
+        quant(T.qk[:], T.sk[:], T.kill[:], "k0 k1 k2 km0 km1 km2", "qk", C)
+        mm(bank("pb", 0, 0, C), T.qo[:], T.so[:], T.qk[:], T.sk[:], True, True, "qo qk", "PB0")
+
+    def dead_cells(t):
+        for h in range(3):
+            mm(bank("pb", h + 1, 0, 128), *part(T.qk, T.sk, 96 * h, 96 * h + 128), T.qo[:], T.so[:], True, True, "qo qk", "PB%d" % (h + 1), 128)
+            act(T.rd[:, 16 * t + 16 + h:16 * t + 17 + h], bank("pb", h + 1, 0, 1), F.Relu, "PB%d rd%d%d" % (h + 1, t, h), "rd%d%d" % (t + 1, h),
+                bias=T.rd[:, 16 * t + h:16 * t + h + 1])
+
+    dma("y", T.seatb[:], T.seat[:], "d_seat", "", "seatb Pload")
+    dma("s", T.alv[0:16, :], T.alive[:], "d_al0", "", "alv0")
+    dma("y", T.alv[16:32, :], T.alive[:], "d_al1", "", "alv1 Pload")
+    dma("y", T.xt[:, 0:4 * C], T.x[:], "d_x", "", "xt Pload", 3.5)
+    dma("y", T.ut[:], T.u[:], "d_u", "", "ut Pload", 2.5)
+    dma("y", T.qw[:].bitcast(dt.uint8), T.wc[:], "d_wc", "", "qw Pload", 3.2)
+    dma("y", T.sw[:], T.ws[:], "d_ws", "", "sw Pload", 2.2)
+    dma("y", T.vt[:], T.v[:], "d_v", "", "vt Pload", 2.5)
+
+    iota(T.ik[:], [[16, 28]], 0, 1, "ik", False)
+    iota(T.ik9[:], [[0, 4]], 9, 1, "ik9", False)
+    iota(T.w10[:], [[-1, 16]], 1, 0, "w10")
+    iota(T.iof[:], [[1, C]], 0, 0, "iof")
+    iota(T.idwin[:, 0:W], [[1, W]], C + 1, 0, "idwa")
+    iota(T.idwin[:, W + C:2 * W + C], [[1, W]], C + 1 + W, 0, "idwb")
+    iota(T.j4[:], [[0, 12], [1, 4]], 0, 0, "j4")
+    iota(T.r4[:], [[0, 12], [-31000, 4]], 30000, 0, "r4")
+    iota(T.c16[:], [[0, 20], [1, 16]], 0, 0, "c16")
+    iota(T.k64[:], [[0, 516]], 64, 0, "k64")
+    op("g", g.affine_select, (T.eb[:], T.k64[:], [[1, 516]], A.is_equal, 0.0, -3, -4), "k64", "eb", 1.24)
+    iota(T.cc[:], [[96, 3], [0, 16]], -160, 1, "cc")
+    for j, val in ((4, 10000), (5, -10000), (6, 10000), (15, 0)):
+        iota(T.cc[:, j:48:16], [[0, 3]], val, 0, "cc%d" % j, True, "cc")
+    op("g", g.affine_select, (T.f64[:], T.k64[:, 0:512], [[1, 512]], A.not_equal, -64.0, -192, -1), "k64", "f64", 1.24)
+    mul(T.fl[:], T.f64[:], 0.015625, "f64", "fl", 0.57, "s")
+    for ap, n, val, w in ((T.idwin[:, 400:416], 16, C, "idwc"), (T.dwin[:, 0:W], W, 0, "dwiny"), (T.dwin[:, W + C:416], 56, 0, "dwinz"),
+                          (T.idseq[:, K:K + 16], 16, C, "idseqz"), (T.xt[:, 4 * C:4 * C + 16], 16, 0, "xtz"), (T.xn[:, 4 * C:4 * C + 16], 16, 0, "xnz"),
+                          (T.tp[:, C:4 * TP:TP], 4, 0, "tpz"), (T.tp[:, 401:4 * TP:TP], 4, 0, "tpy"), (T.gb[:, 80:96], 16, 0, "gbz"),
+                          (T.ge[:, 0:1], 1, 0, "gez")):
+        iota(ap, [[0, n]], val, 0, w)
+
+    bits(0, p, "ik", 0, 112)
+    ts(col("t1"), p, 48.0, A.is_lt, -1.0, A.add, "ik", "t1")
+    ts(col("t2"), p, 48.0, A.is_ge, None, None, "ik", "t2")
+    lin("sv", col("t3"), "t3", ib(0), "ib0", -0.0625, 3)
+    lin("sv", col("ng16"), "ng16", ib(0), "ib0", -1, 0)
+    ts(col("ndr"), p, 80.0, A.is_lt, col("t1"), A.add, "ik t1", "ndr")
+    ts(col("h"), p, 80.0, A.is_lt, col("t2"), A.mult, "ik t2", "h")
+    ts(col("t4"), p, 64.0, A.is_lt, col("t3"), A.add, "ik t3", "t4")
+    lin("sv", T.kt[:], "kt", T.ik[:], "ik", 1, "ng16")
+    for w, a, m_, a_ in (("invl", "h", 1.0 / 41 - 1.0 / 9, 1.0 / 9), ("ndc", "ndr", -3, "t4"), ("v", "h", -1, 1), ("nl", "h", -32, -9),
+                         ("a3s", "h", -16.5, -4), ("a3b", "h", 23.5, -4), ("b3b", "h", -140, 180), ("b1", "ndr", -360, 0),
+                         ("a3", "ndc", "a3s", "a3b"), ("a1", "ndc", "nl", "v"), ("b3", "ndr", -180, "b3b"), ("t1", "ndr", W, 0),
+                         ("t2", "h", W, "b1"), ("ke", "ndc", -36, 44), ("ke1", "ndc", -36, 45),
+                         ("c1", "ndr", 1, "h"), ("c2b", "v", 4.5, 0), ("d1b", "v", 9, 0), ("d2b", "h", 41, 0), ("d3s", "h", -55.5, 36),
+                         ("d3b", "h", -15.5, 35), ("c2", "ndr", -3.5, "c2b"), ("d1", "ndc", "h", "d1b"), ("d2", "a1", "v", "d2b"),
+                         ("d3", "ndc", "d3s", "d3b")):
+        clin(w, a, m_, a_)
+    lin("sv", tb(0), "tb0", T.kt[:, 0:27], "kt", "invl", -0.488)
+    ts(tb(1), tb(0), RND, A.add, -RND, A.add, "tb0", "tb1")
+    lin("sv", tb(4), "tb4", T.kt[:, 0:27], "kt", "ndc", "a3")
+    lin("sv", tb(3), "tb3", tb(1), "tb1", "a1", 0)
+    lin("sv", tb(2), "tb2", tb(1), "tb1", "t2", 0)
+    lin("sv", tb(5), "tb5", T.kt[:, 0:27], "kt", "t1", "b3")
+    tt(tb(6), tb(3), tb(4), A.add, "tb3 tb4", "tb6", 0.09)
+    tt(tb(7), tb(2), tb(5), A.add, "tb2 tb5", "tb7", 0.09)
+    lin("s", tb(8), "tb8", tb(6), "tb6", 1, -19.5, small, F.Abs)
+    tt(tb(11), tb(7), tb(6), A.add, "tb7 tb6", "tb11", 0.09)
+    ts(tb(10), tb(8), 20.0, A.is_gt, 400.0, A.mult, "tb8", "tb10")
+    tt(tb(9), tb(10), tb(11), A.max, "tb10 tb11", "tb9", 0.09)
+    ts(T.o_sig[:, 0:27], tb(9), 400.0, A.min, None, None, "tb9", "o_sig")
+    for a in range(4):
+        cp(T.o_alive[32 * a:32 * a + 32, :], T.alv[0:32, :], "alv0 alv1", "o_al%d" % a, q="v")
+    cp(T.o_seat[:], T.seatb[:], "seatb", "o_seat", q="v")
+    cp(T.dead[:], T.w10[:].indirect(T.o_alive[:]), "w10 " + al, "dead", 0.58)
+    cp(T.idwin[:, W:W + C], T.iof[:].indirect(T.o_seat[:]), "iof o_seat", "idwd", 0.58)
+    for j, a, b in ((0, 0, 14), (1, 14, 27)):
+        cp(T.idseq[:, 16 * a:16 * b], T.idwin[:].indirect(T.o_sig[:, a:b]), "idwa idwb idwc idwd o_sig", "idseq%d" % j, 0.42)
+    ids = "idseq0 idseq1 idseqz"
+    rays(0)
+    tt(T.delta[:], T.idseq[:, 0:K], T.idseq[:, 1:K + 1], A.subtract, ids, "delta", 0.93)
+    bits(1, p, "ik", 2, 3)
+    bits(2, p, "ik", 0, 3)
+    bits(3, p, "ik", 0, 15)
+    ts(tb(12, 3), T.kt[:, 0:3], W - 1.0, A.min, 9.0, A.mult, "kt", "tb12")
+    ts(T.o_end1[:, 0:3], tb(12, 3), col("ke1"), A.add, None, None, "tb12 ke1", "o_end1")
+    ts(T.o_end[:, 0:3], tb(12, 3), col("ke"), A.add, None, None, "tb12 ke", "o_end")
+    lin("sv", col("q6"), "q6", ib(1), "ib1", -FAR, 0)
+    lin("sv", col("tq"), "tq", ib(2), "ib2", 0.25, 0)
+    lin("sv", col("tmax"), "tmax", ib(2), "ib2", 1, 4 * C)
+    lin("sv", col("ni6"), "ni6", ib(3), "ib3", -FAR, 0)
+    lin("s", T.ev[:], "ev", T.j4[:], "j4", FAR, "q6", 0.08, F.Abs)
+    lin("sv", T.lend[:], "lend", T.ev[:], "ev", 1, "tq", 0.08)
+    lin("s", T.cm[:, 160:336], "cmy", T.iof[:, 0:176], "iof", 0, 0, 0.21)
+    lin("s", T.cm[:, 336:512], "cmz", T.iof[:, 0:176], "iof", 0, 0, 0.21)
+    lin("s", T.iob[:], "iob", T.iof[:], "iof", 1, -160, 0.36)
+    lin("s", T.l16[:], "l16", T.c16[:], "c16", FAR, "ni6", 0.36, F.Abs)
+    lin("s", T.r16[:], "r16", T.c16[:], "c16", -31000, 30000, 0.36)
+    tt(T.aend[:], T.idseq[:].indirect(T.o_end1[:, 0:3]), T.lend[:], A.add, ids + " o_end1 lend", "aend", 0.13)
+    send(0, "xt")
+
+    op("v", V.tensor_copy, (T.inv[:].indirect(T.o_seat[:]), T.iob[:]), "iob o_seat", "inv", 1.32)
+    tt(T.invm[:], T.inv[:], T.l16[:], A.add, "inv l16", "invm", 0.7)
+    scan(T.invs[:], T.r16[:], T.invm[:], A.max, A.min, "r16 invm", "invs", 0.2)
+    lin("v", tc(6), "tc6", T.o_alive[:], al, -1000, 1000)
+    lin("sv", tc(0), "tc0", T.invs[:, 15:C:16], "invs", 0.025, 140.5 / W)
+    ts(tc(1), tc(0), RND, A.add, -RND, A.add, "tc0", "tc1")
+    lin("sv", tc(2), "tc2", tc(1), "tc1", -W, 160)
+    lin("sv", tc(3), "tc3", tc(1), "tc1", "c1", "c2")
+    tt(tc(4), tc(2), T.invs[:, 15:C:16], A.add, "tc2 invs", "tc4")
+    lin("sv", tc(5), "tc5", tc(3), "tc3", "d2", "d3")
+    tt(T.ctab0[:], tc(6), T.kt[:, 0:20], A.add, "tc6 kt", "ctab0")
+    lin("sv", tc(7), "tc7", tc(4), "tc4", "d1", 0)
+    tt(T.o_pos[:], tc(7), tc(5), A.add, "tc7 tc5", "o_pos")
+    for b in range(4):
+        quant(*part(T.qe, T.se, 128 * b, 128 * b + 128), T.eb[:, 3 - b:515 - b], "eb", "qe%d" % b)
+    lin("s", T.k1024[:], "k1024", T.k64[:, 0:512], "k64", 16, 0, 0.57)
+    lin("s", T.id32[:], "id32", T.fl[:, 192:320], "fl", 16, -16, 0.16)
+    quant(T.qo[:], T.so[:], T.k1024[:], "k1024", "qo")
+    quant(T.qu[:], T.su[:], T.ut[:], "ut", "qu")
+    quant(T.qv[:], T.sv[:], T.vt[:], "vt", "qv")
+    bits(4, p, "ik", 0, 7)
+    fill(T.o_u[:, 0:8], 1, "o_u0")
+    lin("v", T.o_u[:, 8:9], "o_u1", ib(4), "ib4", 16, 0)
+    cp(T.qu2[:].bitcast(dt.uint32), T.qu[:].bitcast(dt.uint32).indirect(T.o_u[:, 0:9]), "qu o_u0 o_u1", "qu2", 0.29, "v")
+    cp(T.su2[:], T.su[:].indirect(T.o_u[:, 0:9]), "qu o_u0 o_u1", "su2", 0.3, "s")
+    bits(5, T.ik9[:, 0:1], "ik9", 0, 7)
+    bits(6, T.ik9[:, 0:1], "ik9", 0, 1)
+    bits(7, T.ik9[:, 0:1], "ik9", 0, 8)
+    bits(8, p, "ik", 4, 6)
+    ts(col("y4"), ib(3), 6.0, A.mult, 12.0, A.min, "ib3", "y4")
+    lin("sv", col("y0"), "y0", ib(8), "ib8", 1, 0)
+    lin("sv", col("y1"), "y1", ib(5), "ib5", 10, "y0")
+    lin("sv", col("y2"), "y2", ib(6), "ib6", -9, "y1")
+    lin("sv", col("y3"), "y3", ib(7), "ib7", 16, "y2")
+    lin("sv", tb(13, 3), "tb13", T.j4[:, 0:3], "j4", 6, "y3")
+    ts(T.o_g[:, 0:3], tb(13, 3), 80.0, A.min, None, None, "tb13", "o_g")
+    lin("v", T.o_dc[:, 0:1], "o_dc", ib(0), "ib0", 0.0625, "y4")
+    cp(T.rd[:, 0:16], T.tc[:, 120:140].indirect(T.o_dc[:, 0:1]), "tc6 o_dc", "rd00 rd01 rd02", 0.09)
+    fill(T.rd[96:128, 0:2], 1000.0, "rd00 rd01")
+    lin("s", T.rm16[:], "rm16", T.cc[:], "cc cc4 cc5 cc6 cc15", 1.0e25, -5.0e28, 0.08)
+
+    for t in range(R):
+        xb = "xn" if t else "xt"
+        if t:
+            tt(T.dead[:], bank("pb", 0, 0, C), T.ds[:], A.is_gt, "PB0 ds", "dead", 0.36)
+            rays(t)
+            send(t, xb)
+            tt(T.adyn[:], bank("pb", 0, 0, C), T.l16[:] if t == 1 else T.adyn[:], A.max, "PB0 l16 adyn", "adyn", 0.36)
+            dead_cells(t - 1)
+        mul(T.ds[:], T.dead[:], -BIG, "dead", "ds", 0.36, "s")
+        unpack(t, xb)
+        zlist(t)
+        elist()
+        gather_z(t)
+        contest(t)
+
+    quant(T.qx3[:], T.sx3[:], T.xn[:, 0:4 * C], xs, "qx3", C)
+    mm(bank("pb", 1, 0, C), T.qv[:], T.sv[:], T.qx3[:], T.sx3[:], True, True, "qv qx3", "PB1")
+    dma("y", T.oc[:], T.qx3[:].bitcast(dt.uint8), "d_out", "qx3", "", 2.9)
+    cp(T.ysb[:], bank("pb", 1, 0, C), "PB1", "ysb", 0.36, "sv")
+    dma("s", T.y[:], T.ysb[:], "d_out", "ysb", "", 2.9)
+    for k in range(4):
+        dma("y", T.osc[4 * k:4 * k + 4, :], T.sx3[32 * k:32 * k + 4, :], "d_out", "qx3", "")
+    tt(T.olb[0:32, :], T.pb[0:32, 0:C], T.ds[0:32, :], A.is_le, "PB0 ds", "olb", 0.36)
+    dma("y", T.ol[:], T.olb[0:1, :], "d_out", "olb", "")
+
+    n, wake = len(steps), OPT["wake"]
+    after = [[] for _ in steps]
+    for i, s in enumerate(steps):
+        for j in s["firm"] | s["loose"]:
+            after[j].append(i)
+    tail, seed = [0.0] * n, OPT["seed"]
+    for i in range(n - 1, -1, -1):
+        tail[i] = steps[i]["done"] + max([tail[j] + wake for j in after[i]] + [0.0])
+
+    def lay(tail):
+        left = [len(s["firm"] | s["loose"]) for s in steps]
+        ready = [i for i in range(n) if not left[i]]
+        free, end, queue, plan = {q: 0.0 for q in qs}, [0.0] * n, [None] * n, []
+
+        def earliest(i):
+            best = None
+            for q in steps[i]["ways"]:
+                t0 = max([free[q]] + [end[j] + wake for j in steps[i]["firm"]] + [end[j] + wake for j in steps[i]["loose"] if queue[j] != q])
+                if best is None or t0 < best[0] - 0.02:
+                    best = (t0, q)
+            return best
+
+        while ready:
+            at = {i: earliest(i) for i in ready}
+            x = min(ready, key=lambda i: (at[i][0], -tail[i]))
+            for y in sorted(ready, key=lambda i: -tail[i]):
+                if tail[y] <= tail[x]:
+                    break
+                (tx, qx), (ty, qy) = at[x], at[y]
+                bx = tx + steps[x]["busy"]
+                if qx == qy and ty < bx and bx + tail[y] > max(ty + tail[y], ty + steps[y]["busy"] + tail[x]) + OPT["eps"]:
+                    x = y
+                    break
+            t0, q = at[x]
+            queue[x], free[q], end[x] = q, t0 + steps[x]["busy"], t0 + steps[x]["done"]
+            plan.append(x)
+            ready.remove(x)
+            for j in after[x]:
+                left[j] -= 1
+                if not left[j]:
+                    ready.append(j)
+        return max(end), plan, queue
+
+    def replay(plan, queue, wk, hop):
+        free, end = {q: 0.0 for q in qs}, [0.0] * n
+        for i in plan:
+            s, q = steps[i], queue[i]
+            t0 = max([free[q]] + [end[j] + wk for j in s["firm"]] + [end[j] + wk for j in s["loose"] if queue[j] != q])
+            free[q], end[i] = t0 + s["busy"], t0 + s["done"] + (hop if s["sem"] and s["sem"][0] == "a" else 0.0)
+        return max(end)
+
+    if "best" not in OPT:
+        best, push = None, [0.0] * n
+        for turn in range(OPT["turns"]):
+            other = list(push)
+            for k in range(OPT["muts"] if turn else 0):
+                seed = (seed * 1103515245 + 12345) % 2147483648
+                i = (seed >> 8) % n
+                seed = (seed * 1103515245 + 12345) % 2147483648
+                other[i] += OPT["jit"] * (seed / 1073741824 - 1)
+            got = lay([tail[i] + other[i] for i in range(n)])
+            cost = got[0] + replay(got[1], got[2], 0.5 * wake, -0.7) + replay(got[1], got[2], 2.5 * wake, 0.7)
+            if best is None or cost <= best[0]:
+                best, push = (cost, got[1], got[2], got[0]), other
+        OPT["best"] = best
+    plan, queue = OPT["best"][1], OPT["best"][2]
+
+    count, token, waited = {}, [None] * n, {q: {} for q in qs}
+
+    def wait(q, sem, val):
+        if waited[q].get(sem, 0) < val:
+            waited[q][sem] = val
+            qs[q].wait_ge(T.sem[sem], val)
+
+    for i in plan:
+        s, q = steps[i], queue[i]
+        need = {}
+        for j in list(s["firm"]) + [j for j in s["loose"] if queue[j] != q]:
+            need[token[j][0]] = max(need.get(token[j][0], 0), token[j][1])
+        for sem in sorted(need):
+            wait(q, sem, need[sem])
+        call, args, kw = s["ways"][q]
+        if isinstance(call, list):
+            for trs in call:
+                g.remote_dma_fused(trs, local_sem=T.sem.sent)
+            count["sent"] = count.get("sent", 0) + len(topo.engines(core, below)) + len(topo.engines(core, above))
+            token[i] = (s["sem"], len(topo.engines(above, core)) + len(topo.engines(below, core)))
+        else:
+            sem, k = (s["sem"], 16) if s["sem"] else ("c" + q, 1)
+            count[sem] = count.get(sem, 0) + k
+            call(*args, **kw).then_inc(T.sem[sem], k)
+            token[i] = (sem, count[sem])
+    for sem in sorted(count):
+        wait("g", sem, count[sem])

@@ -23,7 +23,7 @@ SCRATCH = {
     "inv": _sb(C, BF), "invm": _sb(C, BF), "invs": _sb(C, BF),
     "ev": _sb(48, F32), "es": _sb(48, F32), "adyn": _sb(C, F32), "zv": _sb(C, F32), "zs": _sb(C, F32), "zt": _sb(20, F32),
     "vraw": _sb(C, F32), "tr": _sb(C, F32), "gb": _sb(96, F32), "e": _sb(48, F32), "nb": _sb(48, F32), "de": _sb(48, F32),
-    "ms": _sb(48, F32), "rm": _sb(48, F32), "ge": _sb(48, F32), "nm": _sb(48, F32), "rd": _sb(48, F32), "sm": _sb(16, F32),
+    "ms": _sb(48, F32), "rm": _sb(48, F32), "ge": _sb(48, F32), "nm": _sb(48, F32), "rd": _sb(48, F32), "sm": _sb(16, F32), "mk": _sb(4, F32),
     "rowm": _sb(C, F32), "sg": _sb(3 * C, BF), "eq": _sb(3 * C, BF), "fs": _sb(3 * C, BF),
     "f64": _sb(512, BF), "k64": _sb(516, BF), "eb": _sb(516, BF), "fl": _sb(512, BF), "id32": _sb(128, BF), "k1024": _sb(512, BF),
     "xt": _sb(1296, BF), "xn": _sb(1296, BF), "ut": _sb(512, BF), "vt": _sb(512, BF), "tp": _sb(4 * TP, BF),
@@ -38,7 +38,7 @@ SCRATCH = {
 SEMAPHORES = ["cv", "cs", "ct", "cg", "sent", "arr0", "arr1", "arr2", "d_seat", "d_al0", "d_al1", "d_x", "d_u", "d_v", "d_wc", "d_ws", "d_out"]
 COLS = ("ng16 t1 t2 t3 t4 ndr ndc h v invl nl a1 a3 a3s a3b b1 b3 b3b ke ke1 q6 tq tmax ni6 c1 c2 c2b d1 d1b d2 d2b d3 d3s d3b "
         "y0 y1 y2 y3 y4").split()
-OPT = {"seed": 2, "jit": 0.5, "muts": 20, "turns": 1500, "eps": 0.1, "hop": 2.7, "first": 2.5, "wake": 0.08, "small": 0.07}
+OPT = {"seed": 1, "jit": 1.0, "muts": 8, "turns": 6000, "eps": 0.1, "hop": 2.7, "first": 2.5, "wake": 0.13, "small": 0.07}
 
 
 def rank_program(g, core, T, topo):
@@ -145,24 +145,27 @@ def rank_program(g, core, T, topo):
     def part(q, s, lo, hi):
         return q[:, lo:hi], s[:, lo:hi]
 
-    BIG, RND, FAR = 1.0e29, 12582912.0, 1.0e5
+    RND, FAR = 12582912.0, 1.0e5
     p = T.ik[:, 0:1]
-    al = "o_al0 o_al1 o_al2 o_al3"
+    al = "o_al0 o_al1"
     xs = " x0 x1 x2 x3"
 
     def rays(t):
         for q, a, b in (("v", 0, 10), ("s", 10, 20)):
-            cp(T.dwin[:, W + 16 * a:W + 16 * b], T.dead[:].indirect(T.o_seat[:, a:b]), "dead o_seat", "dwin" + q, 0.32, "vs" if t == 0 else q)
+            cp(T.dwin[:, W + 16 * a:W + 16 * b], T.dead[:].indirect(T.o_seat[:, a:b]), "dead0 dead1 o_seat", "dwin" + q, 0.32, "vs" if t == 0 else q)
         for q, a, b in (("v", 0, 14), ("s", 14, 27)):
-            cp(T.dseq[:, 16 * a:16 * b], T.dwin[:].indirect(T.o_sig[:, a:b]), "dwinv dwins dwiny dwinz o_sig", "dseq" + q, 0.42, "vs" if t == 0 else q)
+            o, w = T.dseq[:, 16 * a:16 * b], T.dwin[:].indirect(T.o_sig[:, a:b])
+            step({"v": (V.tensor_scalar, (o, w, 1.0, None, A.min), {}), "s": (S.activation, (o, w, F.Sign), {})},
+                 "dwinv dwins dwiny dwinz o_sig", "dseq" + q, 0.42)
 
     def send(t, xb):
-        scan(T.st[:], T.dseq[:], T.delta[:], A.mult, A.add, "dseqv dseqs delta", "st", 0.48)
+        scan(T.st[:], T.dseq[:], T.delta[:], A.mult, A.add, "dseqv dseqs delta0 delta", "st", 0.48)
         tt(T.ev[:], T.st[:].indirect(T.o_end[:, 0:3]), T.aend[:], A.add, "st o_end aend", "ev", 0.13)
         scan(T.es[:, 0:W], T.r4[:, 0:W], T.ev[:, 0:W], A.max, A.min, "r4 ev", "es", 0.08)
         ts(T.o_cmp[:], T.es[:, 3:W:4], 4.0, A.mult, col("tmax"), A.min, "es tmax", "o_cmp")
-        cp(T.cm[:, 0:160], T[xb][:].indirect(T.o_cmp[:]), xb + " " + xb + "z o_cmp" + (xs if t else ""), "cm", 0.31, "v")
-        quant(*part(T.qc, T.sc, 128 * t, 128 * t + 128), T.cm[:], "cm cmy cmz", "qc%d" % t)
+        for q, a, b in (("v", 0, 6), ("s", 6, 10)):
+            cp(T.cm[:, 16 * a:16 * b], T[xb][:].indirect(T.o_cmp[:, a:b]), xb + " " + xb + "z o_cmp" + (xs if t else ""), "cm" + q, 0.2, q)
+        quant(*part(T.qc, T.sc, 128 * t, 128 * t + 128), T.cm[:], "cmv cms cmy cmz", "qc%d" % t)
         calls = []
         for src, dst, cast in ((T.qc, T["qx%d" % t], True), (T.sc, T["sx%d" % t], False)):
             trs = []
@@ -188,7 +191,7 @@ def rank_program(g, core, T, topo):
             mm(bank("pa", b, 0, C), *part(T.qe, T.se, 128 * b, 128 * b + 128), *q, True, False, "qe%d qx%d" % (b, t), "PA%d" % b)
 
     def zlist(t):
-        a, ak = (T.l16[:], "l16") if t == 0 else (T.adyn[:], "adyn")
+        a, ak = (T.l16[:], "l16") if t == 0 else (T.adyn[:], "adyn0 adyn1")
         tt(T.zv[:], T.st[:].indirect(T.o_pos[:]), a, A.add, "st o_pos " + ak, "zv", 0.57)
         scan(T.zs[:], T.r16[:], T.zv[:], A.max, A.min, "r16 zv", "zs", 0.36)
         tt(T.zt[:], T.zs[:, 15:C:16], T.ctab0[:], A.add, "zs ctab0", "zt")
@@ -212,9 +215,9 @@ def rank_program(g, core, T, topo):
         for b in range(4):
             mm(bank("pb", b, 0, 128), *part(T.qe, T.se, 128 * b, 128 * b + 128), *q, True, True, "qe%d qx%d land%d" % (b, t, t), "PB%d" % b, 128)
         for b in range(4):
-            mul(T.tp[:, TP * b + C + 1:TP * b + C + 81], bank("pb", b, 48, 128), 0.015625, "PB%d" % b, "tn%d" % b, 0.12, "sv"[b % 2])
+            mul(T.tp[:, TP * b + C + 1:TP * b + C + 81], bank("pb", b, 48, 128), 0.015625, "PB%d" % b, "tn%d" % b, 0.12)
         for b in range(4):
-            cp(T.z[:, b:4 * C:4], T.tp[:, TP * b:TP * b + 402].indirect(T.o_z[:]), "tp%d tn%d tpz tpy o_z" % (b, b), "z%d" % b, 0.58, "sv"[b % 2])
+            cp(T.z[:, b:4 * C:4], T.tp[:, TP * b:TP * b + 402].indirect(T.o_z[:]), "tp%d tn%d tpz tpy o_z" % (b, b), "z%d" % b, 0.58)
         quant(T.qz[:], T.sz[:], T.z[:], "z0 z1 z2 z3", "qz", C)
 
     def contest(t):
@@ -228,7 +231,7 @@ def rank_program(g, core, T, topo):
             tt(T.ms[:, 16 * h:16 * h + 16], bank("pb", h + 1, 105, 121), T.nb[:, 16 * h:16 * h + 16], A.add, "PB%d nb" % (h + 1), "ms%d" % h)
         for b in range(4):
             mm(bank("pa", b, 0, C), *part(T.qw, T.sw, 128 * b, 128 * b + 128), T.qz[:], T.sz[:], False, True, "qz qw sw", "PA%d" % b)
-            mul(T.xn[:, b:4 * C:4], bank("pa", b, 0, C), 0.015625, "PA%d" % b, "x%d" % b, 0.36, "s" if t < R - 1 else "sv")
+            mul(T.xn[:, b:4 * C:4], bank("pa", b, 0, C), 0.015625, "PA%d" % b, "x%d" % b, 0.36)
         tt(T.rowm[:], bank("pb", 0, 0, C), T.ds[:], A.add, "PB0 ds", "rowm", 0.36)
         for h in range(3):
             act(seg(T.sg, h), T.rowm[:], F.Sign, "rowm ms%d" % h, "sg%d sa%d" % (h, h), 0.38, scale=-1.0, bias=T.ms[:, 16 * h + 5:16 * h + 6],
@@ -238,26 +241,31 @@ def rank_program(g, core, T, topo):
         tt(T.ge[:, 1:48], T.ms[:, 1:48], T.rm[:, 0:47], A.is_ge, "ms0 ms1 ms2 rm", "ge", 0.13)
         scan(T.nm[:, 0:47], T.ge[:, 0:47], T.de[:, 0:47], A.mult, A.add, "ge gez de", "nm", 0.08)
         for h in range(3):
-            ts(seg(T.eq, h), seg(T.sg, h), 0.0, A.is_equal, None, None, "sg%d" % h, "eq%d" % h, 0.2)
+            if h == 2:
+                ts(seg(T.eq, h), T.rowm[:], T.ms[:, 37:38], A.is_equal, None, None, "rowm ms2", "eq2", 0.36)
+            else:
+                ts(seg(T.eq, h), seg(T.sg, h), 0.0, A.is_equal, None, None, "sg%d" % h, "eq%d" % h, 0.2)
             scan(seg(T.fs, h), T.fl[:, 192 - 96 * h:512 - 96 * h], seg(T.eq, h), A.mult, A.add, "fl eq%d rd%d%d" % (h, t, h), "fs%d" % h, 0.2,
                  T.rd[:, 16 * t + h:16 * t + h + 1])
         tt(T.sm[:, 8:11], T.fs[:, C - 1:3 * C:C], T.sm[:, 4:7], A.is_gt, "fs0 fs1 fs2 thr", "con")
+        tt(T.mk[:, 0:3], T.sm[:, 8:11], T.sm[:, 12:15], A.subtract, "con was", "mk")
         for h in range(3):
             ts(T.kill[:, h:4 * C:4], T.iob[:], T.nm[:, 16 * h + 14:16 * h + 15], A.is_equal, T.sm[:, 8 + h:9 + h], A.mult, "iob nm con", "k%d" % h, 0.2)
             n = 96 if h < 2 else 128
-            mul(T.kill[:, 384 * h + 3:384 * h + 4 * n:4], T.id32[:, 0:n], T.sm[:, 8 + h:9 + h], "id32 con", "km%d" % h, 0.14)
+            mul(T.kill[:, 384 * h + 3:384 * h + 4 * n:4], T.id32[:, 0:n], T.mk[:, h:h + 1], "id32 mk", "km%d" % h, 0.14)
         quant(T.qk[:], T.sk[:], T.kill[:], "k0 k1 k2 km0 km1 km2", "qk", C)
-        mm(bank("pb", 0, 0, C), T.qo[:], T.so[:], T.qk[:], T.sk[:], True, True, "qo qk", "PB0")
+        for j in range(2):
+            mm(bank("pb", j, 0, 160), T.qo[:], T.so[:], *part(T.qk, T.sk, 160 * j, 160 * j + 160), True, True, "qo qk", "PB%d" % j, 160)
 
     def dead_cells(t):
         for h in range(3):
-            mm(bank("pb", h + 1, 0, 128), *part(T.qk, T.sk, 96 * h, 96 * h + 128), T.qo[:], T.so[:], True, True, "qo qk", "PB%d" % (h + 1), 128)
-            act(T.rd[:, 16 * t + 16 + h:16 * t + 17 + h], bank("pb", h + 1, 0, 1), F.Relu, "PB%d rd%d%d" % (h + 1, t, h), "rd%d%d" % (t + 1, h),
+            mm(bank("pb", 3 - h, 0, 128), *part(T.qk, T.sk, 96 * h, 96 * h + 128), T.qo[:], T.so[:], True, True, "qo qk", "PB%d" % (3 - h), 128)
+            act(T.rd[:, 16 * t + 16 + h:16 * t + 17 + h], bank("pb", 3 - h, 0, 1), F.Relu, "PB%d rd%d%d" % (3 - h, t, h), "rd%d%d" % (t + 1, h),
                 bias=T.rd[:, 16 * t + h:16 * t + h + 1])
 
     dma("y", T.seatb[:], T.seat[:], "d_seat", "", "seatb Pload")
-    dma("s", T.alv[0:16, :], T.alive[:], "d_al0", "", "alv0")
-    dma("y", T.alv[16:32, :], T.alive[:], "d_al1", "", "alv1 Pload")
+    for j in range(4):
+        dma("sy"[j % 2], T.alv[16 * j:16 * j + 16, :], T.alive[:], "d_al%d" % (j % 2), "", "alv%d" % j + " Pload" * (j % 2))
     dma("y", T.xt[:, 0:4 * C], T.x[:], "d_x", "", "xt Pload", 3.5)
     dma("y", T.ut[:], T.u[:], "d_u", "", "ut Pload", 2.5)
     dma("y", T.qw[:].bitcast(dt.uint8), T.wc[:], "d_wc", "", "qw Pload", 3.2)
@@ -314,18 +322,19 @@ def rank_program(g, core, T, topo):
     lin("s", tb(8), "tb8", tb(6), "tb6", 1, -19.5, small, F.Abs)
     tt(tb(11), tb(7), tb(6), A.add, "tb7 tb6", "tb11", 0.09)
     ts(tb(10), tb(8), 20.0, A.is_gt, 400.0, A.mult, "tb8", "tb10")
-    tt(tb(9), tb(10), tb(11), A.max, "tb10 tb11", "tb9", 0.09)
-    ts(T.o_sig[:, 0:27], tb(9), 400.0, A.min, None, None, "tb9", "o_sig")
-    for a in range(4):
-        cp(T.o_alive[32 * a:32 * a + 32, :], T.alv[0:32, :], "alv0 alv1", "o_al%d" % a, q="v")
+    ts(tb(9), tb(11), 400.0, A.min, None, None, "tb11", "tb9")
+    tt(T.o_sig[:, 0:27], tb(10), tb(9), A.max, "tb10 tb9", "o_sig", 0.09)
+    for a in range(2):
+        cp(T.o_alive[64 * a:64 * a + 64, :], T.alv[0:64, :], "alv0 alv1 alv2 alv3", "o_al%d" % a, q="v")
     cp(T.o_seat[:], T.seatb[:], "seatb", "o_seat", q="v")
-    cp(T.dead[:], T.w10[:].indirect(T.o_alive[:]), "w10 " + al, "dead", 0.58)
+    cp(T.dead[:], T.w10[:].indirect(T.o_alive[:]), "w10 " + al, "dead0 dead1", 0.58)
     cp(T.idwin[:, W:W + C], T.iof[:].indirect(T.o_seat[:]), "iof o_seat", "idwd", 0.58)
     for j, a, b in ((0, 0, 14), (1, 14, 27)):
         cp(T.idseq[:, 16 * a:16 * b], T.idwin[:].indirect(T.o_sig[:, a:b]), "idwa idwb idwc idwd o_sig", "idseq%d" % j, 0.42)
     ids = "idseq0 idseq1 idseqz"
     rays(0)
-    tt(T.delta[:], T.idseq[:, 0:K], T.idseq[:, 1:K + 1], A.subtract, ids, "delta", 0.93)
+    tt(T.delta[:, 0:223], T.idseq[:, 0:223], T.idseq[:, 1:224], A.subtract, "idseq0", "delta0", 0.5)
+    tt(T.delta[:, 223:K], T.idseq[:, 223:K], T.idseq[:, 224:K + 1], A.subtract, ids, "delta", 0.47)
     bits(1, p, "ik", 2, 3)
     bits(2, p, "ik", 0, 3)
     bits(3, p, "ik", 0, 15)
@@ -346,9 +355,9 @@ def rank_program(g, core, T, topo):
     tt(T.aend[:], T.idseq[:].indirect(T.o_end1[:, 0:3]), T.lend[:], A.add, ids + " o_end1 lend", "aend", 0.13)
     send(0, "xt")
 
-    op("v", V.tensor_copy, (T.inv[:].indirect(T.o_seat[:]), T.iob[:]), "iob o_seat", "inv", 1.32)
-    tt(T.invm[:], T.inv[:], T.l16[:], A.add, "inv l16", "invm", 0.7)
-    scan(T.invs[:], T.r16[:], T.invm[:], A.max, A.min, "r16 invm", "invs", 0.2)
+    tt(T.invm[:], T.l16[:].indirect(T.o_seat[:]), T.iob[:], A.add, "iob l16 o_seat", "invm", 0.57)
+    op("v", V.tensor_copy, (T.inv[:].indirect(T.o_seat[:]), T.invm[:]), "invm o_seat", "inv", 1.32)
+    scan(T.invs[:], T.r16[:], T.inv[:], A.max, A.min, "r16 inv", "invs", 0.2)
     lin("v", tc(6), "tc6", T.o_alive[:], al, -1000, 1000)
     lin("sv", tc(0), "tc0", T.invs[:, 15:C:16], "invs", 0.025, 140.5 / W)
     ts(tc(1), tc(0), RND, A.add, -RND, A.add, "tc0", "tc1")
@@ -362,7 +371,7 @@ def rank_program(g, core, T, topo):
     for b in range(4):
         quant(*part(T.qe, T.se, 128 * b, 128 * b + 128), T.eb[:, 3 - b:515 - b], "eb", "qe%d" % b)
     lin("s", T.k1024[:], "k1024", T.k64[:, 0:512], "k64", 16, 0, 0.57)
-    lin("s", T.id32[:], "id32", T.fl[:, 192:320], "fl", 16, -16, 0.16)
+    lin("s", T.id32[:], "id32", T.f64[:, 192:320], "f64", 0.25, -16, 0.16)
     quant(T.qo[:], T.so[:], T.k1024[:], "k1024", "qo")
     quant(T.qu[:], T.su[:], T.ut[:], "ut", "qu")
     quant(T.qv[:], T.sv[:], T.vt[:], "vt", "qv")
@@ -390,12 +399,15 @@ def rank_program(g, core, T, topo):
     for t in range(R):
         xb = "xn" if t else "xt"
         if t:
-            tt(T.dead[:], bank("pb", 0, 0, C), T.ds[:], A.is_gt, "PB0 ds", "dead", 0.36)
+            ts(T.dead[:, 0:160], bank("pb", 0, 0, 160), 0.5, A.is_gt, None, None, "PB0", "dead0", 0.2)
+            act(T.dead[:, 160:C], bank("pb", 1, 0, 160), F.Relu, "PB1", "dead1", 0.2)
             rays(t)
             send(t, xb)
-            tt(T.adyn[:], bank("pb", 0, 0, C), T.l16[:] if t == 1 else T.adyn[:], A.max, "PB0 l16 adyn", "adyn", 0.36)
+            for j in range(2):
+                tt(T.adyn[:, 160 * j:160 * j + 160], bank("pb", j, 0, 160), T.l16[:, 0:160], A.max, "PB%d l16" % j, "adyn%d" % j, 0.2)
             dead_cells(t - 1)
-        mul(T.ds[:], T.dead[:], -BIG, "dead", "ds", 0.36, "s")
+        mul(T.ds[:], T.dead[:], -1.0e24, "dead0 dead1", "ds", 0.36, "s")
+        act(T.sm[:, 12:15], T.rd[:, 16 * t:16 * t + 3], F.Sign, "rd%d0 rd%d1 rd%d2" % (t, t, t), "was")
         unpack(t, xb)
         zlist(t)
         elist()
@@ -403,14 +415,16 @@ def rank_program(g, core, T, topo):
         contest(t)
 
     quant(T.qx3[:], T.sx3[:], T.xn[:, 0:4 * C], xs, "qx3", C)
-    mm(bank("pb", 1, 0, C), T.qv[:], T.sv[:], T.qx3[:], T.sx3[:], True, True, "qv qx3", "PB1")
+    for j in range(2):
+        mm(bank("pa", j, 0, 160), T.qv[:], T.sv[:], *part(T.qx3, T.sx3, 160 * j, 160 * j + 160), True, True, "qv qx3", "PA%d" % j, 160)
+        cp(T.ysb[:, 160 * j:160 * j + 160], bank("pa", j, 0, 160), "PA%d" % j, "ysb%d" % j, 0.2, "sv")
+        ts(T.olb[0:32, 160 * j:160 * j + 160], T.pb[0:32, 512 * j:512 * j + 160], 0.5, A.is_lt, None, None, "PB%d" % j, "ol%d" % j, 0.2)
     dma("y", T.oc[:], T.qx3[:].bitcast(dt.uint8), "d_out", "qx3", "", 2.9)
-    cp(T.ysb[:], bank("pb", 1, 0, C), "PB1", "ysb", 0.36, "sv")
-    dma("s", T.y[:], T.ysb[:], "d_out", "ysb", "", 2.9)
+    for j in range(2):
+        dma("sy"[j], T.y[:, 160 * j:160 * j + 160], T.ysb[:, 160 * j:160 * j + 160], "d_out", "ysb%d" % j, "", 2.6)
     for k in range(4):
         dma("y", T.osc[4 * k:4 * k + 4, :], T.sx3[32 * k:32 * k + 4, :], "d_out", "qx3", "")
-    tt(T.olb[0:32, :], T.pb[0:32, 0:C], T.ds[0:32, :], A.is_le, "PB0 ds", "olb", 0.36)
-    dma("y", T.ol[:], T.olb[0:1, :], "d_out", "olb", "")
+    dma("y", T.ol[:], T.olb[0:1, :], "d_out", "ol0 ol1", "")
 
     n, wake = len(steps), OPT["wake"]
     after = [[] for _ in steps]
@@ -421,46 +435,55 @@ def rank_program(g, core, T, topo):
     for i in range(n - 1, -1, -1):
         tail[i] = steps[i]["done"] + max([tail[j] + wake for j in after[i]] + [0.0])
 
+    firm, loose = [list(s["firm"]) for s in steps], [list(s["loose"]) for s in steps]
+    busy, done, ways = [s["busy"] for s in steps], [s["done"] for s in steps], [list(s["ways"]) for s in steps]
+    kind = [(s["sem"] or "c")[0:4] for s in steps]
+
     def lay(tail):
-        left = [len(s["firm"] | s["loose"]) for s in steps]
-        ready = [i for i in range(n) if not left[i]]
+        left = [len(firm[i]) + len(loose[i]) for i in range(n)]
+        ready = {i: [(0.0, q) for q in ways[i]] for i in range(n) if not left[i]}
         free, end, queue, plan = {q: 0.0 for q in qs}, [0.0] * n, [None] * n, []
-
-        def earliest(i):
-            best = None
-            for q in steps[i]["ways"]:
-                t0 = max([free[q]] + [end[j] + wake for j in steps[i]["firm"]] + [end[j] + wake for j in steps[i]["loose"] if queue[j] != q])
-                if best is None or t0 < best[0] - 0.02:
-                    best = (t0, q)
-            return best
-
         while ready:
-            at = {i: earliest(i) for i in ready}
-            x = min(ready, key=lambda i: (at[i][0], -tail[i]))
-            for y in sorted(ready, key=lambda i: -tail[i]):
-                if tail[y] <= tail[x]:
-                    break
-                (tx, qx), (ty, qy) = at[x], at[y]
-                bx = tx + steps[x]["busy"]
-                if qx == qy and ty < bx and bx + tail[y] > max(ty + tail[y], ty + steps[y]["busy"] + tail[x]) + OPT["eps"]:
-                    x = y
-                    break
+            at, x = {}, None
+            for i in ready:
+                best = None
+                for t0, q in ready[i]:
+                    t0 = max(t0, free[q])
+                    if best is None or t0 < best[0] - 0.02:
+                        best = (t0, q)
+                at[i] = best
+                if x is None or (best[0], -tail[i]) < (at[x][0], -tail[x]):
+                    x = i
+            (tx, qx), z = at[x], None
+            bx = tx + busy[x]
+            for y in ready:
+                ty, qy = at[y]
+                if qy == qx and tail[y] > tail[x] and ty < bx and (z is None or tail[y] > tail[z]) \
+                        and bx + tail[y] > max(ty + tail[y], ty + busy[y] + tail[x]) + OPT["eps"]:
+                    z = y
+            x = x if z is None else z
             t0, q = at[x]
-            queue[x], free[q], end[x] = q, t0 + steps[x]["busy"], t0 + steps[x]["done"]
+            queue[x], free[q], end[x] = q, t0 + busy[x], t0 + done[x]
             plan.append(x)
-            ready.remove(x)
+            del ready[x]
             for j in after[x]:
                 left[j] -= 1
                 if not left[j]:
-                    ready.append(j)
+                    t1 = max([0.0] + [end[k] + wake for k in firm[j]])
+                    ready[j] = [(max([t1] + [end[k] + wake for k in loose[j] if queue[k] != q1]), q1) for q1 in ways[j]]
         return max(end), plan, queue
 
-    def replay(plan, queue, wk, hop):
+    def replay(plan, queue, wk, hop, first, slow):
         free, end = {q: 0.0 for q in qs}, [0.0] * n
         for i in plan:
-            s, q = steps[i], queue[i]
-            t0 = max([free[q]] + [end[j] + wk for j in s["firm"]] + [end[j] + wk for j in s["loose"] if queue[j] != q])
-            free[q], end[i] = t0 + s["busy"], t0 + s["done"] + (hop if s["sem"] and s["sem"][0] == "a" else 0.0)
+            q, t0 = queue[i], free[queue[i]]
+            for j in firm[i]:
+                t0 = max(t0, end[j] + wk)
+            for j in loose[i]:
+                if queue[j] != q:
+                    t0 = max(t0, end[j] + wk)
+            k, more = (slow, 0.0) if kind[i] == "c" else (1.0, hop + (first if kind[i] == "arr0" else 0.0) if kind[i][0] == "a" else 0.0)
+            free[q], end[i] = t0 + k * busy[i], t0 + k * done[i] + more
         return max(end)
 
     if "best" not in OPT:
@@ -473,7 +496,7 @@ def rank_program(g, core, T, topo):
                 seed = (seed * 1103515245 + 12345) % 2147483648
                 other[i] += OPT["jit"] * (seed / 1073741824 - 1)
             got = lay([tail[i] + other[i] for i in range(n)])
-            cost = got[0] + replay(got[1], got[2], 0.5 * wake, -0.7) + replay(got[1], got[2], 2.5 * wake, 0.7)
+            cost = got[0] + replay(got[1], got[2], 1.6 * wake, 0.7, 0.5, 0.85) + replay(got[1], got[2], wake, -0.3, -1.2, 1.25)
             if best is None or cost <= best[0]:
                 best, push = (cost, got[1], got[2], got[0]), other
         OPT["best"] = best

@@ -1,10 +1,10 @@
 from concourse.bass import DstId, RemoteDMATransfer
 from concourse.mybir import dt, AluOpType as A, ActivationFunctionType as F
 
-H, W, C, M, R = 8, 40, 320, 24, 3
-K = 432
-TP = 416
+W, C, L, M, R = 40, 320, 256, 24, 3
+K, KP = 360, 368
 X4, U8, BF, F32, I32, U16 = "float8_e4m3fn_x4", "uint8", "bfloat16", "float32", "int32", "uint16"
+SIZE = {X4: 4, U8: 1, BF: 2, F32: 4, I32: 4, U16: 2}
 
 
 def _sb(n, d):
@@ -12,33 +12,36 @@ def _sb(n, d):
 
 
 SCRATCH = {
-    "seatb": _sb(20, I32), "alv": _sb(20, I32), "ik": _sb(28, I32), "ib": _sb(16, I32), "ik9": _sb(4, I32),
-    "o_seat": _sb(20, U16), "o_alive": _sb(20, U16), "o_sig": _sb(28, U16), "o_end": _sb(4, U16), "o_end1": _sb(4, U16),
-    "o_pos": _sb(20, U16), "o_z": _sb(20, U16), "o_cmp": _sb(10, U16), "o_u": _sb(10, U16), "o_g": _sb(4, U16), "o_dc": _sb(2, U16),
-    "cf": _sb(64, F32), "kt": _sb(28, F32), "tb": _sb(15 * 28, F32), "tc": _sb(9 * 20, F32), "ctab0": _sb(20, F32),
-    "iof": _sb(C, F32), "iob": _sb(C, BF), "c16": _sb(C, F32), "l16": _sb(C, BF), "r16": _sb(C, BF), "j4": _sb(48, F32),
-    "lend": _sb(48, F32), "aend": _sb(48, F32), "r4": _sb(48, F32), "rm16": _sb(48, F32), "cc": _sb(48, F32),
-    "w10": _sb(16, BF), "idwin": _sb(416, F32), "dwin": _sb(416, BF), "dead": _sb(C, BF), "ds": _sb(C, BF),
-    "idseq": _sb(448, F32), "delta": _sb(K, F32), "dseq": _sb(K, BF), "st": _sb(K, F32),
-    "inv": _sb(C, BF), "invm": _sb(C, BF), "invs": _sb(C, BF),
-    "ev": _sb(48, F32), "es": _sb(48, F32), "adyn": _sb(C, F32), "zv": _sb(C, F32), "zs": _sb(C, F32), "zt": _sb(20, F32),
-    "vraw": _sb(C, F32), "tr": _sb(C, F32), "gb": _sb(96, F32), "e": _sb(48, F32), "nb": _sb(48, F32), "de": _sb(48, F32),
-    "ms": _sb(48, F32), "rm": _sb(48, F32), "ge": _sb(48, F32), "nm": _sb(48, F32), "rd": _sb(48, F32), "sm": _sb(16, F32), "mk": _sb(4, F32),
-    "rowm": _sb(C, F32), "sg": _sb(3 * C, BF), "eq": _sb(3 * C, BF), "fs": _sb(3 * C, BF),
-    "f64": _sb(512, BF), "k64": _sb(516, BF), "eb": _sb(516, BF), "fl": _sb(512, BF), "id32": _sb(128, BF), "k1024": _sb(512, BF),
-    "xt": _sb(1296, BF), "xn": _sb(1296, BF), "ut": _sb(512, BF), "vt": _sb(512, BF), "tp": _sb(4 * TP, BF),
-    "z": _sb(4 * C, BF), "kill": _sb(4 * C, BF), "cm": _sb(512, BF), "ysb": _sb(C, F32), "olb": _sb(C, F32),
+    "seatb": _sb(20, I32), "alv": _sb(20, I32), "ik": _sb(24, I32), "ib": _sb(16, I32), "oi": _sb(32, I32),
+    "o_seat": _sb(20, U16), "o_al": _sb(20, U16), "o_p": _sb(24, U16), "o_o": _sb(24, U16), "o_live": _sb(16, U16),
+    "o_dead": _sb(8, U16), "o_slot": _sb(20, U16), "o_pos": _sb(16, U16), "o_ray": _sb(24, U16), "o_z": _sb(64, U16), "o_cmp": _sb(10, U16),
+    "o_u": _sb(10, U16), "o_g": _sb(2, U16),
+    "cf": _sb(64, F32), "kt": _sb(24, F32), "kt1": _sb(20, F32), "tb": _sb(24 * 40, F32), "sums": _sb(20, F32), "bt": _sb(20, F32),
+    "pm": _sb(8, I32), "win": _sb(C + 1, F32), "one": _sb(384, BF), "c16": _sb(KP, F32), "l16": _sb(KP, BF), "r16": _sb(KP, BF), "rl16": _sb(C, BF),
+    "v256": _sb(L, F32), "l4c": _sb(L, F32), "r4z": _sb(L, F32), "r4": _sb(144, F32), "lend": _sb(80, F32), "iob": _sb(L, BF),
+    "w0": _sb(C, F32), "wb": _sb(416, F32), "vb": _sb(416, F32), "wr": _sb(KP, F32), "own": _sb(KP, F32), "delta": _sb(KP, F32),
+    "am": _sb(KP, BF), "ams": _sb(KP, BF), "al": _sb(C, BF), "pre": _sb(C, BF), "dpre": _sb(C, BF), "ps": _sb(C, BF),
+    "junk": _sb(1280, BF), "junk2": _sb(1088, BF), "inv": _sb(C, BF), "pz": _sb(L, BF), "pzs": _sb(L, BF),
+    "dead": _sb(352, BF), "dseq": _sb(KP, BF), "st": _sb(K, F32), "ev": _sb(W, F32), "es": _sb(W, F32),
+    "adyn": _sb(L, F32), "zv": _sb(L, F32), "zs": _sb(L, F32), "tr": _sb(L, F32), "gb": _sb(272, F32),
+    "cc": _sb(32, F32), "rm16": _sb(32, F32), "e": _sb(32, F32), "nb": _sb(32, F32), "de": _sb(32, F32), "ms": _sb(32, F32), "rm": _sb(32, F32),
+    "ge": _sb(32, F32), "nm": _sb(32, F32), "sm": _sb(8, F32),
+    "rowm": _sb(L, F32), "sg": _sb(2 * L, BF), "eq": _sb(2 * L + 2, BF), "fs": _sb(2 * L + 2, BF), "ds": _sb(L, BF),
+    "k64": _sb(516, BF), "eb": _sb(516, BF), "fl": _sb(2 * L + 2, BF), "idm": _sb(128, BF), "ko": _sb(512, BF),
+    "xt": _sb(1296, BF), "xn": _sb(1040, BF), "ut": _sb(512, BF), "vt": _sb(512, BF), "tl": _sb(1872, BF),
+    "z": _sb(4 * L, BF), "kill": _sb(4 * L, BF), "ysb": _sb(C, F32), "olw": _sb(C, BF), "olb": _sb(C, F32),
     "qe": _sb(512, X4), "se": _sb(512, U8), "qw": _sb(512, X4), "sw": _sb(512, U8), "qu": _sb(128, X4), "su": _sb(128, U8),
     "qu2": _sb(144, X4), "su2": _sb(144, U8), "qv": _sb(128, X4), "sv": _sb(128, U8), "qo": _sb(128, X4), "so": _sb(128, U8),
-    "qz": _sb(C, X4), "sz": _sb(C, U8), "qk": _sb(C, X4), "sk": _sb(C, U8), "qc": _sb(384, X4), "sc": _sb(384, U8),
-    "qx0": _sb(400, X4), "sx0": _sb(400, U8), "qx1": _sb(400, X4), "sx1": _sb(400, U8), "qx2": _sb(400, X4), "sx2": _sb(400, U8),
-    "qx3": _sb(C, X4), "sx3": _sb(C, U8),
+    "qa": _sb(C, X4), "sa": _sb(C, U8), "qd": _sb(128, X4), "sd": _sb(128, U8), "qd2": _sb(128, X4), "sd2": _sb(128, U8),
+    "qf": _sb(C, X4), "sf": _sb(C, U8),
+    "qz": _sb(L, X4), "sz": _sb(L, U8), "qk": _sb(L, X4), "sk": _sb(L, U8),
+    "qx0": _sb(464, X4), "sx0": _sb(464, U8), "qx1": _sb(464, X4), "sx1": _sb(464, U8), "qx2": _sb(464, X4), "sx2": _sb(464, U8),
+    "qx3": _sb(384, X4), "sx3": _sb(384, U8),
     "pa": ("psum", [128, 2048], F32), "pb": ("psum", [128, 2048], F32),
 }
 SEMAPHORES = ["cv", "cs", "ct", "cg", "sent", "arr0", "arr1", "arr2", "d_seat", "d_al0", "d_al1", "d_x", "d_u", "d_v", "d_wc", "d_ws", "d_out"]
-COLS = ("ng16 t1 t2 t3 t4 ndr ndc h v invl nl a1 a3 a3s a3b b1 b3 b3b ke ke1 q6 tq tmax ni6 c1 c2 c2b d1 d1b d2 d2b d3 d3s d3b "
-        "y0 y1 y2 y3 y4").split()
-OPT = {"seed": 1, "jit": 1.0, "muts": 8, "turns": 6000, "eps": 0.1, "hop": 2.7, "first": 2.5, "wake": 0.13, "small": 0.07}
+OPT = {"seed": 1, "turns": 40000, "slack": 0.3, "eps": 0.1, "hop": 2.7, "first": 2.5, "wake": 0.17, "cyc": 0.00104, "gat": 1.56, "sca": 3.8,
+       "guesses": ((0.8, 0.05, 0.13, 1.0, 0.0, 0.0), (0.85, 0.0, 0.24, 1.0, -0.8, -0.5), (1.0, 0.0, 0.13, 1.9, 0.0, 0.0), (1.2, 0.03, 0.2, 1.4, 0.5, 0.3))}
 
 
 def rank_program(g, core, T, topo):
@@ -49,395 +52,488 @@ def rank_program(g, core, T, topo):
     below, above = T.cores[(rank + 1) % n_ranks], T.cores[(rank - 1) % n_ranks]
     qs = {"v": g.vector, "s": g.scalar, "t": g.tensor, "g": g, "y": g.sync}
     V, S, PE = g.vector, g.scalar, g.tensor
-    steps, writer, readers = [], {}, {}
-    small = OPT["small"]
+    steps, seen, names = [], {}, []
+    cyc = OPT["cyc"]
 
-    def step(ways, r, w, busy, done=None, sem=None):
-        r, w = r.split(), w.split()
-        firm, loose = set(), set()
-        for k in r:
-            firm.update([writer[k]] if k in writer else [])
-            if k[0] == "P":
-                loose.update(readers.get(k, []))
-        for k in w:
-            firm.update(readers.get(k, []))
-            if k in writer:
-                (loose if k[0] == "P" else firm).add(writer[k])
-        n = len(steps)
-        steps.append({"ways": ways, "firm": firm, "loose": loose - firm, "busy": busy, "done": done or busy, "sem": sem})
-        for k in r:
-            readers.setdefault(k, []).append(n)
-        for k in w:
-            writer[k] = n
-            readers[k] = []
+    def v(name, lo=0, hi=None, by=1, p=(0, 128)):
+        return (name, range(lo, SCRATCH[name][1][1] if hi is None else hi, by), p, None)
 
-    def op(q, call, args, r, w, us=small, **kw):
-        step({q: (call, args, kw)}, r, w, us)
+    def ind(win, off):
+        return win[0:3] + (off,)
 
-    def dma(q, out, in_, sem, r, w, us=1.9):
-        step({q: (qs[q].dma_start, (out, in_), {})}, r, w, 0.1, us, sem)
+    def ap(x, cast=None):
+        if not isinstance(x, tuple):
+            return x
+        a = T[x[0]][x[2][0]:x[2][1], x[1].start:x[1].stop:x[1].step]
+        a = a.bitcast(cast) if cast else a
+        return a.indirect(ap(x[3])) if x[3] else a
 
-    def ts(out, in0, s1, op0, s2, op1, r, w, us=small):
-        op("v", V.tensor_scalar, (out, in0, s1, s2, op0) + (() if s2 is None else (op1,)), r, w, us)
+    def step(ways, r, w, busy, done=None, sem=None, chain=None):
+        n, firm, loose = len(steps), set(), set()
+        r = [x for x in r if isinstance(x, tuple)]
+        r += [x[3] for x in r + w if x[3]]
+        for x, writes in [(x, False) for x in r] + [(x, True) for x in w]:
+            if SCRATCH[x[0]][0] == "psum":
+                key = (x[0], x[1].start // 512)
+                for j, wj in seen.get(key, []):
+                    (firm if wj != writes else loose).add(j)
+                seen[key] = [(n, True)] if writes else seen.get(key, []) + [(n, False)]
+                continue
+            cols = set(x[1])
+            for j, wj, pj, cj in seen.setdefault(x[0], []):
+                if j != n and (writes or wj) and pj[0] < x[2][1] and x[2][0] < pj[1] and not cols.isdisjoint(cj):
+                    firm.add(j)
+            seen[x[0]].append((n, writes, x[2], cols))
+        if chain:
+            loose.update(seen.get(chain, []))
+            seen[chain] = [n]
+        firm.discard(n)
+        loose.discard(n)
+        steps.append({"ways": ways, "firm": firm, "loose": loose - firm, "busy": busy, "done": done, "sem": sem})
 
-    def tt(out, a, b, o, r, w, us=small):
-        op("v", V.tensor_tensor, (out, a, b, o), r, w, us)
+    def cost(q, out, ins, per):
+        big = [x for x in [out] + ins if isinstance(x, tuple) and (len(x[1]) > 1 or x is out)]
+        for x in big:
+            if x[3]:
+                return 0.06 + 16 * len(x[3][1]) * cyc * OPT["sca" if x is out else "gat"]
+        if q == "v" and per == 1 and all(SIZE[SCRATCH[x[0]][2]] == 2 for x in big):
+            per = 0.5
+        return max(64, len(out[1]) * per) * cyc
 
-    def cp(out, a, r, w, us=small, q="vs"):
-        ways = {"v": (V.tensor_copy, (out, a), {}), "s": (S.activation, (out, a, F.Copy), {})}
-        step({k: ways[k] for k in q}, r, w, us)
+    def op(ways, out, ins, per=1, more=()):
+        step(ways, ins, [out] + list(more), {q: cost(q, out, ins, per) for q in ways})
 
-    def mul(out, a, c, r, w, us=small, q="sv"):
-        ways = {"v": (V.tensor_scalar, (out, a, c, None, A.mult), {}), "s": (S.activation, (out, a, F.Copy), {"scale": c})}
-        step({k: ways[k] for k in q}, r, w, us)
+    def ts(out, a, s1, o0, s2=None, o1=None):
+        op({"v": (V.tensor_scalar, (ap(out), ap(a), ap(s1), ap(s2), o0) + (() if s2 is None else (o1,)), {})}, out, [a, s1, s2])
 
-    def scan(out, d0, d1, o0, o1, r, w, us, first=0.0):
-        op("v", V.tensor_tensor_scan, (out, d0, d1, first, o0, o1), r, w, us)
+    def tt(out, a, b, o):
+        op({"v": (V.tensor_tensor, (ap(out), ap(a), ap(b), o), {})}, out, [a, b], 1.01 if "p" in (SCRATCH[a[0]][0][0], SCRATCH[b[0]][0][0]) else 2)
 
-    def fill(ap, val, w):
-        op("v", V.memset, (ap, val), "", w)
+    def both(q, out, a, vway, sway, ins=()):
+        op({k: w for k, w in (("v", vway), ("s", sway)) if k in q}, out, [a] + list(ins))
 
-    def act(out, a, f, r, w, us=small, **kw):
-        op("s", S.activation, (out, a, f), r, w, us, **kw)
+    def cp(out, a, q="vs"):
+        both(q, out, a, (V.tensor_copy, (ap(out), ap(a)), {}), (S.activation, (ap(out), ap(a), F.Copy), {}))
 
-    def quant(q, s, a, r, w, n=128):
-        op("v", V.quantize_mx, (q, s, a), r, w, 0.015 + 0.0011 * n)
+    def mul(out, a, c, q="sv"):
+        both(q, out, a, (V.tensor_scalar, (ap(out), ap(a), ap(c), None, A.mult), {}), (S.activation, (ap(out), ap(a), F.Copy), {"scale": ap(c)}), [c])
 
-    def mm(out, lq, ls, rq, rs, start, stop, r, w, n=C):
-        op("t", PE.matmul_mx, (out, lq, ls, rq, rs, start, stop), r, w, (n + 16) * 0.0006)
+    def lin(out, a, m_, a_, q="sv", f=F.Identity):
+        m_, a_ = [col(x) if isinstance(x, str) else x if isinstance(x, tuple) else float(x) for x in (m_, a_)]
+        both(q if f == F.Identity else "s", out, a, (V.tensor_scalar, (ap(out), ap(a), ap(m_), ap(a_), A.mult, A.add), {}),
+             (S.activation, (ap(out), ap(a), f), {"scale": ap(m_), "bias": ap(a_)}), [m_, a_])
 
-    def iota(out, pat, base, cm, w, flt=True, r=""):
-        n = 1
-        for a in pat:
-            n *= a[1]
-        op("g", g.iota, (out, pat, base, cm), r, w, 0.13 + 0.0021 * n, **({"allow_small_or_imprecise_dtypes": True} if flt else {}))
+    def flag(out, a, q="vs"):
+        both(q, out, a, (V.tensor_scalar, (ap(out), ap(a), 1.0, None, A.min), {}), (S.activation, (ap(out), ap(a), F.Sign), {}))
+
+    def count_below(acc, out, a, bias, scale=1.0):
+        op({"s": (S.activation, (ap(out), ap(a), F.Sign), {"scale": scale, "bias": ap(bias), "accum_out": ap(acc)})}, out, [a, bias], 1.1, [acc])
+
+    def scan(out, d0, d1, o0, o1, first=0.0):
+        op({"v": (V.tensor_tensor_scan, (ap(out), ap(d0), ap(d1), first, o0, o1), {})}, out, [d0, d1])
+
+    def fill(out, val):
+        op({"v": (V.memset, (ap(out), val), {})}, out, [])
+
+    def qs_(name, lo=0, hi=None):
+        return v("q" + name, lo, hi), v("s" + name, lo, hi)
+
+    def quant(q, a):
+        step({"v": (V.quantize_mx, (ap(q[0]), ap(q[1]), ap(a)), {})}, [a], list(q), {"v": 0.015 + 0.0011 * len(q[0][1])})
+
+    def mm(out, l, r, start=True, stop=True):
+        step({"t": (PE.matmul_mx, (ap(out), ap(l[0]), ap(l[1]), ap(r[0]), ap(r[1]), start, stop), {})}, list(l + r), [out],
+             {"t": (len(out[1]) + 16) * 0.0006})
+
+    def pick(dst, src, off):
+        op({"v": (V.tensor_copy, (ap(dst[0], dt.uint32), ap(ind(src[0], off), dt.uint32)), {})}, dst[0], [ind(src[0], off)])
+        cp(dst[1], ind(src[1], off), "sv")
+
+    def iota(out, pat, base, cm=0):
+        kw = {} if SCRATCH[out[0]][2] == I32 else {"allow_small_or_imprecise_dtypes": True}
+        step({"g": (g.iota, (ap(out), pat, base, cm), kw)}, [], [out], {"g": 0.16 + 0.0021 * len(out[1])})
+
+    def select(out, a, o, fill_, base, cm):
+        step({"g": (g.affine_select, (ap(out), ap(a), [[1, len(out[1])]], o, fill_, base, cm), {})}, [a], [out], {"g": 0.21 + 0.0021 * len(out[1])})
+
+    def dma(q, out, in_, sem, r, w, us=1.9, chain=None):
+        step({q: (qs[q].dma_start, (out, in_), {})}, r, w, {q: 0.1}, us, sem, chain)
 
     def col(n):
-        return T.cf[:, COLS.index(n):COLS.index(n) + 1]
-
-    def lin(q, out, w, a, r, m_, a_, us=small, f=F.Identity):
-        rr = r + "".join(" " + x for x in (m_, a_) if isinstance(x, str))
-        m_, a_ = [col(x) if isinstance(x, str) else float(x) for x in (m_, a_)]
-        ways = {"v": (V.tensor_scalar, (out, a, m_, a_, A.mult, A.add), {}), "s": (S.activation, (out, a, f), {"scale": m_, "bias": a_})}
-        step({k: ways[k] for k in q}, rr, w, us)
+        if n not in names:
+            names.append(n)
+        return v("cf", names.index(n), names.index(n) + 1)
 
     def clin(w, a, m_, a_):
-        lin("sv", col(w), w, col(a), a, m_, a_)
+        lin(col(w), col(a), m_, a_)
 
-    def ib(j):
-        return T.ib[:, j:j + 1]
-
-    def bits(j, src, r, sh, mask):
+    def bits(j, src, sh, mask):
         if sh:
-            ts(ib(j), src, sh, A.logical_shift_right, mask, A.bitwise_and, r, "ib%d" % j)
+            ts(v("ib", j, j + 1), src, sh, A.logical_shift_right, mask, A.bitwise_and)
         else:
-            ts(ib(j), src, mask, A.bitwise_and, None, None, r, "ib%d" % j)
+            ts(v("ib", j, j + 1), src, mask, A.bitwise_and)
+        return v("ib", j, j + 1)
 
-    def tb(j, n=27):
-        return T.tb[:, 28 * j:28 * j + n]
+    def tmp(n, used=[0]):
+        steps_used = seen.setdefault("tmp", [0])
+        steps_used[0] += 1
+        return v("tb", 24 * steps_used[0] - 24, 24 * steps_used[0] - 24 + n)
 
-    def tc(j):
-        return T.tc[:, 20 * j:20 * j + 20]
+    def bank(name, b, lo, hi, by=1):
+        return v(name, 512 * b + lo, 512 * b + hi, by)
 
-    def bank(name, b, lo, hi):
-        return T[name][:, 512 * b + lo:512 * b + hi]
+    def halves(n):
+        return (("v", 0, (n + 1) // 2), ("s", (n + 1) // 2, n))
 
-    def part(q, s, lo, hi):
-        return q[:, lo:hi], s[:, lo:hi]
+    def gather2(fn, out, lo, win, off, n, free=False):
+        for q, a, b in halves(n):
+            fn(v(out, lo + 16 * a, lo + 16 * b), ind(win, v(off, a, b)), "vs" if free else q)
 
-    RND, FAR = 12582912.0, 1.0e5
-    p = T.ik[:, 0:1]
-    al = "o_al0 o_al1"
-    xs = " x0 x1 x2 x3"
+    def rounded(a):
+        o = tmp(len(a[1]))
+        ts(o, a, RND, A.add, -RND, A.add)
+        return o
 
-    def rays(t):
-        for q, a, b in (("v", 0, 10), ("s", 10, 20)):
-            cp(T.dwin[:, W + 16 * a:W + 16 * b], T.dead[:].indirect(T.o_seat[:, a:b]), "dead0 dead1 o_seat", "dwin" + q, 0.32, "vs" if t == 0 else q)
-        for q, a, b in (("v", 0, 14), ("s", 14, 27)):
-            o, w = T.dseq[:, 16 * a:16 * b], T.dwin[:].indirect(T.o_sig[:, a:b])
-            step({"v": (V.tensor_scalar, (o, w, 1.0, None, A.min), {}), "s": (S.activation, (o, w, F.Sign), {})},
-                 "dwinv dwins dwiny dwinz o_sig", "dseq" + q, 0.42)
+    def lin2(n, a, ma, b, mb, c):
+        x, y, o = tmp(n), tmp(n), tmp(n)
+        lin(x, a, ma, 0)
+        lin(y, b, mb, c)
+        tt(o, x, y, A.add)
+        return o
 
-    def send(t, xb):
-        scan(T.st[:], T.dseq[:], T.delta[:], A.mult, A.add, "dseqv dseqs delta0 delta", "st", 0.48)
-        tt(T.ev[:], T.st[:].indirect(T.o_end[:, 0:3]), T.aend[:], A.add, "st o_end aend", "ev", 0.13)
-        scan(T.es[:, 0:W], T.r4[:, 0:W], T.ev[:, 0:W], A.max, A.min, "r4 ev", "es", 0.08)
-        ts(T.o_cmp[:], T.es[:, 3:W:4], 4.0, A.mult, col("tmax"), A.min, "es tmax", "o_cmp")
+    RND, FAR, D = 12582912.0, 1.0e5, 4194304.0
+    p = v("ik", 0, 1)
+    E = [qs_("e", 128 * b, 128 * b + 128) for b in range(4)]
+
+    def send(t, xw):
         for q, a, b in (("v", 0, 6), ("s", 6, 10)):
-            cp(T.cm[:, 16 * a:16 * b], T[xb][:].indirect(T.o_cmp[:, a:b]), xb + " " + xb + "z o_cmp" + (xs if t else ""), "cm" + q, 0.2, q)
-        quant(*part(T.qc, T.sc, 128 * t, 128 * t + 128), T.cm[:], "cmv cms cmy cmz", "qc%d" % t)
+            cp(v("tl", 16 * a, 16 * b), ind(xw, v("o_cmp", a, b)), q)
+        x = "x%d" % t
+        quant(qs_(x, 0, 128), v("tl", 0, 512))
         calls = []
-        for src, dst, cast in ((T.qc, T["qx%d" % t], True), (T.sc, T["sx%d" % t], False)):
+        for name, cast in (("q" + x, dt.uint8), ("s" + x, None)):
             trs = []
             for j, to in enumerate((below, above)):
                 eng = topo.engines(core, to)
-                half = eng[j * len(eng) // 2:(j + 1) * len(eng) // 2]
+                half = eng[j::2]
                 rid, pid = topo.addr(to)[:2]
-                a, b = src[:, 128 * t:128 * t + W], dst[:, C + W * j:C + W * j + W]
                 trs.append(RemoteDMATransfer(dst_ids=[DstId(rid=rid, pnc=pid)], dma_engine_mask=sum(1 << e for e in half),
-                                             remote_sem=T.sem["arr%d" % t], src=a.bitcast(dt.uint8) if cast else a,
-                                             dst=b.bitcast(dt.uint8) if cast else b))
+                                             remote_sem=T.sem["arr%d" % t], src=ap(v(name, 0, W), cast),
+                                             dst=ap(v(name, 384 + W * j, 384 + W * j + W), cast)))
             calls.append(trs)
         late = 0.0 if t else OPT["first"]
-        step({"g": (calls, (), {})}, "qc%d" % t, "land%d" % t, 0.8 + late, OPT["hop"] + late, "arr%d" % t)
+        step({"g": (calls, (), {})}, list(qs_(x, 0, W)), list(qs_(x, 384, 464)), {"g": 0.8 + late}, OPT["hop"] + late, "arr%d" % t)
 
-    def unpack(t, xb):
-        q = part(T["qx%d" % t], T["sx%d" % t], 0, C)
-        quant(*q, T[xb][:, 0:4 * C], xb + (xs if t else ""), "qx%d" % t, C)
+    def unpack(t):
         for b in range(4):
-            mm(bank("pb", b, 0, C), *part(T.qe, T.se, 128 * b, 128 * b + 128), *q, True, True, "qe%d qx%d" % (b, t), "PB%d" % b)
-            mul(T.tp[:, TP * b:TP * b + C], bank("pb", b, 0, C), 0.015625, "PB%d" % b, "tp%d" % b, 0.36)
+            mm(bank("pa", b, 0, L), E[b], qs_("x%d" % t, 128, 384))
+            mul(v("tl", 512 + b, 1536, 4), bank("pa", b, 0, L), 0.015625)
+            mm(bank("pa", b, 0, L), E[b], qs_("x%d" % t, 128, 384), True, False)
+
+    def unpack_dead(q, lo):
         for b in range(4):
-            mm(bank("pa", b, 0, C), *part(T.qe, T.se, 128 * b, 128 * b + 128), *q, True, False, "qe%d qx%d" % (b, t), "PA%d" % b)
+            mm(bank("pb", 2 + b % 2, 0, 128), E[b], qs_(q, 0, 128))
+            mul(v("tl", 256 + b, 512, 4), bank("pb", 2 + b % 2, lo, lo + 64), 0.015625)
 
-    def zlist(t):
-        a, ak = (T.l16[:], "l16") if t == 0 else (T.adyn[:], "adyn0 adyn1")
-        tt(T.zv[:], T.st[:].indirect(T.o_pos[:]), a, A.add, "st o_pos " + ak, "zv", 0.57)
-        scan(T.zs[:], T.r16[:], T.zv[:], A.max, A.min, "r16 zv", "zs", 0.36)
-        tt(T.zt[:], T.zs[:, 15:C:16], T.ctab0[:], A.add, "zs ctab0", "zt")
-        ts(T.o_z[:], T.zt[:], 401.0, A.min, None, None, "zt", "o_z")
-
-    def elist():
-        cp(T.vraw[:], T.st[:].indirect(T.o_pos[:]), "st o_pos", "vraw", 0.58, "s")
-        op("v", V.transpose, (T.tr[:], T.vraw[:]), "vraw", "tr", 0.36)
+    def lists(t):
+        tt(v("zv"), ind(v("st"), v("o_pos")), v("adyn") if t else v("l4c"), A.add)
+        scan(v("zs"), v("r4z"), v("zv"), A.max, A.min)
+        ts(v("o_z"), v("zs", 3, L, 4), 4.0, A.mult)
+        op({"v": (V.transpose, (ap(v("tr")), ap(v("zv"))), {})}, v("tr"), [v("zv")])
+        scan(v("gb", 0, 64), v("r4", 80, 144), v("tr", 0, L, 4), A.max, A.min)
+        for a in (0, 64):
+            cp(v("gb", 67, 128, 4, (a, a + 64)), v("gb", 3, 64, 4, (64 - a, 128 - a)), "sv")
         for a in range(4):
-            for d in (a, a ^ 1):
-                cp(T.gb[32 * d:32 * d + 32, 20 * a:20 * a + 20], T.tr[32 * a:32 * a + 32, 0:C:16], "tr", "gb%d%d" % (a, d), q="sv")
-        cp(T.gb[64:128, 0:40], T.gb[0:64, 0:40], "gb00 gb01 gb10 gb11", "gbl", q="sv")
-        cp(T.gb[0:64, 40:80], T.gb[64:128, 40:80], "gb22 gb23 gb32 gb33", "gbh", q="sv")
-        tt(T.e[:], T.gb[:].indirect(T.o_g[:, 0:3]), T.cc[:], A.add,
-           "gb00 gb01 gb10 gb11 gb22 gb23 gb32 gb33 gbl gbh gbz o_g cc cc4 cc5 cc6 cc15", "e", 0.13)
-        act(T.nb[:], T.e[:], F.Relu, "e", "nb", 0.08, scale=1.0e27, bias=-159.5e27)
-        tt(T.de[:, 0:47], T.e[:, 0:47], T.e[:, 1:48], A.subtract, "e", "de", 0.13)
+            cp(v("gb", 131, 256, 4, (32 * a, 32 * a + 32)), v("gb", 3, 128, 4, (32 * (a ^ 1), 32 * (a ^ 1) + 32)), "sv")
+        tt(v("e"), ind(v("gb"), v("o_g")), v("cc"), A.add)
+        lin(v("nb"), v("e"), 1.0e26, -255.5e26, "s", F.Relu)
+        tt(v("de", 0, 31), v("e", 0, 31), v("e", 1, 32), A.subtract)
 
     def gather_z(t):
-        q = part(T["qx%d" % t], T["sx%d" % t], 272, 400)
         for b in range(4):
-            mm(bank("pb", b, 0, 128), *part(T.qe, T.se, 128 * b, 128 * b + 128), *q, True, True, "qe%d qx%d land%d" % (b, t, t), "PB%d" % b, 128)
+            mm(bank("pb", b, 0, 128), E[b], qs_("x%d" % t, 336, 464))
         for b in range(4):
-            mul(T.tp[:, TP * b + C + 1:TP * b + C + 81], bank("pb", b, 48, 128), 0.015625, "PB%d" % b, "tn%d" % b, 0.12)
-        for b in range(4):
-            cp(T.z[:, b:4 * C:4], T.tp[:, TP * b:TP * b + 402].indirect(T.o_z[:]), "tp%d tn%d tpz tpy o_z" % (b, b), "z%d" % b, 0.58)
-        quant(T.qz[:], T.sz[:], T.z[:], "z0 z1 z2 z3", "qz", C)
+            mul(v("tl", 1536 + b, 1856, 4), bank("pb", b, 48, 128), 0.015625, "vs"[b % 2])
+        gather2(cp, "z", 0, v("tl", 512, 1872), "o_z", 64)
+        quant(qs_("z"), v("z"))
 
     def contest(t):
         def seg(b, h):
-            return b[:, C * h:C * h + C]
+            return v(b, L * h, L * h + L)
 
-        mm(bank("pb", 0, 0, C), *part(T.qu2, T.su2, 0, 128), T.qz[:], T.sz[:], True, True, "qz qu2 su2", "PB0")
-        for h in range(3):
-            mm(bank("pb", h + 1, 0, 128), *part(T.qz, T.sz, 96 * h, 96 * h + 128), *part(T.qu2, T.su2, 16, 144), True, True,
-               "qz qu2 su2", "PB%d" % (h + 1), 128)
-            tt(T.ms[:, 16 * h:16 * h + 16], bank("pb", h + 1, 105, 121), T.nb[:, 16 * h:16 * h + 16], A.add, "PB%d nb" % (h + 1), "ms%d" % h)
+        if t:
+            mm(bank("pb", 0, 0, L), qs_("u2", 0, 128), qs_("z"))
+        for h in range(2):
+            mm(bank("pb", h + 2, 0, 128), qs_("z", 128 * h, 128 * h + 128), qs_("u2", 16, 144))
+            tt(v("ms", 16 * h, 16 * h + 16), bank("pb", h + 2, 105, 121), v("nb", 16 * h, 16 * h + 16), A.add)
+        if t:
+            tt(v("rowm"), bank("pb", 0, 0, L), v("ds"), A.add)
+            rows = [v("rowm"), v("rowm")]
+        else:
+            rows = [bank("pb", j, 0, L) for j in range(2)]
+            for j in range(2):
+                mm(rows[j], qs_("u2", 0, 128), qs_("z"))
         for b in range(4):
-            mm(bank("pa", b, 0, C), *part(T.qw, T.sw, 128 * b, 128 * b + 128), T.qz[:], T.sz[:], False, True, "qz qw sw", "PA%d" % b)
-            mul(T.xn[:, b:4 * C:4], bank("pa", b, 0, C), 0.015625, "PA%d" % b, "x%d" % b, 0.36)
-        tt(T.rowm[:], bank("pb", 0, 0, C), T.ds[:], A.add, "PB0 ds", "rowm", 0.36)
-        for h in range(3):
-            act(seg(T.sg, h), T.rowm[:], F.Sign, "rowm ms%d" % h, "sg%d sa%d" % (h, h), 0.38, scale=-1.0, bias=T.ms[:, 16 * h + 5:16 * h + 6],
-                accum_out=T.sm[:, h:h + 1])
-        lin("s", T.sm[:, 4:7], "thr", T.sm[:, 0:3], "sa0 sa1 sa2", -1, C + 1 - 2 * M)
-        scan(T.rm[:], T.rm16[:], T.ms[:], A.max, A.min, "rm16 ms0 ms1 ms2", "rm", 0.08)
-        tt(T.ge[:, 1:48], T.ms[:, 1:48], T.rm[:, 0:47], A.is_ge, "ms0 ms1 ms2 rm", "ge", 0.13)
-        scan(T.nm[:, 0:47], T.ge[:, 0:47], T.de[:, 0:47], A.mult, A.add, "ge gez de", "nm", 0.08)
-        for h in range(3):
-            if h == 2:
-                ts(seg(T.eq, h), T.rowm[:], T.ms[:, 37:38], A.is_equal, None, None, "rowm ms2", "eq2", 0.36)
-            else:
-                ts(seg(T.eq, h), seg(T.sg, h), 0.0, A.is_equal, None, None, "sg%d" % h, "eq%d" % h, 0.2)
-            scan(seg(T.fs, h), T.fl[:, 192 - 96 * h:512 - 96 * h], seg(T.eq, h), A.mult, A.add, "fl eq%d rd%d%d" % (h, t, h), "fs%d" % h, 0.2,
-                 T.rd[:, 16 * t + h:16 * t + h + 1])
-        tt(T.sm[:, 8:11], T.fs[:, C - 1:3 * C:C], T.sm[:, 4:7], A.is_gt, "fs0 fs1 fs2 thr", "con")
-        tt(T.mk[:, 0:3], T.sm[:, 8:11], T.sm[:, 12:15], A.subtract, "con was", "mk")
-        for h in range(3):
-            ts(T.kill[:, h:4 * C:4], T.iob[:], T.nm[:, 16 * h + 14:16 * h + 15], A.is_equal, T.sm[:, 8 + h:9 + h], A.mult, "iob nm con", "k%d" % h, 0.2)
-            n = 96 if h < 2 else 128
-            mul(T.kill[:, 384 * h + 3:384 * h + 4 * n:4], T.id32[:, 0:n], T.mk[:, h:h + 1], "id32 mk", "km%d" % h, 0.14)
-        quant(T.qk[:], T.sk[:], T.kill[:], "k0 k1 k2 km0 km1 km2", "qk", C)
-        for j in range(2):
-            mm(bank("pb", j, 0, 160), T.qo[:], T.so[:], *part(T.qk, T.sk, 160 * j, 160 * j + 160), True, True, "qo qk", "PB%d" % j, 160)
+            mm(bank("pa", b, 0, L), qs_("w", 128 * b, 128 * b + 128), qs_("z"), False)
+            mul(v("xn", b, 4 * L, 4), bank("pa", b, 0, L), 0.015625)
+        key = [v("ms", 16 * h + 5, 16 * h + 6) for h in range(2)]
+        for h in range(2):
+            count_below(v("sm", h, h + 1), seg("sg", h), rows[0], key[h], -1.0)
+        scan(v("rm"), v("rm16"), v("ms"), A.max, A.min)
+        tt(v("ge", 1, 32), v("ms", 1, 32), v("rm", 0, 31), A.is_ge)
+        scan(v("nm", 1, 31), v("ge", 1, 31), v("de", 1, 31), A.mult, A.add)
+        ts(v("eq", L + 2, 2 * L + 2), rows[1], key[1], A.is_equal)
+        ts(v("eq", 1, L + 1), seg("sg", 0), 0.0, A.is_equal)
+        scan(v("fs"), v("fl"), v("eq"), A.mult, A.subtract)
+        tt(v("sm", 2, 4), v("sm", 0, 2), v("fs", L, 2 * L + 2, L + 1), A.is_gt)
+        for h in range(2):
+            con = v("sm", 2 + h, 3 + h)
+            ts(v("kill", 1 + h, 4 * L, 4), v("iob"), v("nm", 16 * h + 14, 16 * h + 15), A.is_equal, con, A.mult)
+            mul(v("kill", 512 * h + 3, 512 * h + 512, 4), v("idm"), con)
+        quant(qs_("k"), v("kill"))
+        if t == 0:
+            for j in range(2):
+                mm(bank("pb", j, 0, 128), qs_("o"), qs_("k", 128 * j, 128 * j + 128))
+        else:
+            mm(bank("pb", 0, 0, L), qs_("o"), qs_("k"))
+        if t < R - 1:
+            mm(bank("pb", 2, 0, L), qs_("o"), qs_("k"))
 
-    def dead_cells(t):
-        for h in range(3):
-            mm(bank("pb", 3 - h, 0, 128), *part(T.qk, T.sk, 96 * h, 96 * h + 128), T.qo[:], T.so[:], True, True, "qo qk", "PB%d" % (3 - h), 128)
-            act(T.rd[:, 16 * t + 16 + h:16 * t + 17 + h], bank("pb", 3 - h, 0, 1), F.Relu, "PB%d rd%d%d" % (3 - h, t, h), "rd%d%d" % (t + 1, h),
-                bias=T.rd[:, 16 * t + h:16 * t + h + 1])
-
-    dma("y", T.seatb[:], T.seat[:], "d_seat", "", "seatb Pload")
     for j in range(4):
-        dma("sy"[j % 2], T.alv[16 * j:16 * j + 16, :], T.alive[:], "d_al%d" % (j % 2), "", "alv%d" % j + " Pload" * (j % 2))
-    dma("y", T.xt[:, 0:4 * C], T.x[:], "d_x", "", "xt Pload", 3.5)
-    dma("y", T.ut[:], T.u[:], "d_u", "", "ut Pload", 2.5)
-    dma("y", T.qw[:].bitcast(dt.uint8), T.wc[:], "d_wc", "", "qw Pload", 3.2)
-    dma("y", T.sw[:], T.ws[:], "d_ws", "", "sw Pload", 2.2)
-    dma("y", T.vt[:], T.v[:], "d_v", "", "vt Pload", 2.5)
+        dma("ys"[j % 2], T.alv[16 * j:16 * j + 16, :], T.alive[:], "d_al%d" % (j % 2), [], [v("alv", p=(16 * j, 16 * j + 16))], 1.9, "ld%d" % (j % 2))
+    dma("y", T.seatb[:], T.seat[:], "d_seat", [], [v("seatb")], 1.9, "ld0")
+    dma("y", T.xt[:, 0:4 * C], T.x[:], "d_x", [], [v("xt", 0, 4 * C)], 3.5, "ld0")
+    dma("y", T.ut[:], T.u[:], "d_u", [], [v("ut")], 2.5, "ld0")
+    dma("y", T.qw[:].bitcast(dt.uint8), T.wc[:], "d_wc", [], [v("qw")], 3.2, "ld0")
+    dma("y", T.sw[:], T.ws[:], "d_ws", [], [v("sw")], 2.2, "ld0")
+    dma("y", T.vt[:], T.v[:], "d_v", [], [v("vt")], 2.5, "ld0")
 
-    iota(T.ik[:], [[16, 28]], 0, 1, "ik", False)
-    iota(T.ik9[:], [[0, 4]], 9, 1, "ik9", False)
-    iota(T.w10[:], [[-1, 16]], 1, 0, "w10")
-    iota(T.iof[:], [[1, C]], 0, 0, "iof")
-    iota(T.idwin[:, 0:W], [[1, W]], C + 1, 0, "idwa")
-    iota(T.idwin[:, W + C:2 * W + C], [[1, W]], C + 1 + W, 0, "idwb")
-    iota(T.j4[:], [[0, 12], [1, 4]], 0, 0, "j4")
-    iota(T.r4[:], [[0, 12], [-31000, 4]], 30000, 0, "r4")
-    iota(T.c16[:], [[0, 20], [1, 16]], 0, 0, "c16")
-    iota(T.k64[:], [[0, 516]], 64, 0, "k64")
-    op("g", g.affine_select, (T.eb[:], T.k64[:], [[1, 516]], A.is_equal, 0.0, -3, -4), "k64", "eb", 1.24)
-    iota(T.cc[:], [[96, 3], [0, 16]], -160, 1, "cc")
-    for j, val in ((4, 10000), (5, -10000), (6, 10000), (15, 0)):
-        iota(T.cc[:, j:48:16], [[0, 3]], val, 0, "cc%d" % j, True, "cc")
-    op("g", g.affine_select, (T.f64[:], T.k64[:, 0:512], [[1, 512]], A.not_equal, -64.0, -192, -1), "k64", "f64", 1.24)
-    mul(T.fl[:], T.f64[:], 0.015625, "f64", "fl", 0.57, "s")
-    for ap, n, val, w in ((T.idwin[:, 400:416], 16, C, "idwc"), (T.dwin[:, 0:W], W, 0, "dwiny"), (T.dwin[:, W + C:416], 56, 0, "dwinz"),
-                          (T.idseq[:, K:K + 16], 16, C, "idseqz"), (T.xt[:, 4 * C:4 * C + 16], 16, 0, "xtz"), (T.xn[:, 4 * C:4 * C + 16], 16, 0, "xnz"),
-                          (T.tp[:, C:4 * TP:TP], 4, 0, "tpz"), (T.tp[:, 401:4 * TP:TP], 4, 0, "tpy"), (T.gb[:, 80:96], 16, 0, "gbz"),
-                          (T.ge[:, 0:1], 1, 0, "gez")):
-        iota(ap, [[0, n]], val, 0, w)
+    iota(v("ik"), [[16, 24]], 0, 1)
+    iota(v("win", 1), [[1, C]], -160)
+    iota(v("r4z"), [[0, 64], [-31000, 4]], L + 2 * W)
+    iota(v("v256"), [[4, 64], [30001, 4]], 0)
+    iota(v("c16"), [[0, 23], [1, 16]], 0)
+    for out, val in ((v("win", 0, 1), D * 512), (v("one"), 1.0), (v("k64"), 64.0), (v("wb", 0, W), -255.375), (v("wb", W + C, 416), -255.375),
+                     (v("tl", 160, 512), 0.0), (v("o_u", 0, 8), 1), (v("o_dead", 4, 8), 0)):
+        fill(out, val)
+    for out, val in ((v("xt", 4 * C), 0), (v("vb", 400, 416), L + 2 * W - 169), (v("tl", 1856), 0), (v("xn", 4 * L), 0), (v("gb"), 0), (v("cc"), 0),
+                     (v("cc", 4, 32, 16), 10000), (v("cc", 6, 32, 16), 10000), (v("cc", 5, 32, 16), -10000), (v("kill", 0, 4 * L, 4), 0),
+                     (v("dead", L), 0), (v("dead", 339, 340), 1), (v("olw", 0, 64), 0), (v("fl", 0, 2 * L + 2, L + 1), 0),
+                     (v("eq", 0, 2 * L + 2, L + 1), L - 2 * M)):
+        iota(out, [[0, len(out[1])]], val)
+    select(v("eb"), v("k64"), A.is_equal, 0.0, -3, -4)
+    for h in range(2):
+        select(v("fl", (L + 1) * h + 1, (L + 1) * (h + 1)), v("one", 0, L), A.not_equal, -1.0, -128 * h, -1)
+    select(v("idm"), v("one", 0, 128), A.is_equal, 0.0, 0, -1)
+    iota(v("ko"), [[0, 128], [-31744, 2], [-31744, 2]], 32768)
+    iota(v("iob"), [[1, L]], 0)
+    iota(v("r16"), [[0, 23], [-31000, 16]], 170)
 
-    bits(0, p, "ik", 0, 112)
-    ts(col("t1"), p, 48.0, A.is_lt, -1.0, A.add, "ik", "t1")
-    ts(col("t2"), p, 48.0, A.is_ge, None, None, "ik", "t2")
-    lin("sv", col("t3"), "t3", ib(0), "ib0", -0.0625, 3)
-    lin("sv", col("ng16"), "ng16", ib(0), "ib0", -1, 0)
-    ts(col("ndr"), p, 80.0, A.is_lt, col("t1"), A.add, "ik t1", "ndr")
-    ts(col("h"), p, 80.0, A.is_lt, col("t2"), A.mult, "ik t2", "h")
-    ts(col("t4"), p, 64.0, A.is_lt, col("t3"), A.add, "ik t3", "t4")
-    lin("sv", T.kt[:], "kt", T.ik[:], "ik", 1, "ng16")
-    for w, a, m_, a_ in (("invl", "h", 1.0 / 41 - 1.0 / 9, 1.0 / 9), ("ndc", "ndr", -3, "t4"), ("v", "h", -1, 1), ("nl", "h", -32, -9),
-                         ("a3s", "h", -16.5, -4), ("a3b", "h", 23.5, -4), ("b3b", "h", -140, 180), ("b1", "ndr", -360, 0),
-                         ("a3", "ndc", "a3s", "a3b"), ("a1", "ndc", "nl", "v"), ("b3", "ndr", -180, "b3b"), ("t1", "ndr", W, 0),
-                         ("t2", "h", W, "b1"), ("ke", "ndc", -36, 44), ("ke1", "ndc", -36, 45),
-                         ("c1", "ndr", 1, "h"), ("c2b", "v", 4.5, 0), ("d1b", "v", 9, 0), ("d2b", "h", 41, 0), ("d3s", "h", -55.5, 36),
-                         ("d3b", "h", -15.5, 35), ("c2", "ndr", -3.5, "c2b"), ("d1", "ndc", "h", "d1b"), ("d2", "a1", "v", "d2b"),
-                         ("d3", "ndc", "d3s", "d3b")):
+    g16, lane, quad, elem = bits(0, p, 0, 112), bits(1, p, 0, 15), bits(2, p, 2, 3), bits(3, p, 0, 3)
+    ts(col("t1"), p, 48.0, A.is_ge, -1.0, A.add)
+    ts(col("t2"), p, 48.0, A.is_ge)
+    lin(col("t3"), g16, 0.0625, -4)
+    lin(col("ng16"), g16, -1, 0)
+    ts(col("dr"), p, 80.0, A.is_ge, col("t1"), A.add)
+    ts(col("h"), p, 80.0, A.is_lt, col("t2"), A.mult)
+    ts(col("t4"), p, 64.0, A.is_ge, col("t3"), A.add)
+    lin(v("kt"), v("ik"), 1, "ng16")
+    lin(v("kt1"), v("kt", 0, 20), 1, 1)
+    for w, a, m_, a_ in (("invl", "h", 1.0 / W - 1.0 / 9, 1.0 / 9), ("dc", "dr", -3, "t4"), ("v", "h", -1, 1), ("len", "h", 31, 9),
+                         ("a3s", "h", 11.5, 8), ("h19", "h", 19.5, 0), ("b1s", "h", W, 0), ("b3s", "h", -140, 180),
+                         ("ndc", "dc", -1, 0), ("a1", "dc", "len", "v"), ("a3", "dc", "a3s", "h19"), ("b1", "dr", 360, "b1s"), ("b2", "dr", -W, 0),
+                         ("b3", "dr", 140, "b3s"), ("thr", "dc", 19.5, 20), ("wrap", "dc", -W, 0), ("edge", "dc", 19.5, 19.5), ("hop", "dr", W, "dc")):
         clin(w, a, m_, a_)
-    lin("sv", tb(0), "tb0", T.kt[:, 0:27], "kt", "invl", -0.488)
-    ts(tb(1), tb(0), RND, A.add, -RND, A.add, "tb0", "tb1")
-    lin("sv", tb(4), "tb4", T.kt[:, 0:27], "kt", "ndc", "a3")
-    lin("sv", tb(3), "tb3", tb(1), "tb1", "a1", 0)
-    lin("sv", tb(2), "tb2", tb(1), "tb1", "t2", 0)
-    lin("sv", tb(5), "tb5", T.kt[:, 0:27], "kt", "t1", "b3")
-    tt(tb(6), tb(3), tb(4), A.add, "tb3 tb4", "tb6", 0.09)
-    tt(tb(7), tb(2), tb(5), A.add, "tb2 tb5", "tb7", 0.09)
-    lin("s", tb(8), "tb8", tb(6), "tb6", 1, -19.5, small, F.Abs)
-    tt(tb(11), tb(7), tb(6), A.add, "tb7 tb6", "tb11", 0.09)
-    ts(tb(10), tb(8), 20.0, A.is_gt, 400.0, A.mult, "tb8", "tb10")
-    ts(tb(9), tb(11), 400.0, A.min, None, None, "tb11", "tb9")
-    tt(T.o_sig[:, 0:27], tb(10), tb(9), A.max, "tb10 tb9", "o_sig", 0.09)
-    for a in range(2):
-        cp(T.o_alive[64 * a:64 * a + 64, :], T.alv[0:64, :], "alv0 alv1 alv2 alv3", "o_al%d" % a, q="v")
-    cp(T.o_seat[:], T.seatb[:], "seatb", "o_seat", q="v")
-    cp(T.dead[:], T.w10[:].indirect(T.o_alive[:]), "w10 " + al, "dead0 dead1", 0.58)
-    cp(T.idwin[:, W:W + C], T.iof[:].indirect(T.o_seat[:]), "iof o_seat", "idwd", 0.58)
-    for j, a, b in ((0, 0, 14), (1, 14, 27)):
-        cp(T.idseq[:, 16 * a:16 * b], T.idwin[:].indirect(T.o_sig[:, a:b]), "idwa idwb idwc idwd o_sig", "idseq%d" % j, 0.42)
-    ids = "idseq0 idseq1 idseqz"
-    rays(0)
-    tt(T.delta[:, 0:223], T.idseq[:, 0:223], T.idseq[:, 1:224], A.subtract, "idseq0", "delta0", 0.5)
-    tt(T.delta[:, 223:K], T.idseq[:, 223:K], T.idseq[:, 224:K + 1], A.subtract, ids, "delta", 0.47)
-    bits(1, p, "ik", 2, 3)
-    bits(2, p, "ik", 0, 3)
-    bits(3, p, "ik", 0, 15)
-    ts(tb(12, 3), T.kt[:, 0:3], W - 1.0, A.min, 9.0, A.mult, "kt", "tb12")
-    ts(T.o_end1[:, 0:3], tb(12, 3), col("ke1"), A.add, None, None, "tb12 ke1", "o_end1")
-    ts(T.o_end[:, 0:3], tb(12, 3), col("ke"), A.add, None, None, "tb12 ke", "o_end")
-    lin("sv", col("q6"), "q6", ib(1), "ib1", -FAR, 0)
-    lin("sv", col("tq"), "tq", ib(2), "ib2", 0.25, 0)
-    lin("sv", col("tmax"), "tmax", ib(2), "ib2", 1, 4 * C)
-    lin("sv", col("ni6"), "ni6", ib(3), "ib3", -FAR, 0)
-    lin("s", T.ev[:], "ev", T.j4[:], "j4", FAR, "q6", 0.08, F.Abs)
-    lin("sv", T.lend[:], "lend", T.ev[:], "ev", 1, "tq", 0.08)
-    lin("s", T.cm[:, 160:336], "cmy", T.iof[:, 0:176], "iof", 0, 0, 0.21)
-    lin("s", T.cm[:, 336:512], "cmz", T.iof[:, 0:176], "iof", 0, 0, 0.21)
-    lin("s", T.iob[:], "iob", T.iof[:], "iof", 1, -160, 0.36)
-    lin("s", T.l16[:], "l16", T.c16[:], "c16", FAR, "ni6", 0.36, F.Abs)
-    lin("s", T.r16[:], "r16", T.c16[:], "c16", -31000, 30000, 0.36)
-    tt(T.aend[:], T.idseq[:].indirect(T.o_end1[:, 0:3]), T.lend[:], A.add, ids + " o_end1 lend", "aend", 0.13)
-    send(0, "xt")
+    kk = v("kt", 0, 23)
+    x = tmp(23)
+    lin(x, kk, "invl", -0.4875)
+    line = rounded(x)
+    u = lin2(23, line, "a1", kk, "ndc", "a3")
+    row = lin2(23, line, "b1", kk, "b2", "b3")
+    f, w, place, sq, off, nxt = [tmp(23) for j in range(6)]
+    ts(f, u, col("dc"), A.mult, col("thr"), A.is_gt)
+    lin(w, f, "wrap", 0)
+    tt(place, u, w, A.add)
+    tt(sq, row, place, A.add)
+    ts(off, place, col("edge"), A.is_equal, 400.0, A.mult)
+    ts(nxt, sq, col("hop"), A.add, 400.0, A.min)
+    tt(v("o_p", 0, 23), nxt, off, A.max)
+    ts(v("o_o", 0, 23), sq, 400.0, A.min)
 
-    tt(T.invm[:], T.l16[:].indirect(T.o_seat[:]), T.iob[:], A.add, "iob l16 o_seat", "invm", 0.57)
-    op("v", V.tensor_copy, (T.inv[:].indirect(T.o_seat[:]), T.invm[:]), "invm o_seat", "inv", 1.32)
-    scan(T.invs[:], T.r16[:], T.inv[:], A.max, A.min, "r16 inv", "invs", 0.2)
-    lin("v", tc(6), "tc6", T.o_alive[:], al, -1000, 1000)
-    lin("sv", tc(0), "tc0", T.invs[:, 15:C:16], "invs", 0.025, 140.5 / W)
-    ts(tc(1), tc(0), RND, A.add, -RND, A.add, "tc0", "tc1")
-    lin("sv", tc(2), "tc2", tc(1), "tc1", -W, 160)
-    lin("sv", tc(3), "tc3", tc(1), "tc1", "c1", "c2")
-    tt(tc(4), tc(2), T.invs[:, 15:C:16], A.add, "tc2 invs", "tc4")
-    lin("sv", tc(5), "tc5", tc(3), "tc3", "d2", "d3")
-    tt(T.ctab0[:], tc(6), T.kt[:, 0:20], A.add, "tc6 kt", "ctab0")
-    lin("sv", tc(7), "tc7", tc(4), "tc4", "d1", 0)
-    tt(T.o_pos[:], tc(7), tc(5), A.add, "tc7 tc5", "o_pos")
+    for a in range(2):
+        tt(v("o_al", p=(64 * a, 64 * a + 64)), v("alv", p=(0, 64)), v("kt1", p=(0, 64)), A.mult)
+    cp(v("o_seat"), v("seatb"), "v")
+    gather2(lambda o, a, q: lin(o, a, 1.0 / 512, 160.0 / 512 - 256, q), "w0", 0, v("win"), "o_al", 20, True)
+    gather2(cp, "wb", W, v("w0"), "o_seat", 20, True)
+    gather2(cp, "wr", 0, v("wb"), "o_p", 23, True)
+    scan(v("st"), v("one", 0, K), v("wr", 0, K), A.add, A.min)
+    lin(col("m1"), quad, -31000, L + 2 * W + 256)
+    lin(col("m2"), elem, 1, 0)
+    lin(col("m3"), col("h"), 4 * D, "m1")
+    lin(v("lend", 0, W), v("r4z", 0, W), -1, "m3", "s", F.Abs)
+    for lo, n, val in ((0, W, 12.625), (W, W, L), (2 * W, 64, 20000)):
+        lin(v("r4", lo, lo + n), v("r4z", 0, n), 1, val - L - 2 * W)
+    tt(v("ev"), v("st", 8, K, 9), v("lend", 0, W), A.add)
+    scan(v("es"), v("r4", 0, W), v("ev"), A.max, A.min)
+    ts(v("oi", 0, 10), v("es", 3, W, 4), 2048.0, A.mult, col("m2"), A.add)
+    ts(v("oi", 16, 26), v("oi", 0, 10), 2047, A.bitwise_and)
+    cp(v("o_cmp"), v("oi", 16, 26), "v")
+    send(0, v("xt"))
+
+    lin(v("al"), v("w0"), -2.0 / D, 1, "s", F.Relu)
+    scan(v("pre"), v("al"), v("one", 0, C), A.add, A.mult, -170.0)
+    lin(v("bt", 0, 16), v("kt", 0, 16), -1, 169.5)
+    for k in range(16):
+        count_below(v("sums", k, k + 1), v("junk", 80 * k, 80 * k + 80), v("pre", 16 * k, 16 * k + 80), v("bt", k, k + 1))
+    lin(col("n1"), lane, -1, 40)
+    x = tmp(16)
+    lin(x, v("sums", 0, 16), -0.5, "n1")
+    tt(v("o_live"), x, v("kt", 0, 16), A.add)
+    quant(qs_("a"), v("xt", 0, 4 * C))
+    pick(qs_("x0", 128, 384), qs_("a"), v("o_live"))
+    tt(v("vb", W, W + C), ind(v("pre"), v("o_seat")), v("wb", W, W + C), A.max)
+    for j in range(2):
+        clin("hd%d" % j, "dc", -1, L - 9 + W * j)
+        lin(v("vb", (W + C) * j, (W + C) * j + W), v("win", 1, W + 1), 1, "hd%d" % j)
+    cp(v("own"), ind(v("vb"), v("o_o", 0, 23)), "sv")
+    tt(v("delta"), ind(v("vb"), v("o_p", 0, 23)), v("own"), A.subtract)
+    lin(v("dseq"), v("wr"), 1.0 / D, -1.0 / 2048, "s", F.Relu)
+    op({"v": (V.tensor_copy, (ap(ind(v("inv"), v("o_seat"))), ap(v("win", 1))), {})}, ind(v("inv"), v("o_seat")), [v("win", 1)])
+    lin(col("nl"), lane, -FAR, 0)
+    lin(v("l16"), v("c16"), FAR, "nl", "s", F.Abs)
+    tt(v("pz"), ind(v("inv"), v("o_live")), v("l16", 0, L), A.add)
+    scan(v("pzs"), v("r16", 0, L), v("pz"), A.max, A.min)
+    for w, a, m_, a_ in (("e1", "h", "ndc", "v"), ("drc", "dc", "dr", 0), ("e3a", "dr", 3.5, -4.5), ("m9", "h", -8, 9), ("f1", "dr", -1, "b1s"),
+                         ("f2a", "v", 3.5, 0), ("e2a", "e1", -W, 0), ("e3b", "h", 24, "e3a"), ("f2", "dr", 3.5, "f2a"), ("nthr", "dc", -19.5, 20),
+                         ("e2", "drc", -1, "e2a"), ("e3c", "dc", "e3b", "h19"), ("e3", "e1", 160, "e3c"), ("wrap9", "wrap", "m9", 0)):
+        clin(w, a, m_, a_)
+    ss = v("pzs", 15, L, 16)
+    x, f, w = tmp(16), tmp(16), tmp(16)
+    lin(x, ss, 1.0 / W, 4 - 0.4875)
+    rho = rounded(x)
+    u = lin2(16, rho, "e2", ss, "e1", "e3")
+    ts(f, u, col("ndc"), A.mult, col("nthr"), A.is_gt)
+    lin(w, f, "wrap9", 0)
+    tt(v("o_pos"), lin2(16, u, "m9", rho, "f1", "f2"), w, A.subtract)
+    lin(col("k1"), quad, -30000, 0)
+    lin(col("k2"), elem, 0.25, "k1")
+    lin(v("l4c"), v("v256"), 1, "k2", "s", F.Abs)
     for b in range(4):
-        quant(*part(T.qe, T.se, 128 * b, 128 * b + 128), T.eb[:, 3 - b:515 - b], "eb", "qe%d" % b)
-    lin("s", T.k1024[:], "k1024", T.k64[:, 0:512], "k64", 16, 0, 0.57)
-    lin("s", T.id32[:], "id32", T.f64[:, 192:320], "f64", 0.25, -16, 0.16)
-    quant(T.qo[:], T.so[:], T.k1024[:], "k1024", "qo")
-    quant(T.qu[:], T.su[:], T.ut[:], "ut", "qu")
-    quant(T.qv[:], T.sv[:], T.vt[:], "vt", "qv")
-    bits(4, p, "ik", 0, 7)
-    fill(T.o_u[:, 0:8], 1, "o_u0")
-    lin("v", T.o_u[:, 8:9], "o_u1", ib(4), "ib4", 16, 0)
-    cp(T.qu2[:].bitcast(dt.uint32), T.qu[:].bitcast(dt.uint32).indirect(T.o_u[:, 0:9]), "qu o_u0 o_u1", "qu2", 0.29, "v")
-    cp(T.su2[:], T.su[:].indirect(T.o_u[:, 0:9]), "qu o_u0 o_u1", "su2", 0.3, "s")
-    bits(5, T.ik9[:, 0:1], "ik9", 0, 7)
-    bits(6, T.ik9[:, 0:1], "ik9", 0, 1)
-    bits(7, T.ik9[:, 0:1], "ik9", 0, 8)
-    bits(8, p, "ik", 4, 6)
-    ts(col("y4"), ib(3), 6.0, A.mult, 12.0, A.min, "ib3", "y4")
-    lin("sv", col("y0"), "y0", ib(8), "ib8", 1, 0)
-    lin("sv", col("y1"), "y1", ib(5), "ib5", 10, "y0")
-    lin("sv", col("y2"), "y2", ib(6), "ib6", -9, "y1")
-    lin("sv", col("y3"), "y3", ib(7), "ib7", 16, "y2")
-    lin("sv", tb(13, 3), "tb13", T.j4[:, 0:3], "j4", 6, "y3")
-    ts(T.o_g[:, 0:3], tb(13, 3), 80.0, A.min, None, None, "tb13", "o_g")
-    lin("v", T.o_dc[:, 0:1], "o_dc", ib(0), "ib0", 0.0625, "y4")
-    cp(T.rd[:, 0:16], T.tc[:, 120:140].indirect(T.o_dc[:, 0:1]), "tc6 o_dc", "rd00 rd01 rd02", 0.09)
-    fill(T.rd[96:128, 0:2], 1000.0, "rd00 rd01")
-    lin("s", T.rm16[:], "rm16", T.cc[:], "cc cc4 cc5 cc6 cc15", 1.0e25, -5.0e28, 0.08)
+        quant(E[b], v("eb", 3 - b, 515 - b))
+    quant(qs_("u"), v("ut"))
+    lin(v("o_u", 8, 9), bits(4, p, 0, 7), 16, 0, "v")
+    pick(qs_("u2"), qs_("u"), v("o_u", 0, 9))
+    quant(qs_("o"), v("ko"))
+    quant(qs_("v"), v("vt"))
+    lin(v("rm16"), v("cc"), 1.0e25, -5.0e28)
+    for j, (base, by) in enumerate(((0, 4), (0, 2), (9, 64), (9, 32), (9, 128), (9, 16))):
+        iota(v("pm", j, j + 1), [[0, 1]], base * by, by)
+    ts(v("ib", 8, 14), v("pm", 0, 6), 128, A.bitwise_and)
+    bit = [v("ib", 8 + j, 9 + j) for j in range(6)]
+    lin(col("d0"), bit[0], -1, 0)
+    lin(col("d1"), bit[1], -0.5, 0)
+    lin(col("s0"), bit[2], 1, "d0", "s", F.Abs)
+    lin(col("s1"), bit[3], 0.5, "d1", "s", F.Abs)
+    lin(col("y0"), bit[4], 1.0 / 32, "s0")
+    lin(col("y1"), bit[0], 1.0 / 16, "s1")
+    lin(col("y2"), bit[5], 8, "y0")
+    lin(col("y4"), bit[1], 1.0 / 8, "y1")
+    ts(col("y3"), col("y4"), col("y2"), A.add, 3.0, A.add)
+    x = tmp(2)
+    lin(x, v("c16", 0, 2), 32, "y3")
+    ts(v("o_g"), x, 256.0, A.min)
+    tt(v("am"), ind(v("vb"), v("o_p", 0, 23)), v("l16"), A.add)
+    scan(v("ams"), v("r16"), v("am"), A.max, A.min)
+    ts(v("o_ray", 0, 23), v("ams", 15, KP, 16), 169.0, A.add)
+    clin("k3", "dr", -W / 2, "k2")
+    clin("k4", "dc", -1, "k3")
+    ts(col("k6"), col("k4"), L + W / 2, A.add, col("v"), A.mult)
+    clin("v4", "v", 4, 0)
+    clin("hz", "h", 4 * L, 0)
+    lin(v("lend", W, 2 * W), v("v256", 0, W), "v", "k6", "s", F.Abs)
+    tt(v("delta", 8, K, 9), v("delta", 8, K, 9), v("lend", W, 2 * W), A.add)
+    scan(v("dpre"), v("one", 0, C), v("al"), A.add, A.subtract)
+    lin(v("bt", 16, 20), v("kt", 0, 4), -1, -0.5)
+    for k in range(4):
+        count_below(v("sums", 16 + k, 17 + k), v("junk2", 272 * k, 272 * k + 272), v("dpre", 16 * k, 16 * k + 272), v("bt", 16 + k, 17 + k))
+    x = tmp(4)
+    clin("n2", "n1", 1, 96)
+    lin(x, v("sums", 16, 20), -0.5, "n2")
+    tt(v("o_dead", 0, 4), x, v("kt", 0, 4), A.add)
+    pick(qs_("d"), qs_("a"), v("o_dead"))
+    lin(v("rl16"), v("l16", 0, C), -1, 1000)
+    scan(v("ps"), v("rl16"), v("pre"), A.max, A.min)
+    a1, a2, a3, a4 = [tmp(20) for j in range(4)]
+    lin(a3, v("ps", 15, C, 16), 1, 170 + 63)
+    ts(a2, v("o_al"), 1.0, A.min)
+    lin(a1, v("kt", 0, 20), 1, 63)
+    tt(a4, a2, a3, A.mult)
+    x = tmp(20)
+    tt(x, a1, a3, A.subtract)
+    tt(v("o_slot"), x, a4, A.max)
 
     for t in range(R):
-        xb = "xn" if t else "xt"
+        if t == 1:
+            ts(v("dead", 0, 128), bank("pb", 0, 0, 128), 0.0, A.max)
+            lin(v("dead", 128, L), bank("pb", 1, 0, 128), 1, 0, "s", F.Relu)
+        if t == 2:
+            tt(v("dead", 0, L), bank("pb", 0, 0, L), v("dead", 0, L), A.max)
         if t:
-            ts(T.dead[:, 0:160], bank("pb", 0, 0, 160), 0.5, A.is_gt, None, None, "PB0", "dead0", 0.2)
-            act(T.dead[:, 160:C], bank("pb", 1, 0, 160), F.Relu, "PB1", "dead1", 0.2)
-            rays(t)
-            send(t, xb)
-            for j in range(2):
-                tt(T.adyn[:, 160 * j:160 * j + 160], bank("pb", j, 0, 160), T.l16[:, 0:160], A.max, "PB%d l16" % j, "adyn%d" % j, 0.2)
-            dead_cells(t - 1)
-        mul(T.ds[:], T.dead[:], -1.0e24, "dead0 dead1", "ds", 0.36, "s")
-        act(T.sm[:, 12:15], T.rd[:, 16 * t:16 * t + 3], F.Sign, "rd%d0 rd%d1 rd%d2" % (t, t, t), "was")
-        unpack(t, xb)
-        zlist(t)
-        elist()
+            gather2(flag, "dseq", 0, v("dead"), "o_ray", 23)
+        scan(v("st"), v("dseq", 0, K), v("delta", 0, K), A.mult, A.add)
+        if t:
+            scan(v("es"), v("r4", W, 2 * W), v("st", 8, K, 9), A.max, A.min)
+            ts(v("o_cmp"), v("es", 3, W, 4), col("v4"), A.mult, col("hz"), A.add)
+            send(t, v("xn"))
+            tt(v("adyn"), bank("pb", 2, 0, L), v("adyn") if t > 1 else v("l4c"), A.max)
+            mul(v("ds"), v("dead", 0, L), -1.0e21)
+            quant(qs_("x%d" % t, 128, 384), v("xn", 0, 4 * L))
+        unpack(t)
+        lists(t)
+        if t == 1:
+            unpack_dead("d", 0)
+        if t == 2:
+            unpack_dead("x2", 64)
+            quant(qs_("d2"), v("tl", 0, 512))
+            unpack_dead("d2", 64)
         gather_z(t)
         contest(t)
 
-    quant(T.qx3[:], T.sx3[:], T.xn[:, 0:4 * C], xs, "qx3", C)
+    quant(qs_("x3", 0, 128), v("tl", 0, 512))
+    quant(qs_("x3", 128, 384), v("xn", 0, 4 * L))
+    tt(v("olw", 64, C), bank("pb", 0, 0, L), v("ds"), A.is_le)
+    gather2(cp, "olb", 0, v("olw"), "o_slot", 20)
+    dma("y", T.ol[:], T.olb[0:1, :], "d_out", [v("olb")], [])
     for j in range(2):
-        mm(bank("pa", j, 0, 160), T.qv[:], T.sv[:], *part(T.qx3, T.sx3, 160 * j, 160 * j + 160), True, True, "qv qx3", "PA%d" % j, 160)
-        cp(T.ysb[:, 160 * j:160 * j + 160], bank("pa", j, 0, 160), "PA%d" % j, "ysb%d" % j, 0.2, "sv")
-        ts(T.olb[0:32, 160 * j:160 * j + 160], T.pb[0:32, 512 * j:512 * j + 160], 0.5, A.is_lt, None, None, "PB%d" % j, "ol%d" % j, 0.2)
-    dma("y", T.oc[:], T.qx3[:].bitcast(dt.uint8), "d_out", "qx3", "", 2.9)
-    for j in range(2):
-        dma("sy"[j], T.y[:, 160 * j:160 * j + 160], T.ysb[:, 160 * j:160 * j + 160], "d_out", "ysb%d" % j, "", 2.6)
+        lo, hi = 160 * j, 160 * j + 160
+        pick(qs_("f", lo, hi), qs_("x3", 64, 384), v("o_slot", 10 * j, 10 * j + 10))
+        mm(bank("pa", j, 0, 160), qs_("v"), qs_("f", lo, hi))
+        cp(v("ysb", lo, hi), bank("pa", j, 0, 160), "sv")
+        dma("sy"[j], T.y[:, lo:hi], T.ysb[:, lo:hi], "d_out", [v("ysb", lo, hi)], [], 2.6)
+        dma("y", T.oc[:, 4 * lo:4 * hi], T.qf[:, lo:hi].bitcast(dt.uint8), "d_out", [v("qf", lo, hi)], [], 2.6)
     for k in range(4):
-        dma("y", T.osc[4 * k:4 * k + 4, :], T.sx3[32 * k:32 * k + 4, :], "d_out", "qx3", "")
-    dma("y", T.ol[:], T.olb[0:1, :], "d_out", "ol0 ol1", "")
+        dma("y", T.osc[4 * k:4 * k + 4, :], T.sf[32 * k:32 * k + 4, :], "d_out", [v("sf")], [])
 
     n, wake = len(steps), OPT["wake"]
-    after = [[] for _ in steps]
+    behind = [0] * n
     for i, s in enumerate(steps):
-        for j in s["firm"] | s["loose"]:
-            after[j].append(i)
-    tail, seed = [0.0] * n, OPT["seed"]
-    for i in range(n - 1, -1, -1):
-        tail[i] = steps[i]["done"] + max([tail[j] + wake for j in after[i]] + [0.0])
-
-    firm, loose = [list(s["firm"]) for s in steps], [list(s["loose"]) for s in steps]
-    busy, done, ways = [s["busy"] for s in steps], [s["done"] for s in steps], [list(s["ways"]) for s in steps]
+        far = 0
+        for j in s["firm"]:
+            far |= behind[j]
+        s["firm"], s["loose"] = [sorted(j for j in s[k] if not far >> j & 1) for k in ("firm", "loose")]
+        behind[i] = far | sum(1 << j for j in s["firm"])
+    firm, loose = [s["firm"] for s in steps], [s["loose"] for s in steps]
+    busy, ways = [s["busy"] for s in steps], [list(s["ways"]) for s in steps]
+    late = [s["done"] - min(s["busy"].values()) if s["done"] else 0.0 for s in steps]
+    least = [min(b.values()) for b in busy]
     kind = [(s["sem"] or "c")[0:4] for s in steps]
+    after = [[] for _ in steps]
+    for i in range(n):
+        for j in firm[i] + loose[i]:
+            after[j].append(i)
+    tail, seed = [0.0] * n, [OPT["seed"]]
+    for i in range(n - 1, -1, -1):
+        tail[i] = least[i] + late[i] + max([tail[j] + wake for j in after[i]] + [0.0])
 
     def lay(tail):
         left = [len(firm[i]) + len(loose[i]) for i in range(n)]
@@ -449,21 +545,21 @@ def rank_program(g, core, T, topo):
                 best = None
                 for t0, q in ready[i]:
                     t0 = max(t0, free[q])
-                    if best is None or t0 < best[0] - 0.02:
-                        best = (t0, q)
+                    if best is None or t0 + busy[i][q] < best[2] - 0.02:
+                        best = (t0, q, t0 + busy[i][q])
                 at[i] = best
                 if x is None or (best[0], -tail[i]) < (at[x][0], -tail[x]):
                     x = i
-            (tx, qx), z = at[x], None
-            bx = tx + busy[x]
+            tx, qx, bx = at[x]
+            z = None
             for y in ready:
-                ty, qy = at[y]
+                ty, qy, by = at[y]
                 if qy == qx and tail[y] > tail[x] and ty < bx and (z is None or tail[y] > tail[z]) \
-                        and bx + tail[y] > max(ty + tail[y], ty + busy[y] + tail[x]) + OPT["eps"]:
+                        and bx + tail[y] > max(ty + tail[y], by + tail[x]) + OPT["eps"]:
                     z = y
             x = x if z is None else z
-            t0, q = at[x]
-            queue[x], free[q], end[x] = q, t0 + busy[x], t0 + done[x]
+            t0, q, t1 = at[x]
+            queue[x], free[q], end[x] = q, t1, t1 + late[x]
             plan.append(x)
             del ready[x]
             for j in after[x]:
@@ -473,33 +569,75 @@ def rank_program(g, core, T, topo):
                     ready[j] = [(max([t1] + [end[k] + wake for k in loose[j] if queue[k] != q1]), q1) for q1 in ways[j]]
         return max(end), plan, queue
 
-    def replay(plan, queue, wk, hop, first, slow):
-        free, end = {q: 0.0 for q in qs}, [0.0] * n
+    def guess(slow, fix, wk, pe, hop, dma_):
+        b = [{q: x * (pe if q == "t" else slow) + (fix if q in "vs" else 0.0) if kind[i] == "c" else x for q, x in busy[i].items()} for i in range(n)]
+        return b, [late[i] + wk + (0.0 if kind[i] == "c" else hop if kind[i][0] == "a" else dma_) for i in range(n)]
+
+    def replay(plan, queue, b, more):
+        free, last, end, start, why = {q: 0.0 for q in qs}, {}, [0.0] * n, [0.0] * n, [None] * n
         for i in plan:
-            q, t0 = queue[i], free[queue[i]]
+            q = queue[i]
+            t0, w = free[q], last.get(q)
             for j in firm[i]:
-                t0 = max(t0, end[j] + wk)
+                if end[j] > t0:
+                    t0, w = end[j], j
             for j in loose[i]:
-                if queue[j] != q:
-                    t0 = max(t0, end[j] + wk)
-            k, more = (slow, 0.0) if kind[i] == "c" else (1.0, hop + (first if kind[i] == "arr0" else 0.0) if kind[i][0] == "a" else 0.0)
-            free[q], end[i] = t0 + k * busy[i], t0 + k * done[i] + more
-        return max(end)
+                if end[j] > t0 and queue[j] != q:
+                    t0, w = end[j], j
+            start[i], why[i], last[q] = t0, w, i
+            free[q] = t0 = t0 + b[i][q]
+            end[i] = t0 + more[i]
+        return end, start, why
+
+    def draw(k):
+        seed[0] = (seed[0] * 1103515245 + 12345) % 2147483648
+        return (seed[0] >> 8) % k
 
     if "best" not in OPT:
-        best, push = None, [0.0] * n
+        guesses = [guess(*x) for x in OPT["guesses"]]
+        plan, queue = lay(tail)[1:]
+        now = [replay(plan, queue, *x) for x in guesses]
+        total = sum(max(x[0]) for x in now)
+        best = (total, plan, queue)
         for turn in range(OPT["turns"]):
-            other = list(push)
-            for k in range(OPT["muts"] if turn else 0):
-                seed = (seed * 1103515245 + 12345) % 2147483648
-                i = (seed >> 8) % n
-                seed = (seed * 1103515245 + 12345) % 2147483648
-                other[i] += OPT["jit"] * (seed / 1073741824 - 1)
-            got = lay([tail[i] + other[i] for i in range(n)])
-            cost = got[0] + replay(got[1], got[2], 1.6 * wake, 0.7, 0.5, 0.85) + replay(got[1], got[2], wake, -0.3, -1.2, 1.25)
-            if best is None or cost <= best[0]:
-                best, push = (cost, got[1], got[2], got[0]), other
-        OPT["best"] = best
+            end, start, why = now[draw(len(now))]
+            i, pairs = end.index(max(end)), []
+            while why[i] is not None:
+                if queue[why[i]] == queue[i] and why[i] not in firm[i] and why[i] not in loose[i]:
+                    pairs.append((i, why[i]))
+                i = why[i]
+            if not pairs:
+                break
+            x, y = pairs[draw(len(pairs))]
+            how, plan2, queue2 = draw(5), list(plan), queue
+            if how < 2:
+                plan2.remove(y)
+                lo, hi = plan2.index(x) + 1, min([plan2.index(j) for j in after[y]] + [n - 1])
+                if lo > hi:
+                    continue
+                plan2.insert(lo if how else lo + draw(min(hi - lo, 40) + 1), y)
+            elif how < 4:
+                z = x if how == 2 else y
+                hi = plan2.index(y) - (z == y)
+                plan2.remove(z)
+                lo = max([plan2.index(j) + 1 for j in firm[z] + loose[z]] + [0])
+                if lo > hi:
+                    continue
+                plan2.insert(hi - draw(min(hi - lo, 3 if how == 2 else 60) + 1), z)
+            else:
+                z = (x, y)[draw(2)]
+                if len(ways[z]) < 2:
+                    continue
+                queue2 = list(queue)
+                queue2[z] = [q for q in ways[z] if q != queue[z]][0]
+            got = [replay(plan2, queue2, *x) for x in guesses]
+            sum2 = sum(max(x[0]) for x in got)
+            if sum2 <= total + OPT["slack"] * (1 - turn / OPT["turns"]) * draw(100) / 100:
+                plan, queue, now, total = sorted(plan2, key=lambda i: got[0][1][i]), queue2, got, sum2
+                if total < best[0]:
+                    best = (total, plan, queue)
+        OPT["best"] = best + ([max(replay(best[1], best[2], *x)[0]) for x in guesses],)
+        OPT["all"] = (firm, loose, busy, late, kind, steps)
     plan, queue = OPT["best"][1], OPT["best"][2]
 
     count, token, waited = {}, [None] * n, {q: {} for q in qs}
@@ -512,7 +650,7 @@ def rank_program(g, core, T, topo):
     for i in plan:
         s, q = steps[i], queue[i]
         need = {}
-        for j in list(s["firm"]) + [j for j in s["loose"] if queue[j] != q]:
+        for j in firm[i] + [j for j in loose[i] if queue[j] != q]:
             need[token[j][0]] = max(need.get(token[j][0], 0), token[j][1])
         for sem in sorted(need):
             wait(q, sem, need[sem])

from concourse.bass import DstId, RemoteDMATransfer
from concourse.mybir import dt, AluOpType as A, ActivationFunctionType as F

W, C, L, M, R = 40, 320, 256, 24, 3
K, KP = 360, 368
X4, U8, BF, F32, I32, U16 = "float8_e4m3fn_x4", "uint8", "bfloat16", "float32", "int32", "uint16"
SIZE = {X4: 4, U8: 1, BF: 2, F32: 4, I32: 4, U16: 2}


def _sb(n, d):
    return ("sbuf", [128, n], d)


SCRATCH = {
    "seatb": _sb(20, I32), "alv": _sb(20, I32), "ik": _sb(24, I32), "ib": _sb(16, I32), "oi": _sb(32, I32),
    "o_seat": _sb(20, U16), "o_al": _sb(20, U16), "o_p": _sb(24, U16), "o_o": _sb(24, U16), "o_live": _sb(16, U16),
    "o_dead": _sb(8, U16), "o_slot": _sb(20, U16), "o_pos": _sb(16, U16), "o_ray": _sb(24, U16), "o_z": _sb(64, U16), "o_cmp": _sb(10, U16),
    "o_u": _sb(10, U16), "o_g": _sb(2, U16),
    "cf": _sb(64, F32), "kt": _sb(24, F32), "kt1": _sb(20, F32), "tb": _sb(24 * 40, F32), "sums": _sb(20, F32), "bt": _sb(20, F32),
    "pm": _sb(8, I32), "win": _sb(C + 1, F32), "one": _sb(384, BF), "c16": _sb(KP, F32), "l16": _sb(KP, BF), "r16": _sb(KP, BF), "rl16": _sb(C, BF),
    "v256": _sb(L, F32), "l4c": _sb(L, F32), "r4z": _sb(L, F32), "r4": _sb(144, F32), "lend": _sb(80, F32), "iob": _sb(L, BF),
    "w0": _sb(C, F32), "wb": _sb(416, F32), "vb": _sb(416, F32), "wr": _sb(KP, F32), "own": _sb(KP, F32), "delta": _sb(KP, F32),
    "am": _sb(KP, BF), "ams": _sb(KP, BF), "al": _sb(C, BF), "pre": _sb(C, BF), "dpre": _sb(C, BF), "ps": _sb(C, BF),
    "junk": _sb(1280, BF), "junk2": _sb(1088, BF), "inv": _sb(C, BF), "pz": _sb(L, BF), "pzs": _sb(L, BF),
    "dead": _sb(352, BF), "dseq": _sb(KP, BF), "st": _sb(K, F32), "ev": _sb(W, F32), "es": _sb(W, F32),
    "adyn": _sb(L, F32), "zv": _sb(L, F32), "zs": _sb(L, F32), "tr": _sb(L, F32), "gb": _sb(272, F32),
    "cc": _sb(32, F32), "rm16": _sb(32, F32), "e": _sb(32, F32), "nb": _sb(32, F32), "de": _sb(32, F32), "ms": _sb(32, F32), "rm": _sb(32, F32),
    "ge": _sb(32, F32), "nm": _sb(32, F32), "sm": _sb(8, F32),
    "rowm": _sb(L, F32), "sg": _sb(2 * L, BF), "eq": _sb(2 * L + 2, BF), "fs": _sb(2 * L + 2, BF), "ds": _sb(L, BF),
    "k64": _sb(516, BF), "eb": _sb(516, BF), "fl": _sb(2 * L + 2, BF), "idm": _sb(128, BF), "ko": _sb(512, BF),
    "xt": _sb(1296, BF), "xn": _sb(1040, BF), "ut": _sb(512, BF), "vt": _sb(512, BF), "tl": _sb(1872, BF),
    "z": _sb(4 * L, BF), "kill": _sb(4 * L, BF), "ysb": _sb(C, F32), "olw": _sb(C, BF), "olb": _sb(C, F32),
    "qe": _sb(512, X4), "se": _sb(512, U8), "qw": _sb(512, X4), "sw": _sb(512, U8), "qu": _sb(128, X4), "su": _sb(128, U8),
    "qu2": _sb(144, X4), "su2": _sb(144, U8), "qv": _sb(128, X4), "sv": _sb(128, U8), "qo": _sb(128, X4), "so": _sb(128, U8),
    "qa": _sb(C, X4), "sa": _sb(C, U8), "qd": _sb(128, X4), "sd": _sb(128, U8), "qd2": _sb(128, X4), "sd2": _sb(128, U8),
    "qf": _sb(C, X4), "sf": _sb(C, U8),
    "qz": _sb(L, X4), "sz": _sb(L, U8), "qk": _sb(L, X4), "sk": _sb(L, U8),
    "qx0": _sb(464, X4), "sx0": _sb(464, U8), "qx1": _sb(464, X4), "sx1": _sb(464, U8), "qx2": _sb(464, X4), "sx2": _sb(464, U8),
    "qx3": _sb(384, X4), "sx3": _sb(384, U8),
    "pa": ("psum", [128, 2048], F32), "pb": ("psum", [128, 2048], F32),
}
SEMAPHORES = ["cv", "cs", "ct", "cg", "sent", "arr0", "arr1", "arr2", "d_seat", "d_al0", "d_al1", "d_x", "d_u", "d_v", "d_wc", "d_ws", "d_out"]
OPT = {"seed": 1, "turns": 40000, "slack": 0.3, "eps": 0.1, "hop": 2.7, "first": 2.5, "wake": 0.17, "cyc": 0.00104, "gat": 1.56, "sca": 3.8,
       "guesses": ((0.8, 0.05, 0.13, 1.0, 0.0, 0.0), (0.85, 0.0, 0.24, 1.0, -0.8, -0.5), (1.0, 0.0, 0.13, 1.9, 0.0, 0.0), (1.2, 0.03, 0.2, 1.4, 0.5, 0.3))}


def rank_program(g, core, T, topo):
    rank = T.rank_of(core)
    if rank is None:
        return
    n_ranks = len(T.cores)
    below, above = T.cores[(rank + 1) % n_ranks], T.cores[(rank - 1) % n_ranks]
    qs = {"v": g.vector, "s": g.scalar, "t": g.tensor, "g": g, "y": g.sync}
    V, S, PE = g.vector, g.scalar, g.tensor
    steps, seen, names = [], {}, []
    cyc = OPT["cyc"]

    def v(name, lo=0, hi=None, by=1, p=(0, 128)):
        return (name, range(lo, SCRATCH[name][1][1] if hi is None else hi, by), p, None)

    def ind(win, off):
        return win[0:3] + (off,)

    def ap(x, cast=None):
        if not isinstance(x, tuple):
            return x
        a = T[x[0]][x[2][0]:x[2][1], x[1].start:x[1].stop:x[1].step]
        a = a.bitcast(cast) if cast else a
        return a.indirect(ap(x[3])) if x[3] else a

    def step(ways, r, w, busy, done=None, sem=None, chain=None):
        n, firm, loose = len(steps), set(), set()
        r = [x for x in r if isinstance(x, tuple)]
        r += [x[3] for x in r + w if x[3]]
        for x, writes in [(x, False) for x in r] + [(x, True) for x in w]:
            if SCRATCH[x[0]][0] == "psum":
                key = (x[0], x[1].start // 512)
                for j, wj in seen.get(key, []):
                    (firm if wj != writes else loose).add(j)
                seen[key] = [(n, True)] if writes else seen.get(key, []) + [(n, False)]
                continue
            cols = set(x[1])
            for j, wj, pj, cj in seen.setdefault(x[0], []):
                if j != n and (writes or wj) and pj[0] < x[2][1] and x[2][0] < pj[1] and not cols.isdisjoint(cj):
                    firm.add(j)
            seen[x[0]].append((n, writes, x[2], cols))
        if chain:
            loose.update(seen.get(chain, []))
            seen[chain] = [n]
        firm.discard(n)
        loose.discard(n)
        steps.append({"ways": ways, "firm": firm, "loose": loose - firm, "busy": busy, "done": done, "sem": sem})

    def cost(q, out, ins, per):
        big = [x for x in [out] + ins if isinstance(x, tuple) and (len(x[1]) > 1 or x is out)]
        for x in big:
            if x[3]:
                return 0.06 + 16 * len(x[3][1]) * cyc * OPT["sca" if x is out else "gat"]
        if q == "v" and per == 1 and all(SIZE[SCRATCH[x[0]][2]] == 2 for x in big):
            per = 0.5
        return max(64, len(out[1]) * per) * cyc

    def op(ways, out, ins, per=1, more=()):
        step(ways, ins, [out] + list(more), {q: cost(q, out, ins, per) for q in ways})

    def ts(out, a, s1, o0, s2=None, o1=None):
        op({"v": (V.tensor_scalar, (ap(out), ap(a), ap(s1), ap(s2), o0) + (() if s2 is None else (o1,)), {})}, out, [a, s1, s2])

    def tt(out, a, b, o):
        op({"v": (V.tensor_tensor, (ap(out), ap(a), ap(b), o), {})}, out, [a, b], 1.01 if "p" in (SCRATCH[a[0]][0][0], SCRATCH[b[0]][0][0]) else 2)

    def both(q, out, a, vway, sway, ins=()):
        op({k: w for k, w in (("v", vway), ("s", sway)) if k in q}, out, [a] + list(ins))

    def cp(out, a, q="vs"):
        both(q, out, a, (V.tensor_copy, (ap(out), ap(a)), {}), (S.activation, (ap(out), ap(a), F.Copy), {}))

    def mul(out, a, c, q="sv"):
        both(q, out, a, (V.tensor_scalar, (ap(out), ap(a), ap(c), None, A.mult), {}), (S.activation, (ap(out), ap(a), F.Copy), {"scale": ap(c)}), [c])

    def lin(out, a, m_, a_, q="sv", f=F.Identity):
        m_, a_ = [col(x) if isinstance(x, str) else x if isinstance(x, tuple) else float(x) for x in (m_, a_)]
        both(q if f == F.Identity else "s", out, a, (V.tensor_scalar, (ap(out), ap(a), ap(m_), ap(a_), A.mult, A.add), {}),
             (S.activation, (ap(out), ap(a), f), {"scale": ap(m_), "bias": ap(a_)}), [m_, a_])

    def flag(out, a, q="vs"):
        both(q, out, a, (V.tensor_scalar, (ap(out), ap(a), 1.0, None, A.min), {}), (S.activation, (ap(out), ap(a), F.Sign), {}))

    def count_below(acc, out, a, bias, scale=1.0):
        op({"s": (S.activation, (ap(out), ap(a), F.Sign), {"scale": scale, "bias": ap(bias), "accum_out": ap(acc)})}, out, [a, bias], 1.1, [acc])

    def scan(out, d0, d1, o0, o1, first=0.0):
        op({"v": (V.tensor_tensor_scan, (ap(out), ap(d0), ap(d1), first, o0, o1), {})}, out, [d0, d1])

    def fill(out, val):
        op({"v": (V.memset, (ap(out), val), {})}, out, [])

    def qs_(name, lo=0, hi=None):
        return v("q" + name, lo, hi), v("s" + name, lo, hi)

    def quant(q, a):
        step({"v": (V.quantize_mx, (ap(q[0]), ap(q[1]), ap(a)), {})}, [a], list(q), {"v": 0.015 + 0.0011 * len(q[0][1])})

    def mm(out, l, r, start=True, stop=True):
        step({"t": (PE.matmul_mx, (ap(out), ap(l[0]), ap(l[1]), ap(r[0]), ap(r[1]), start, stop), {})}, list(l + r), [out],
             {"t": (len(out[1]) + 16) * 0.0006})

    def pick(dst, src, off):
        op({"v": (V.tensor_copy, (ap(dst[0], dt.uint32), ap(ind(src[0], off), dt.uint32)), {})}, dst[0], [ind(src[0], off)])
        cp(dst[1], ind(src[1], off), "sv")

    def iota(out, pat, base, cm=0):
        kw = {} if SCRATCH[out[0]][2] == I32 else {"allow_small_or_imprecise_dtypes": True}
        step({"g": (g.iota, (ap(out), pat, base, cm), kw)}, [], [out], {"g": 0.16 + 0.0021 * len(out[1])})

    def select(out, a, o, fill_, base, cm):
        step({"g": (g.affine_select, (ap(out), ap(a), [[1, len(out[1])]], o, fill_, base, cm), {})}, [a], [out], {"g": 0.21 + 0.0021 * len(out[1])})

    def dma(q, out, in_, sem, r, w, us=1.9, chain=None):
        step({q: (qs[q].dma_start, (out, in_), {})}, r, w, {q: 0.1}, us, sem, chain)

    def col(n):
        if n not in names:
            names.append(n)
        return v("cf", names.index(n), names.index(n) + 1)

    def clin(w, a, m_, a_):
        lin(col(w), col(a), m_, a_)

    def bits(j, src, sh, mask):
        if sh:
            ts(v("ib", j, j + 1), src, sh, A.logical_shift_right, mask, A.bitwise_and)
        else:
            ts(v("ib", j, j + 1), src, mask, A.bitwise_and)
        return v("ib", j, j + 1)

    def tmp(n, used=[0]):
        steps_used = seen.setdefault("tmp", [0])
        steps_used[0] += 1
        return v("tb", 24 * steps_used[0] - 24, 24 * steps_used[0] - 24 + n)

    def bank(name, b, lo, hi, by=1):
        return v(name, 512 * b + lo, 512 * b + hi, by)

    def halves(n):
        return (("v", 0, (n + 1) // 2), ("s", (n + 1) // 2, n))

    def gather2(fn, out, lo, win, off, n, free=False):
        for q, a, b in halves(n):
            fn(v(out, lo + 16 * a, lo + 16 * b), ind(win, v(off, a, b)), "vs" if free else q)

    def rounded(a):
        o = tmp(len(a[1]))
        ts(o, a, RND, A.add, -RND, A.add)
        return o

    def lin2(n, a, ma, b, mb, c):
        x, y, o = tmp(n), tmp(n), tmp(n)
        lin(x, a, ma, 0)
        lin(y, b, mb, c)
        tt(o, x, y, A.add)
        return o

    RND, FAR, D = 12582912.0, 1.0e5, 4194304.0
    p = v("ik", 0, 1)
    E = [qs_("e", 128 * b, 128 * b + 128) for b in range(4)]

    def send(t, xw):
        for q, a, b in (("v", 0, 6), ("s", 6, 10)):
            cp(v("tl", 16 * a, 16 * b), ind(xw, v("o_cmp", a, b)), q)
        x = "x%d" % t
        quant(qs_(x, 0, 128), v("tl", 0, 512))
        calls = []
        for name, cast in (("q" + x, dt.uint8), ("s" + x, None)):
            trs = []
            for j, to in enumerate((below, above)):
                eng = topo.engines(core, to)
                half = eng[j::2]
                rid, pid = topo.addr(to)[:2]
                trs.append(RemoteDMATransfer(dst_ids=[DstId(rid=rid, pnc=pid)], dma_engine_mask=sum(1 << e for e in half),
                                             remote_sem=T.sem["arr%d" % t], src=ap(v(name, 0, W), cast),
                                             dst=ap(v(name, 384 + W * j, 384 + W * j + W), cast)))
            calls.append(trs)
        late = 0.0 if t else OPT["first"]
        step({"g": (calls, (), {})}, list(qs_(x, 0, W)), list(qs_(x, 384, 464)), {"g": 0.8 + late}, OPT["hop"] + late, "arr%d" % t)

    def unpack(t):
        for b in range(4):
            mm(bank("pa", b, 0, L), E[b], qs_("x%d" % t, 128, 384))
            mul(v("tl", 512 + b, 1536, 4), bank("pa", b, 0, L), 0.015625)
            mm(bank("pa", b, 0, L), E[b], qs_("x%d" % t, 128, 384), True, False)

    def unpack_dead(q, lo):
        for b in range(4):
            mm(bank("pb", 2 + b % 2, 0, 128), E[b], qs_(q, 0, 128))
            mul(v("tl", 256 + b, 512, 4), bank("pb", 2 + b % 2, lo, lo + 64), 0.015625)

    def lists(t):
        tt(v("zv"), ind(v("st"), v("o_pos")), v("adyn") if t else v("l4c"), A.add)
        scan(v("zs"), v("r4z"), v("zv"), A.max, A.min)
        ts(v("o_z"), v("zs", 3, L, 4), 4.0, A.mult)
        op({"v": (V.transpose, (ap(v("tr")), ap(v("zv"))), {})}, v("tr"), [v("zv")])
        scan(v("gb", 0, 64), v("r4", 80, 144), v("tr", 0, L, 4), A.max, A.min)
        for a in (0, 64):
            cp(v("gb", 67, 128, 4, (a, a + 64)), v("gb", 3, 64, 4, (64 - a, 128 - a)), "sv")
        for a in range(4):
            cp(v("gb", 131, 256, 4, (32 * a, 32 * a + 32)), v("gb", 3, 128, 4, (32 * (a ^ 1), 32 * (a ^ 1) + 32)), "sv")
        tt(v("e"), ind(v("gb"), v("o_g")), v("cc"), A.add)
        lin(v("nb"), v("e"), 1.0e26, -255.5e26, "s", F.Relu)
        tt(v("de", 0, 31), v("e", 0, 31), v("e", 1, 32), A.subtract)

    def gather_z(t):
        for b in range(4):
            mm(bank("pb", b, 0, 128), E[b], qs_("x%d" % t, 336, 464))
        for b in range(4):
            mul(v("tl", 1536 + b, 1856, 4), bank("pb", b, 48, 128), 0.015625, "vs"[b % 2])
        gather2(cp, "z", 0, v("tl", 512, 1872), "o_z", 64)
        quant(qs_("z"), v("z"))

    def contest(t):
        def seg(b, h):
            return v(b, L * h, L * h + L)

        if t:
            mm(bank("pb", 0, 0, L), qs_("u2", 0, 128), qs_("z"))
        for h in range(2):
            mm(bank("pb", h + 2, 0, 128), qs_("z", 128 * h, 128 * h + 128), qs_("u2", 16, 144))
            tt(v("ms", 16 * h, 16 * h + 16), bank("pb", h + 2, 105, 121), v("nb", 16 * h, 16 * h + 16), A.add)
        if t:
            tt(v("rowm"), bank("pb", 0, 0, L), v("ds"), A.add)
            rows = [v("rowm"), v("rowm")]
        else:
            rows = [bank("pb", j, 0, L) for j in range(2)]
            for j in range(2):
                mm(rows[j], qs_("u2", 0, 128), qs_("z"))
        for b in range(4):
            mm(bank("pa", b, 0, L), qs_("w", 128 * b, 128 * b + 128), qs_("z"), False)
            mul(v("xn", b, 4 * L, 4), bank("pa", b, 0, L), 0.015625)
        key = [v("ms", 16 * h + 5, 16 * h + 6) for h in range(2)]
        for h in range(2):
            count_below(v("sm", h, h + 1), seg("sg", h), rows[0], key[h], -1.0)
        scan(v("rm"), v("rm16"), v("ms"), A.max, A.min)
        tt(v("ge", 1, 32), v("ms", 1, 32), v("rm", 0, 31), A.is_ge)
        scan(v("nm", 1, 31), v("ge", 1, 31), v("de", 1, 31), A.mult, A.add)
        ts(v("eq", L + 2, 2 * L + 2), rows[1], key[1], A.is_equal)
        ts(v("eq", 1, L + 1), seg("sg", 0), 0.0, A.is_equal)
        scan(v("fs"), v("fl"), v("eq"), A.mult, A.subtract)
        tt(v("sm", 2, 4), v("sm", 0, 2), v("fs", L, 2 * L + 2, L + 1), A.is_gt)
        for h in range(2):
            con = v("sm", 2 + h, 3 + h)
            ts(v("kill", 1 + h, 4 * L, 4), v("iob"), v("nm", 16 * h + 14, 16 * h + 15), A.is_equal, con, A.mult)
            mul(v("kill", 512 * h + 3, 512 * h + 512, 4), v("idm"), con)
        quant(qs_("k"), v("kill"))
        if t == 0:
            for j in range(2):
                mm(bank("pb", j, 0, 128), qs_("o"), qs_("k", 128 * j, 128 * j + 128))
        else:
            mm(bank("pb", 0, 0, L), qs_("o"), qs_("k"))
        if t < R - 1:
            mm(bank("pb", 2, 0, L), qs_("o"), qs_("k"))

    for j in range(4):
        dma("ys"[j % 2], T.alv[16 * j:16 * j + 16, :], T.alive[:], "d_al%d" % (j % 2), [], [v("alv", p=(16 * j, 16 * j + 16))], 1.9, "ld%d" % (j % 2))
    dma("y", T.seatb[:], T.seat[:], "d_seat", [], [v("seatb")], 1.9, "ld0")
    dma("y", T.xt[:, 0:4 * C], T.x[:], "d_x", [], [v("xt", 0, 4 * C)], 3.5, "ld0")
    dma("y", T.ut[:], T.u[:], "d_u", [], [v("ut")], 2.5, "ld0")
    dma("y", T.qw[:].bitcast(dt.uint8), T.wc[:], "d_wc", [], [v("qw")], 3.2, "ld0")
    dma("y", T.sw[:], T.ws[:], "d_ws", [], [v("sw")], 2.2, "ld0")
    dma("y", T.vt[:], T.v[:], "d_v", [], [v("vt")], 2.5, "ld0")

    iota(v("ik"), [[16, 24]], 0, 1)
    iota(v("win", 1), [[1, C]], -160)
    iota(v("r4z"), [[0, 64], [-31000, 4]], L + 2 * W)
    iota(v("v256"), [[4, 64], [30001, 4]], 0)
    iota(v("c16"), [[0, 23], [1, 16]], 0)
    for out, val in ((v("win", 0, 1), D * 512), (v("one"), 1.0), (v("k64"), 64.0), (v("wb", 0, W), -255.375), (v("wb", W + C, 416), -255.375),
                     (v("tl", 160, 512), 0.0), (v("o_u", 0, 8), 1), (v("o_dead", 4, 8), 0)):
        fill(out, val)
    for out, val in ((v("xt", 4 * C), 0), (v("vb", 400, 416), L + 2 * W - 169), (v("tl", 1856), 0), (v("xn", 4 * L), 0), (v("gb"), 0), (v("cc"), 0),
                     (v("cc", 4, 32, 16), 10000), (v("cc", 6, 32, 16), 10000), (v("cc", 5, 32, 16), -10000), (v("kill", 0, 4 * L, 4), 0),
                     (v("dead", L), 0), (v("dead", 339, 340), 1), (v("olw", 0, 64), 0), (v("fl", 0, 2 * L + 2, L + 1), 0),
                     (v("eq", 0, 2 * L + 2, L + 1), L - 2 * M)):
        iota(out, [[0, len(out[1])]], val)
    select(v("eb"), v("k64"), A.is_equal, 0.0, -3, -4)
    for h in range(2):
        select(v("fl", (L + 1) * h + 1, (L + 1) * (h + 1)), v("one", 0, L), A.not_equal, -1.0, -128 * h, -1)
    select(v("idm"), v("one", 0, 128), A.is_equal, 0.0, 0, -1)
    iota(v("ko"), [[0, 128], [-31744, 2], [-31744, 2]], 32768)
    iota(v("iob"), [[1, L]], 0)
    iota(v("r16"), [[0, 23], [-31000, 16]], 170)

    g16, lane, quad, elem = bits(0, p, 0, 112), bits(1, p, 0, 15), bits(2, p, 2, 3), bits(3, p, 0, 3)
    ts(col("t1"), p, 48.0, A.is_ge, -1.0, A.add)
    ts(col("t2"), p, 48.0, A.is_ge)
    lin(col("t3"), g16, 0.0625, -4)
    lin(col("ng16"), g16, -1, 0)
    ts(col("dr"), p, 80.0, A.is_ge, col("t1"), A.add)
    ts(col("h"), p, 80.0, A.is_lt, col("t2"), A.mult)
    ts(col("t4"), p, 64.0, A.is_ge, col("t3"), A.add)
    lin(v("kt"), v("ik"), 1, "ng16")
    lin(v("kt1"), v("kt", 0, 20), 1, 1)
    for w, a, m_, a_ in (("invl", "h", 1.0 / W - 1.0 / 9, 1.0 / 9), ("dc", "dr", -3, "t4"), ("v", "h", -1, 1), ("len", "h", 31, 9),
                         ("a3s", "h", 11.5, 8), ("h19", "h", 19.5, 0), ("b1s", "h", W, 0), ("b3s", "h", -140, 180),
                         ("ndc", "dc", -1, 0), ("a1", "dc", "len", "v"), ("a3", "dc", "a3s", "h19"), ("b1", "dr", 360, "b1s"), ("b2", "dr", -W, 0),
                         ("b3", "dr", 140, "b3s"), ("thr", "dc", 19.5, 20), ("wrap", "dc", -W, 0), ("edge", "dc", 19.5, 19.5), ("hop", "dr", W, "dc")):
        clin(w, a, m_, a_)
    kk = v("kt", 0, 23)
    x = tmp(23)
    lin(x, kk, "invl", -0.4875)
    line = rounded(x)
    u = lin2(23, line, "a1", kk, "ndc", "a3")
    row = lin2(23, line, "b1", kk, "b2", "b3")
    f, w, place, sq, off, nxt = [tmp(23) for j in range(6)]
    ts(f, u, col("dc"), A.mult, col("thr"), A.is_gt)
    lin(w, f, "wrap", 0)
    tt(place, u, w, A.add)
    tt(sq, row, place, A.add)
    ts(off, place, col("edge"), A.is_equal, 400.0, A.mult)
    ts(nxt, sq, col("hop"), A.add, 400.0, A.min)
    tt(v("o_p", 0, 23), nxt, off, A.max)
    ts(v("o_o", 0, 23), sq, 400.0, A.min)

    for a in range(2):
        tt(v("o_al", p=(64 * a, 64 * a + 64)), v("alv", p=(0, 64)), v("kt1", p=(0, 64)), A.mult)
    cp(v("o_seat"), v("seatb"), "v")
    gather2(lambda o, a, q: lin(o, a, 1.0 / 512, 160.0 / 512 - 256, q), "w0", 0, v("win"), "o_al", 20, True)
    gather2(cp, "wb", W, v("w0"), "o_seat", 20, True)
    gather2(cp, "wr", 0, v("wb"), "o_p", 23, True)
    scan(v("st"), v("one", 0, K), v("wr", 0, K), A.add, A.min)
    lin(col("m1"), quad, -31000, L + 2 * W + 256)
    lin(col("m2"), elem, 1, 0)
    lin(col("m3"), col("h"), 4 * D, "m1")
    lin(v("lend", 0, W), v("r4z", 0, W), -1, "m3", "s", F.Abs)
    for lo, n, val in ((0, W, 12.625), (W, W, L), (2 * W, 64, 20000)):
        lin(v("r4", lo, lo + n), v("r4z", 0, n), 1, val - L - 2 * W)
    tt(v("ev"), v("st", 8, K, 9), v("lend", 0, W), A.add)
    scan(v("es"), v("r4", 0, W), v("ev"), A.max, A.min)
    ts(v("oi", 0, 10), v("es", 3, W, 4), 2048.0, A.mult, col("m2"), A.add)
    ts(v("oi", 16, 26), v("oi", 0, 10), 2047, A.bitwise_and)
    cp(v("o_cmp"), v("oi", 16, 26), "v")
    send(0, v("xt"))

    lin(v("al"), v("w0"), -2.0 / D, 1, "s", F.Relu)
    scan(v("pre"), v("al"), v("one", 0, C), A.add, A.mult, -170.0)
    lin(v("bt", 0, 16), v("kt", 0, 16), -1, 169.5)
    for k in range(16):
        count_below(v("sums", k, k + 1), v("junk", 80 * k, 80 * k + 80), v("pre", 16 * k, 16 * k + 80), v("bt", k, k + 1))
    lin(col("n1"), lane, -1, 40)
    x = tmp(16)
    lin(x, v("sums", 0, 16), -0.5, "n1")
    tt(v("o_live"), x, v("kt", 0, 16), A.add)
    quant(qs_("a"), v("xt", 0, 4 * C))
    pick(qs_("x0", 128, 384), qs_("a"), v("o_live"))
    tt(v("vb", W, W + C), ind(v("pre"), v("o_seat")), v("wb", W, W + C), A.max)
    for j in range(2):
        clin("hd%d" % j, "dc", -1, L - 9 + W * j)
        lin(v("vb", (W + C) * j, (W + C) * j + W), v("win", 1, W + 1), 1, "hd%d" % j)
    cp(v("own"), ind(v("vb"), v("o_o", 0, 23)), "sv")
    tt(v("delta"), ind(v("vb"), v("o_p", 0, 23)), v("own"), A.subtract)
    lin(v("dseq"), v("wr"), 1.0 / D, -1.0 / 2048, "s", F.Relu)
    op({"v": (V.tensor_copy, (ap(ind(v("inv"), v("o_seat"))), ap(v("win", 1))), {})}, ind(v("inv"), v("o_seat")), [v("win", 1)])
    lin(col("nl"), lane, -FAR, 0)
    lin(v("l16"), v("c16"), FAR, "nl", "s", F.Abs)
    tt(v("pz"), ind(v("inv"), v("o_live")), v("l16", 0, L), A.add)
    scan(v("pzs"), v("r16", 0, L), v("pz"), A.max, A.min)
    for w, a, m_, a_ in (("e1", "h", "ndc", "v"), ("drc", "dc", "dr", 0), ("e3a", "dr", 3.5, -4.5), ("m9", "h", -8, 9), ("f1", "dr", -1, "b1s"),
                         ("f2a", "v", 3.5, 0), ("e2a", "e1", -W, 0), ("e3b", "h", 24, "e3a"), ("f2", "dr", 3.5, "f2a"), ("nthr", "dc", -19.5, 20),
                         ("e2", "drc", -1, "e2a"), ("e3c", "dc", "e3b", "h19"), ("e3", "e1", 160, "e3c"), ("wrap9", "wrap", "m9", 0)):
        clin(w, a, m_, a_)
    ss = v("pzs", 15, L, 16)
    x, f, w = tmp(16), tmp(16), tmp(16)
    lin(x, ss, 1.0 / W, 4 - 0.4875)
    rho = rounded(x)
    u = lin2(16, rho, "e2", ss, "e1", "e3")
    ts(f, u, col("ndc"), A.mult, col("nthr"), A.is_gt)
    lin(w, f, "wrap9", 0)
    tt(v("o_pos"), lin2(16, u, "m9", rho, "f1", "f2"), w, A.subtract)
    lin(col("k1"), quad, -30000, 0)
    lin(col("k2"), elem, 0.25, "k1")
    lin(v("l4c"), v("v256"), 1, "k2", "s", F.Abs)
    for b in range(4):
        quant(E[b], v("eb", 3 - b, 515 - b))
    quant(qs_("u"), v("ut"))
    lin(v("o_u", 8, 9), bits(4, p, 0, 7), 16, 0, "v")
    pick(qs_("u2"), qs_("u"), v("o_u", 0, 9))
    quant(qs_("o"), v("ko"))
    quant(qs_("v"), v("vt"))
    lin(v("rm16"), v("cc"), 1.0e25, -5.0e28)
    for j, (base, by) in enumerate(((0, 4), (0, 2), (9, 64), (9, 32), (9, 128), (9, 16))):
        iota(v("pm", j, j + 1), [[0, 1]], base * by, by)
    ts(v("ib", 8, 14), v("pm", 0, 6), 128, A.bitwise_and)
    bit = [v("ib", 8 + j, 9 + j) for j in range(6)]
    lin(col("d0"), bit[0], -1, 0)
    lin(col("d1"), bit[1], -0.5, 0)
    lin(col("s0"), bit[2], 1, "d0", "s", F.Abs)
    lin(col("s1"), bit[3], 0.5, "d1", "s", F.Abs)
    lin(col("y0"), bit[4], 1.0 / 32, "s0")
    lin(col("y1"), bit[0], 1.0 / 16, "s1")
    lin(col("y2"), bit[5], 8, "y0")
    lin(col("y4"), bit[1], 1.0 / 8, "y1")
    ts(col("y3"), col("y4"), col("y2"), A.add, 3.0, A.add)
    x = tmp(2)
    lin(x, v("c16", 0, 2), 32, "y3")
    ts(v("o_g"), x, 256.0, A.min)
    tt(v("am"), ind(v("vb"), v("o_p", 0, 23)), v("l16"), A.add)
    scan(v("ams"), v("r16"), v("am"), A.max, A.min)
    ts(v("o_ray", 0, 23), v("ams", 15, KP, 16), 169.0, A.add)
    clin("k3", "dr", -W / 2, "k2")
    clin("k4", "dc", -1, "k3")
    ts(col("k6"), col("k4"), L + W / 2, A.add, col("v"), A.mult)
    clin("v4", "v", 4, 0)
    clin("hz", "h", 4 * L, 0)
    lin(v("lend", W, 2 * W), v("v256", 0, W), "v", "k6", "s", F.Abs)
    tt(v("delta", 8, K, 9), v("delta", 8, K, 9), v("lend", W, 2 * W), A.add)
    scan(v("dpre"), v("one", 0, C), v("al"), A.add, A.subtract)
    lin(v("bt", 16, 20), v("kt", 0, 4), -1, -0.5)
    for k in range(4):
        count_below(v("sums", 16 + k, 17 + k), v("junk2", 272 * k, 272 * k + 272), v("dpre", 16 * k, 16 * k + 272), v("bt", 16 + k, 17 + k))
    x = tmp(4)
    clin("n2", "n1", 1, 96)
    lin(x, v("sums", 16, 20), -0.5, "n2")
    tt(v("o_dead", 0, 4), x, v("kt", 0, 4), A.add)
    pick(qs_("d"), qs_("a"), v("o_dead"))
    lin(v("rl16"), v("l16", 0, C), -1, 1000)
    scan(v("ps"), v("rl16"), v("pre"), A.max, A.min)
    a1, a2, a3, a4 = [tmp(20) for j in range(4)]
    lin(a3, v("ps", 15, C, 16), 1, 170 + 63)
    ts(a2, v("o_al"), 1.0, A.min)
    lin(a1, v("kt", 0, 20), 1, 63)
    tt(a4, a2, a3, A.mult)
    x = tmp(20)
    tt(x, a1, a3, A.subtract)
    tt(v("o_slot"), x, a4, A.max)

    for t in range(R):
        if t == 1:
            ts(v("dead", 0, 128), bank("pb", 0, 0, 128), 0.0, A.max)
            lin(v("dead", 128, L), bank("pb", 1, 0, 128), 1, 0, "s", F.Relu)
        if t == 2:
            tt(v("dead", 0, L), bank("pb", 0, 0, L), v("dead", 0, L), A.max)
        if t:
            gather2(flag, "dseq", 0, v("dead"), "o_ray", 23)
        scan(v("st"), v("dseq", 0, K), v("delta", 0, K), A.mult, A.add)
        if t:
            scan(v("es"), v("r4", W, 2 * W), v("st", 8, K, 9), A.max, A.min)
            ts(v("o_cmp"), v("es", 3, W, 4), col("v4"), A.mult, col("hz"), A.add)
            send(t, v("xn"))
            tt(v("adyn"), bank("pb", 2, 0, L), v("adyn") if t > 1 else v("l4c"), A.max)
            mul(v("ds"), v("dead", 0, L), -1.0e21)
            quant(qs_("x%d" % t, 128, 384), v("xn", 0, 4 * L))
        unpack(t)
        lists(t)
        if t == 1:
            unpack_dead("d", 0)
        if t == 2:
            unpack_dead("x2", 64)
            quant(qs_("d2"), v("tl", 0, 512))
            unpack_dead("d2", 64)
        gather_z(t)
        contest(t)

    quant(qs_("x3", 0, 128), v("tl", 0, 512))
    quant(qs_("x3", 128, 384), v("xn", 0, 4 * L))
    tt(v("olw", 64, C), bank("pb", 0, 0, L), v("ds"), A.is_le)
    gather2(cp, "olb", 0, v("olw"), "o_slot", 20)
    dma("y", T.ol[:], T.olb[0:1, :], "d_out", [v("olb")], [])
    for j in range(2):
        lo, hi = 160 * j, 160 * j + 160
        pick(qs_("f", lo, hi), qs_("x3", 64, 384), v("o_slot", 10 * j, 10 * j + 10))
        mm(bank("pa", j, 0, 160), qs_("v"), qs_("f", lo, hi))
        cp(v("ysb", lo, hi), bank("pa", j, 0, 160), "sv")
        dma("sy"[j], T.y[:, lo:hi], T.ysb[:, lo:hi], "d_out", [v("ysb", lo, hi)], [], 2.6)
        dma("y", T.oc[:, 4 * lo:4 * hi], T.qf[:, lo:hi].bitcast(dt.uint8), "d_out", [v("qf", lo, hi)], [], 2.6)
    for k in range(4):
        dma("y", T.osc[4 * k:4 * k + 4, :], T.sf[32 * k:32 * k + 4, :], "d_out", [v("sf")], [])

    n, wake = len(steps), OPT["wake"]
    behind = [0] * n
    for i, s in enumerate(steps):
        far = 0
        for j in s["firm"]:
            far |= behind[j]
        s["firm"], s["loose"] = [sorted(j for j in s[k] if not far >> j & 1) for k in ("firm", "loose")]
        behind[i] = far | sum(1 << j for j in s["firm"])
    firm, loose = [s["firm"] for s in steps], [s["loose"] for s in steps]
    busy, ways = [s["busy"] for s in steps], [list(s["ways"]) for s in steps]
    late = [s["done"] - min(s["busy"].values()) if s["done"] else 0.0 for s in steps]
    least = [min(b.values()) for b in busy]
    kind = [(s["sem"] or "c")[0:4] for s in steps]
    after = [[] for _ in steps]
    for i in range(n):
        for j in firm[i] + loose[i]:
            after[j].append(i)
    tail, seed = [0.0] * n, [OPT["seed"]]
    for i in range(n - 1, -1, -1):
        tail[i] = least[i] + late[i] + max([tail[j] + wake for j in after[i]] + [0.0])

    def lay(tail):
        left = [len(firm[i]) + len(loose[i]) for i in range(n)]
        ready = {i: [(0.0, q) for q in ways[i]] for i in range(n) if not left[i]}
        free, end, queue, plan = {q: 0.0 for q in qs}, [0.0] * n, [None] * n, []
        while ready:
            at, x = {}, None
            for i in ready:
                best = None
                for t0, q in ready[i]:
                    t0 = max(t0, free[q])
                    if best is None or t0 + busy[i][q] < best[2] - 0.02:
                        best = (t0, q, t0 + busy[i][q])
                at[i] = best
                if x is None or (best[0], -tail[i]) < (at[x][0], -tail[x]):
                    x = i
            tx, qx, bx = at[x]
            z = None
            for y in ready:
                ty, qy, by = at[y]
                if qy == qx and tail[y] > tail[x] and ty < bx and (z is None or tail[y] > tail[z]) \
                        and bx + tail[y] > max(ty + tail[y], by + tail[x]) + OPT["eps"]:
                    z = y
            x = x if z is None else z
            t0, q, t1 = at[x]
            queue[x], free[q], end[x] = q, t1, t1 + late[x]
            plan.append(x)
            del ready[x]
            for j in after[x]:
                left[j] -= 1
                if not left[j]:
                    t1 = max([0.0] + [end[k] + wake for k in firm[j]])
                    ready[j] = [(max([t1] + [end[k] + wake for k in loose[j] if queue[k] != q1]), q1) for q1 in ways[j]]
        return max(end), plan, queue

    def guess(slow, fix, wk, pe, hop, dma_):
        b = [{q: x * (pe if q == "t" else slow) + (fix if q in "vs" else 0.0) if kind[i] == "c" else x for q, x in busy[i].items()} for i in range(n)]
        return b, [late[i] + wk + (0.0 if kind[i] == "c" else hop if kind[i][0] == "a" else dma_) for i in range(n)]

    def replay(plan, queue, b, more):
        free, last, end, start, why = {q: 0.0 for q in qs}, {}, [0.0] * n, [0.0] * n, [None] * n
        for i in plan:
            q = queue[i]
            t0, w = free[q], last.get(q)
            for j in firm[i]:
                if end[j] > t0:
                    t0, w = end[j], j
            for j in loose[i]:
                if end[j] > t0 and queue[j] != q:
                    t0, w = end[j], j
            start[i], why[i], last[q] = t0, w, i
            free[q] = t0 = t0 + b[i][q]
            end[i] = t0 + more[i]
        return end, start, why

    def draw(k):
        seed[0] = (seed[0] * 1103515245 + 12345) % 2147483648
        return (seed[0] >> 8) % k

    if "best" not in OPT:
        guesses = [guess(*x) for x in OPT["guesses"]]
        plan, queue = lay(tail)[1:]
        now = [replay(plan, queue, *x) for x in guesses]
        total = sum(max(x[0]) for x in now)
        best = (total, plan, queue)
        for turn in range(OPT["turns"]):
            end, start, why = now[draw(len(now))]
            i, pairs = end.index(max(end)), []
            while why[i] is not None:
                if queue[why[i]] == queue[i] and why[i] not in firm[i] and why[i] not in loose[i]:
                    pairs.append((i, why[i]))
                i = why[i]
            if not pairs:
                break
            x, y = pairs[draw(len(pairs))]
            how, plan2, queue2 = draw(5), list(plan), queue
            if how < 2:
                plan2.remove(y)
                lo, hi = plan2.index(x) + 1, min([plan2.index(j) for j in after[y]] + [n - 1])
                if lo > hi:
                    continue
                plan2.insert(lo if how else lo + draw(min(hi - lo, 40) + 1), y)
            elif how < 4:
                z = x if how == 2 else y
                hi = plan2.index(y) - (z == y)
                plan2.remove(z)
                lo = max([plan2.index(j) + 1 for j in firm[z] + loose[z]] + [0])
                if lo > hi:
                    continue
                plan2.insert(hi - draw(min(hi - lo, 3 if how == 2 else 60) + 1), z)
            else:
                z = (x, y)[draw(2)]
                if len(ways[z]) < 2:
                    continue
                queue2 = list(queue)
                queue2[z] = [q for q in ways[z] if q != queue[z]][0]
            got = [replay(plan2, queue2, *x) for x in guesses]
            sum2 = sum(max(x[0]) for x in got)
            if sum2 <= total + OPT["slack"] * (1 - turn / OPT["turns"]) * draw(100) / 100:
                plan, queue, now, total = sorted(plan2, key=lambda i: got[0][1][i]), queue2, got, sum2
                if total < best[0]:
                    best = (total, plan, queue)
        OPT["best"] = best + ([max(replay(best[1], best[2], *x)[0]) for x in guesses],)
        OPT["all"] = (firm, loose, busy, late, kind, steps)
    plan, queue = OPT["best"][1], OPT["best"][2]

    count, token, waited = {}, [None] * n, {q: {} for q in qs}

    def wait(q, sem, val):
        if waited[q].get(sem, 0) < val:
            waited[q][sem] = val
            qs[q].wait_ge(T.sem[sem], val)

    for i in plan:
        s, q = steps[i], queue[i]
        need = {}
        for j in firm[i] + [j for j in loose[i] if queue[j] != q]:
            need[token[j][0]] = max(need.get(token[j][0], 0), token[j][1])
        for sem in sorted(need):
            wait(q, sem, need[sem])
        call, args, kw = s["ways"][q]
        if isinstance(call, list):
            for trs in call:
                g.remote_dma_fused(trs, local_sem=T.sem.sent)
            count["sent"] = count.get("sent", 0) + len(topo.engines(core, below)) + len(topo.engines(core, above))
            token[i] = (s["sem"], len(topo.engines(above, core)) + len(topo.engines(below, core)))
        else:
            sem, k = (s["sem"], 16) if s["sem"] else ("c" + q, 1)
            count[sem] = count.get(sem, 0) + k
            call(*args, **kw).then_inc(T.sem[sem], k)
            token[i] = (sem, count[sem])
    for sem in sorted(count):
        wait("g", sem, count[sem])
